import numpy as np
import ml_dtypes


def mxq(x, axis, fmt="e4m3"):
    dtype, down = {"e4m3": (ml_dtypes.float8_e4m3fn, 7), "e5m2": (ml_dtypes.float8_e5m2, 14)}[fmt]
    v = np.moveaxis(np.asarray(x, np.float32).astype(ml_dtypes.bfloat16).astype(np.float64), axis, -1)
    blocks = v.reshape(v.shape[:-1] + (-1, 32))
    amax = np.abs(blocks).max(-1, keepdims=True)
    byte = np.maximum(np.where(amax > 0, np.frexp(amax)[1] - 1 + 127, 0) - down, 1)
    scale = np.exp2(byte - 127.0)
    codes = (blocks / scale).astype(np.float32).astype(dtype).astype(np.float64)
    return np.moveaxis((codes * scale).reshape(v.shape), -1, axis)


WIDE = False


def mx_kscale(k):
    if not WIDE:
        return np.ones(k)
    levels = np.array([10, -10, 5, -5, 0])
    if k % 512:
        return np.exp2(np.random.permutation(np.resize(levels, k // 32))).repeat(32)
    a = np.empty((k // 512, 16))
    for p in range(k // 512):
        a[p, :8] = np.random.permutation(np.resize(levels, 8))
        for g in range(8):
            far = levels[np.abs(levels - a[p, g]) >= 10]
            a[p, g + 8] = far[np.random.randint(len(far))]
    return np.exp2(a.ravel()).repeat(32)


def f64(x):
    return np.asarray(x).astype(np.float64)


def striped(idx):
    return np.tile(idx.reshape(-1, 16).T, (8, 1)).astype(np.uint16)


def unstriped(offs):
    return offs[:16].T.reshape(-1).astype(np.int64)


E2M1 = np.array([0.0, 0.5, 1.0, 1.5, 2.0, 3.0, 4.0, 6.0, -0.0, -0.5, -1.0, -1.5, -2.0, -3.0, -4.0, -6.0])


def pack_weight(w, fmt):
    k, n = w.shape
    w = f64(np.asarray(w, np.float32).astype(ml_dtypes.bfloat16)).reshape(k // 32, 32, n)
    amax = np.abs(w).max(1)
    if fmt == "e4m3":
        byte = np.frexp(amax)[1] - 1 + 127 - 7
    else:
        mant, ex = np.frexp(amax / 6.0)
        byte = np.where(mant > 0.5, ex, ex - 1) + 127
    byte = np.clip(np.where(amax > 0, byte, 1), 1, 254)
    scaled = (w * np.exp2(127.0 - byte)[:, None, :]).reshape(k, n).astype(np.float32)
    by_word = np.ascontiguousarray(scaled.reshape(k // 512, 128, 4, n).transpose(0, 1, 3, 2))
    if fmt == "e4m3":
        words = by_word.astype(ml_dtypes.float8_e4m3fn).view(np.uint8)
    else:
        c = by_word.astype(ml_dtypes.float4_e2m1fn).view(np.uint8) & 0xF
        words = (c[..., 0::2] | (c[..., 1::2] << 4)).reshape(k // 512, 128, 2 * n)
    return np.ascontiguousarray(words), np.ascontiguousarray(byte.astype(np.uint8).reshape(k // 512, 16, n))


def unpack_weight(words, scales, fmt):
    g, _, n = scales.shape
    words = np.ascontiguousarray(words).reshape(g, 128, n, -1)
    if fmt == "e4m3":
        vals = words.view(ml_dtypes.float8_e4m3fn).astype(np.float64)
    else:
        nib = np.empty((g, 128, n, 4), np.uint8)
        nib[..., 0::2] = words & 0xF
        nib[..., 1::2] = words >> 4
        vals = E2M1[nib]
    vals = vals * np.repeat(np.exp2(scales.astype(np.float64) - 127.0), 8, axis=1)[..., None]
    return vals.transpose(0, 1, 3, 2).reshape(g * 512, n)


def gelu(v):
    return 0.5 * v * (1.0 + np.tanh(np.sqrt(2.0 / np.pi) * (v + 0.044715 * v**3)))


def bf(x):
    return np.asarray(x, np.float32).astype(ml_dtypes.bfloat16)


def planes(Y):
    n, m = Y.shape
    b = f64(bf(Y)).reshape(n // 32, 32, m)
    amax = np.abs(b).max(1)
    byte = np.clip(np.where(amax > 0, np.frexp(amax)[1] - 1 + 127 - 7, 1), 1, 254)
    codes = (b * np.exp2(127.0 - byte)[:, None, :]).reshape(n, m).astype(np.float32).astype(ml_dtypes.float8_e4m3fn).view(np.uint8)
    words = codes.reshape(n // 512, 128, 4, m).transpose(0, 1, 3, 2)
    return np.ascontiguousarray(words), np.ascontiguousarray(byte.astype(np.uint8).reshape(n // 512, 16, m))


K, H, N, T, S = 1024, 1024, 512, 4096, 1024

def setup_inputs():
    n = np.random.standard_normal
    s = mx_kscale(K)[:, None]
    u = mx_kscale(H)[:, None]
    tab_words, tab_scales = pack_weight(n((K, T)) * s, "e4m3")
    w1 = (1.5 * n((K, H)) / np.sqrt(K) / s).astype(np.float32)
    w2_words, w2_scales = pack_weight(n((K, H)) / np.sqrt(K) / s, "e2m1")
    gain = (np.exp(0.3 * n(H)) * u[:, 0]).astype(np.float32)
    w3_words, w3_scales = pack_weight(1.4 * n((H, N)) / np.sqrt(H) / u, "e4m3")
    depth = np.exp(np.linspace(-0.5, 0.5, N)[:, None] + 0.3 * n((N, S))).astype(np.float32)
    offs = striped(np.random.permutation(T)[:S])
    return {"tab_words": tab_words, "tab_scales": tab_scales, "offs": offs,
            "w1": w1, "w2_words": w2_words, "w2_scales": w2_scales, "gain": gain,
            "w3_words": w3_words, "w3_scales": w3_scales, "depth": depth}

def reference(tab_words, tab_scales, offs, w1, w2_words, w2_scales, gain,
              w3_words, w3_scales, depth):
    v = unpack_weight(tab_words, tab_scales, "e4m3")[:, unstriped(offs)]
    w2 = unpack_weight(w2_words, w2_scales, "e2m1")
    w3 = unpack_weight(w3_words, w3_scales, "e4m3")
    a = mxq(f64(w1), 0, "e4m3").T @ v
    b = w2.T @ v
    e = np.log(1.0 + np.square(np.concatenate((a, b), axis=0)))
    h = f64(gain)[:, None] * (e[:H] - e[H:])
    y = f64(depth) * (w3.T @ mxq(h, 0, "e4m3"))
    words, scales = planes(h)
    return y, h, words, scales

@@ -1,0 +1,297 @@
+from contextlib import ExitStack
+
+import concourse.mybir as mybir
+
+K, H, N, T, S = 1024, 1024, 512, 4096, 1024
+FLOPS = 2 * S * (2 * K * H + H * N)
+
+F32 = mybir.dt.float32
+BF16 = mybir.dt.bfloat16
+I32 = mybir.dt.int32
+U32 = mybir.dt.uint32
+U16 = mybir.dt.uint16
+U8 = mybir.dt.uint8
+FP8X4 = mybir.dt.float8_e4m3fn_x4
+FP4X4 = mybir.dt.float4_e2m1fn_x4
+ACT = mybir.ActivationFunctionType
+ALU = mybir.AluOpType
+
+P = 128
+PACK = 4
+GROUP = P * PACK
+BANK = 512
+QUADS = 4
+PASSES = K // GROUP
+GROUPS = H // GROUP
+HALVES = S // BANK
+LAYER_TILES = N // P
+
+
+def tile_list_radar_log_contrast_kernel(
+    tc, tab_words, tab_scales, offs, w1, w2_words, w2_scales, gain, w3_words, w3_scales, depth,
+    out_0, out_1, out_2, out_3,
+):
+    nc = tc.nc
+    with ExitStack() as ctx:
+        keep = ctx.enter_context(tc.tile_pool(name="keep", bufs=1))
+        ring = ctx.enter_context(tc.tile_pool(name="ring", bufs=2))
+        psum = ctx.enter_context(tc.psum_pool(name="psum", bufs=4))
+
+        def held(shape, dtype, name, tag=None):
+            return keep.tile(shape, dtype, name=name, tag=tag or name, align_bytes=64)
+
+        offsets = keep.tile([P, S // 16], U16, name="offsets")
+        nc.sync.dma_start(offsets[:], offs)
+
+        w2_raw = held([P, PASSES, 2 * H], U8, "w2_raw")
+        nc.sync.dma_start(w2_raw[:].bitcast(I32), w2_words.rearrange("a p c -> p a c").bitcast(I32))
+
+        def load_table(a, tag):
+            window = held([P, T], I32, "table%d" % a, tag)
+            nc.sync.dma_start(window[:], tab_words[a].rearrange("p t i -> p (t i)").bitcast(I32))
+            return window
+
+        table0 = load_table(0, "slot_b")
+
+        gains = held([P, GROUPS, PACK], F32, "gains")
+        nc.sync.dma_start(gains[:], gain.rearrange("(g p t) -> p g t", g=GROUPS, t=PACK))
+
+        scale_window = held([P, T], U8, "scale_window", "slot_a")
+        nc.vector.memset(scale_window[:].bitcast(I32), 0)
+        nc.sync.dma_start(
+            scale_window[0:P:4, :].bitcast(I32), tab_scales.rearrange("a q t -> q a t").bitcast(I32)
+        )
+
+        w2_scales_raw = held([P, PASSES, H], U8, "w2_scales_raw")
+        nc.vector.memset(w2_scales_raw[:].rearrange("p a c -> p (a c)").bitcast(I32), 0)
+        for quad in range(QUADS):
+            nc.sync.dma_start(
+                w2_scales_raw[32 * quad : 32 * quad + 4].bitcast(I32),
+                w2_scales[:, 4 * quad : 4 * quad + 4, :].rearrange("a r c -> r a c").bitcast(I32),
+            )
+
+        v_scales = held([P, PASSES * S], U8, "v_scales")
+        nc.vector.memset(v_scales[:].bitcast(I32), 0)
+
+        warm = held([P, 2], F32, "warm", "slot_c")
+        nc.vector.memset(warm[:, 0:1], 1.0)
+        nc.scalar.activation(warm[:, 1:2], warm[:, 0:1], ACT.Ln)
+        table1 = load_table(1, "slot_c")
+        tables = [table0, table1]
+
+        w2_codes, w2_planes = {}, {}
+
+        def deal_w2(g):
+            codes = held([P, PASSES, 2 * GROUP], U8, "w2_codes%d" % g)
+            nc.vector.tensor_copy(
+                codes[:].rearrange("p a (t m b) -> p a t m b", t=PACK, b=2),
+                w2_raw[:, :, 2 * GROUP * g : 2 * GROUP * (g + 1)].rearrange("p a (m t b) -> p a t m b", t=PACK, b=2),
+            )
+            plane = held([P, PASSES, GROUP], U8, "w2_plane%d" % g)
+            nc.vector.tensor_copy(
+                plane[:].rearrange("p a (t m) -> p a t m", t=PACK),
+                w2_scales_raw[:, :, GROUP * g : GROUP * (g + 1)].rearrange("p a (m t) -> p a t m", t=PACK),
+            )
+            w2_codes[g], w2_planes[g] = codes, plane
+
+        picked_scales = held([P, S], U8, "picked_scales")
+        nc.vector.tensor_copy(picked_scales[:], scale_window[:].indirect(offsets[:]))
+        for quad in range(QUADS):
+            nc.sync.dma_start(
+                v_scales[32 * quad : 32 * quad + 4, :].bitcast(I32),
+                picked_scales[32 * quad : 32 * quad + 32 : 4, :].bitcast(I32),
+            )
+        deal_w2(0)
+
+        v_codes = {}
+
+        def gather_words(a, u):
+            picked = held([P, BANK], U32, "v_codes%d%d" % (a, u))
+            cols = slice(u * BANK // 16, (u + 1) * BANK // 16)
+            nc.vector.tensor_copy(picked[:], tables[a][:].bitcast(U32).indirect(offsets[:, cols]))
+            v_codes[a, u] = picked
+
+        gather_words(0, 0)
+        gather_words(0, 1)
+        deal_w2(1)
+        gather_words(1, 0)
+        gather_words(1, 1)
+
+        w1_codes, w1_planes = {}, {}
+        w1_slot = {(0, 0): "slot_a", (0, 1): "slot_b", (1, 0): "slot_c", (1, 1): "slot_a"}
+
+        def quantize_w1(g, a):
+            raw = held([P, PACK, GROUP], F32, "w1_raw%d%d" % (g, a), w1_slot[g, a])
+            rows = w1[a * GROUP : (a + 1) * GROUP, g * GROUP : (g + 1) * GROUP]
+            nc.sync.dma_start(raw[:], rows.rearrange("(p i) c -> p i c", i=PACK))
+            rounded = ring.tile([P, PACK * GROUP], BF16, name="w1_rounded", align_bytes=64)
+            nc.vector.tensor_copy(
+                rounded[:].rearrange("p (t m i) -> p m i t", t=PACK, i=PACK),
+                raw[:].rearrange("p i (m t) -> p m i t", t=PACK),
+            )
+            codes = held([P, GROUP], U32, "w1_codes%d%d" % (g, a))
+            plane = held([P, GROUP], U8, "w1_plane%d%d" % (g, a))
+            nc.vector.quantize_mx(out=codes[:].bitcast(FP8X4), scales=plane[:], in_=rounded[:])
+            w1_codes[g, a], w1_planes[g, a] = codes, plane
+
+        def log_energy(dst, stationary, col0, width, slices, step, on_vector=()):
+            u, start = divmod(col0, BANK)
+            per_bank = BANK // width
+            for first in range(0, len(slices), per_bank):
+                part = slices[first : first + per_bank]
+                bank = psum.tile([P, BANK], F32, name="response", tag="response")
+                for place, t in enumerate(part):
+                    for sub in range(0, width, step):
+                        for a in range(PASSES):
+                            codes, plane = stationary(a, t)
+                            nc.tensor.matmul_mx(
+                                out=bank[:, place * width + sub : place * width + sub + step],
+                                lhsT=codes,
+                                lhsT_scale=plane,
+                                rhs=v_codes[a, u][:, start + sub : start + sub + step].bitcast(FP8X4),
+                                rhs_scale=v_scales[:, a * S + col0 + sub : a * S + col0 + sub + step],
+                                start=(a == 0),
+                                stop=(a == PASSES - 1),
+                            )
+                squares = dst[:, part[0] * width : (part[-1] + 1) * width]
+                if part[0] in on_vector:
+                    nc.vector.tensor_copy(squares, bank[:])
+                    nc.vector.tensor_tensor(squares, bank[:], squares, ALU.mult)
+                else:
+                    nc.scalar.activation(squares, bank[:], ACT.Square)
+            run = dst[:, slices[0] * width : (slices[-1] + 1) * width]
+            nc.scalar.activation(run, run, ACT.Ln, bias=1.0)
+
+        clutter = {}
+
+        def clutter_part(g, col0, width, slices, on_vector=()):
+            if slices[0] == 0:
+                clutter[g, col0] = ring.tile([P, PACK * width], F32, name="clutter", bufs=3)
+
+            def stationary(a, t):
+                return (
+                    w2_codes[g][:, a, 2 * P * t : 2 * P * (t + 1)].bitcast(FP4X4),
+                    w2_planes[g][:, a, P * t : P * (t + 1)],
+                )
+
+            log_energy(clutter[g, col0], stationary, col0, width, slices, BANK if width == BANK else P, on_vector)
+            for t in slices:
+                run = clutter[g, col0][:, t * width : (t + 1) * width]
+                nc.vector.tensor_scalar_mul(run, run, gains[:, g, t : t + 1])
+
+        h_codes = [held([P, S], U32, "h_codes%d" % g) for g in range(GROUPS)]
+        h_planes = [held([P, S], U8, "h_plane%d" % g) for g in range(GROUPS)]
+        contrast = {}
+
+        def target_part(g, col0, width, slices):
+            if slices[0] == 0:
+                contrast[g, col0] = ring.tile([P, PACK * width], F32, name="contrast", bufs=3)
+            h = contrast[g, col0]
+
+            def stationary(a, t):
+                return (
+                    w1_codes[g, a][:, P * t : P * (t + 1)].bitcast(FP8X4),
+                    w1_planes[g, a][:, P * t : P * (t + 1)],
+                )
+
+            log_energy(h, stationary, col0, width, slices, width)
+            for t in slices:
+                run = slice(t * width, (t + 1) * width)
+                nc.vector.scalar_tensor_tensor(
+                    h[:, run], h[:, run], gains[:, g, t : t + 1], clutter[g, col0][:, run], ALU.mult, ALU.subtract
+                )
+
+        def finish_contrast(g, col0, width):
+            h = contrast[g, col0]
+            cols = slice(col0, col0 + width)
+            rounded = ring.tile([P, PACK * width], BF16, name="h_rounded", align_bytes=64)
+            nc.vector.tensor_copy(
+                rounded[:].rearrange("p (c i t) -> p c t i", i=4, t=PACK),
+                h[:].rearrange("p (t c i) -> p c t i", i=4, t=PACK),
+            )
+            nc.sync.dma_start(
+                out_1[g * GROUP : (g + 1) * GROUP, cols].rearrange("(p t) j -> p t j", t=PACK),
+                h[:].rearrange("p (t j) -> p t j", t=PACK),
+            )
+            nc.vector.quantize_mx(out=h_codes[g][:, cols].bitcast(FP8X4), scales=h_planes[g][:, cols], in_=rounded[:])
+
+        def store_planes(g, cols):
+            nc.sync.dma_start(
+                out_2[g, :, cols, :].rearrange("p j t -> p (j t)").bitcast(I32), h_codes[g][:, cols].bitcast(I32)
+            )
+
+        def store_scales(g):
+            for quad in range(QUADS):
+                nc.sync.dma_start(
+                    out_3[g, 4 * quad : 4 * quad + 4, :].bitcast(I32),
+                    h_planes[g][32 * quad : 32 * quad + 4, :].bitcast(I32),
+                )
+
+        def layers(col0, width):
+            cols = slice(col0, col0 + width)
+            per_bank = BANK // width
+            for first in range(0, LAYER_TILES, per_bank):
+                bank = psum.tile([P, per_bank, width], F32, name="layer_sums", tag="layer_sums")
+                for place in range(per_bank):
+                    c = first + place
+                    for g in range(GROUPS):
+                        nc.tensor.matmul_mx(
+                            out=bank[:, place, :],
+                            lhsT=w3_codes[:, g, P * c : P * (c + 1)].bitcast(FP8X4),
+                            lhsT_scale=w3_plane[4 * g : P, P * c : P * (c + 1)],
+                            rhs=h_codes[g][:, cols].bitcast(FP8X4),
+                            rhs_scale=h_planes[g][:, cols],
+                            start=(g == 0),
+                            stop=(g == GROUPS - 1),
+                        )
+                y = ring.tile([P, per_bank, width], F32, name="y", bufs=4)
+                nc.vector.tensor_tensor(y[:], bank[:], depths[:, first : first + per_bank, cols], ALU.mult)
+                nc.sync.dma_start(
+                    out_0.rearrange("(c p) j -> p c j", p=P)[:, first : first + per_bank, cols], y[:]
+                )
+
+        first, second, every = [0, 1], [2, 3], [0, 1, 2, 3]
+        clutter_part(0, 0, BANK, first)
+        clutter_part(0, 0, BANK, second)
+        quantize_w1(0, 0)
+        quantize_w1(0, 1)
+        clutter_part(1, 0, BANK, first)
+        quantize_w1(1, 0)
+        quantize_w1(1, 1)
+        target_part(0, 0, BANK, first)
+
+        depths = held([P, LAYER_TILES, S], F32, "depths", "slot_b")
+        nc.sync.dma_start(depths[:], depth.rearrange("(c p) j -> p c j", p=P))
+        w3_codes = held([P, GROUPS, N], I32, "w3_codes", "slot_c")
+        nc.sync.dma_start(w3_codes[:], w3_words.rearrange("g p c i -> p g (c i)").bitcast(I32))
+        w3_plane = held([P, N], U8, "w3_plane", "slot_a")
+        nc.vector.memset(w3_plane[:].bitcast(I32), 0)
+        for quad in range(QUADS):
+            nc.sync.dma_start(
+                w3_plane[32 * quad : 32 * quad + 8, :].bitcast(I32),
+                w3_scales[:, 4 * quad : 4 * quad + 4, :].bitcast(I32),
+            )
+
+        target_part(0, 0, BANK, second)
+        finish_contrast(0, 0, BANK)
+        store_planes(0, slice(0, BANK))
+        target_part(1, 0, BANK, first)
+        clutter_part(1, 0, BANK, second)
+        target_part(1, 0, BANK, second)
+        finish_contrast(1, 0, BANK)
+        store_planes(1, slice(0, BANK))
+        clutter_part(0, BANK, BANK, first)
+        layers(0, BANK)
+        target_part(0, BANK, BANK, first)
+        clutter_part(0, BANK, BANK, second)
+        target_part(0, BANK, BANK, second)
+        finish_contrast(0, BANK, BANK)
+        store_planes(0, slice(BANK, S))
+        store_scales(0)
+        for col0, width in ((512, 256), (768, 128), (896, 128)):
+            clutter_part(1, col0, width, every)
+            target_part(1, col0, width, every)
+            finish_contrast(1, col0, width)
+            layers(col0, width)
+        store_planes(1, slice(BANK, S))
+        store_scales(1)

@@ -21,10 +21,15 @@ PACK = 4
 GROUP = P * PACK
 BANK = 512
 QUADS = 4
+PER_COLUMN = 16
 PASSES = K // GROUP
 GROUPS = H // GROUP
-HALVES = S // BANK
 LAYER_TILES = N // P
+ROWS_AT = 96
+
+
+def halves(width):
+    return slice(0, width // 2), slice(width // 2, width)
 
 
 def tile_list_radar_log_contrast_kernel(
@@ -40,107 +45,103 @@ def tile_list_radar_log_contrast_kernel(
         def held(shape, dtype, name, tag=None):
             return keep.tile(shape, dtype, name=name, tag=tag or name, align_bytes=64)
 
-        offsets = keep.tile([P, S // 16], U16, name="offsets")
+        offsets = keep.tile([P, S // PER_COLUMN], U16, name="offsets")
         nc.sync.dma_start(offsets[:], offs)
 
-        w2_raw = held([P, PASSES, 2 * H], U8, "w2_raw")
-        nc.sync.dma_start(w2_raw[:].bitcast(I32), w2_words.rearrange("a p c -> p a c").bitcast(I32))
+        def load_scale_rows(name, scales, width, tag):
+            rows = held([P, width], U8, name, tag)
+            nc.vector.memset(rows[0:ROWS_AT, :].bitcast(I32), 0)
+            nc.sync.dma_start(rows[ROWS_AT:P, :].bitcast(I32), scales.rearrange("a q c -> q a c").bitcast(I32))
+            return rows
 
-        def load_table(a, tag):
-            window = held([P, T], I32, "table%d" % a, tag)
+        def place_scale_rows(plane, rows):
+            for quad in range(QUADS):
+                nc.sync.dma_start(
+                    plane[32 * quad : 32 * quad + 4, :].bitcast(I32),
+                    rows[ROWS_AT + 8 * quad : ROWS_AT + 8 * quad + 8, :].bitcast(I32),
+                )
+
+        def load_table(a):
+            window = held([P, T], I32, "table%d" % a, "slot_table%d" % a)
             nc.sync.dma_start(window[:], tab_words[a].rearrange("p t i -> p (t i)").bitcast(I32))
             return window
 
-        table0 = load_table(0, "slot_b")
+        w2_rows = load_scale_rows("w2_rows", w2_scales, H, "slot_table1")
+        scale_window = load_scale_rows("scale_window", tab_scales, T, "slot_window")
+        w2_raw = held([P, PASSES, 2 * H], U8, "w2_raw", "slot_w2")
+        nc.sync.dma_start(w2_raw[:].bitcast(I32), w2_words.rearrange("a p c -> p a c").bitcast(I32))
+        tables = [load_table(0)]
 
-        gains = held([P, GROUPS, PACK], F32, "gains")
-        nc.sync.dma_start(gains[:], gain.rearrange("(g p t) -> p g t", g=GROUPS, t=PACK))
-
-        scale_window = held([P, T], U8, "scale_window", "slot_a")
-        nc.vector.memset(scale_window[:].bitcast(I32), 0)
-        nc.sync.dma_start(
-            scale_window[0:P:4, :].bitcast(I32), tab_scales.rearrange("a q t -> q a t").bitcast(I32)
-        )
-
-        w2_scales_raw = held([P, PASSES, H], U8, "w2_scales_raw")
-        nc.vector.memset(w2_scales_raw[:].rearrange("p a c -> p (a c)").bitcast(I32), 0)
-        for quad in range(QUADS):
-            nc.sync.dma_start(
-                w2_scales_raw[32 * quad : 32 * quad + 4].bitcast(I32),
-                w2_scales[:, 4 * quad : 4 * quad + 4, :].rearrange("a r c -> r a c").bitcast(I32),
-            )
-
-        v_scales = held([P, PASSES * S], U8, "v_scales")
-        nc.vector.memset(v_scales[:].bitcast(I32), 0)
-
-        warm = held([P, 2], F32, "warm", "slot_c")
+        warm = held([P, 2], F32, "warm")
         nc.vector.memset(warm[:, 0:1], 1.0)
         nc.scalar.activation(warm[:, 1:2], warm[:, 0:1], ACT.Ln)
-        table1 = load_table(1, "slot_c")
-        tables = [table0, table1]
 
-        w2_codes, w2_planes = {}, {}
+        w2_plane = held([P, PASSES * H], U8, "w2_plane")
+        nc.vector.memset(w2_plane[:].bitcast(I32), 0)
+        v_plane = held([P, PASSES * S], U8, "v_plane")
+        nc.vector.memset(v_plane[:].bitcast(I32), 0)
 
-        def deal_w2(g):
-            codes = held([P, PASSES, 2 * GROUP], U8, "w2_codes%d" % g)
+        w2_rows_dealt = held([P, H], U8, "w2_rows_dealt", "slot_gains")
+        nc.vector.tensor_copy(
+            w2_rows_dealt[:].rearrange("p (g t m) -> p g t m", g=GROUPS, t=PACK),
+            w2_rows[:].rearrange("p (g m t) -> p g t m", g=GROUPS, t=PACK),
+        )
+        place_scale_rows(w2_plane, w2_rows_dealt)
+        tables.append(load_table(1))
+
+        picked_rows = held([P, S], U8, "picked_rows")
+        nc.vector.tensor_copy(picked_rows[:], scale_window[:].indirect(offsets[:]))
+        place_scale_rows(v_plane, picked_rows)
+
+        w2_codes = []
+        for g in range(GROUPS):
+            dealt = held([P, PASSES, 2 * GROUP], U8, "w2_codes%d" % g)
             nc.vector.tensor_copy(
-                codes[:].rearrange("p a (t m b) -> p a t m b", t=PACK, b=2),
+                dealt[:].rearrange("p a (t m b) -> p a t m b", t=PACK, b=2),
                 w2_raw[:, :, 2 * GROUP * g : 2 * GROUP * (g + 1)].rearrange("p a (m t b) -> p a t m b", t=PACK, b=2),
             )
-            plane = held([P, PASSES, GROUP], U8, "w2_plane%d" % g)
-            nc.vector.tensor_copy(
-                plane[:].rearrange("p a (t m) -> p a t m", t=PACK),
-                w2_scales_raw[:, :, GROUP * g : GROUP * (g + 1)].rearrange("p a (m t) -> p a t m", t=PACK),
-            )
-            w2_codes[g], w2_planes[g] = codes, plane
-
-        picked_scales = held([P, S], U8, "picked_scales")
-        nc.vector.tensor_copy(picked_scales[:], scale_window[:].indirect(offsets[:]))
-        for quad in range(QUADS):
-            nc.sync.dma_start(
-                v_scales[32 * quad : 32 * quad + 4, :].bitcast(I32),
-                picked_scales[32 * quad : 32 * quad + 32 : 4, :].bitcast(I32),
-            )
-        deal_w2(0)
+            w2_codes.append(dealt)
 
         v_codes = {}
 
-        def gather_words(a, u):
-            picked = held([P, BANK], U32, "v_codes%d%d" % (a, u))
-            cols = slice(u * BANK // 16, (u + 1) * BANK // 16)
-            nc.vector.tensor_copy(picked[:], tables[a][:].bitcast(U32).indirect(offsets[:, cols]))
-            v_codes[a, u] = picked
+        def gather_words(a):
+            for u in range(S // BANK):
+                picked = held([P, BANK], U32, "v_codes%d%d" % (a, u))
+                entries = offsets[:, u * BANK // PER_COLUMN : (u + 1) * BANK // PER_COLUMN]
+                nc.vector.tensor_copy(picked[:], tables[a][:].bitcast(U32).indirect(entries))
+                v_codes[a, u] = picked
 
-        gather_words(0, 0)
-        gather_words(0, 1)
-        deal_w2(1)
-        gather_words(1, 0)
-        gather_words(1, 1)
+        gather_words(0)
+        gains = held([P, GROUPS, PACK], F32, "gains", "slot_gains")
+        nc.sync.dma_start(gains[:], gain.rearrange("(g p t) -> p g t", g=GROUPS, t=PACK))
+        gather_words(1)
 
         w1_codes, w1_planes = {}, {}
-        w1_slot = {(0, 0): "slot_a", (0, 1): "slot_b", (1, 0): "slot_c", (1, 1): "slot_a"}
+        w1_slot = {(0, 0): "slot_window", (0, 1): "slot_w2", (1, 0): "slot_table0", (1, 1): "slot_table1"}
 
         def quantize_w1(g, a):
             raw = held([P, PACK, GROUP], F32, "w1_raw%d%d" % (g, a), w1_slot[g, a])
             rows = w1[a * GROUP : (a + 1) * GROUP, g * GROUP : (g + 1) * GROUP]
             nc.sync.dma_start(raw[:], rows.rearrange("(p i) c -> p i c", i=PACK))
             rounded = ring.tile([P, PACK * GROUP], BF16, name="w1_rounded", align_bytes=64)
-            nc.vector.tensor_copy(
-                rounded[:].rearrange("p (t m i) -> p m i t", t=PACK, i=PACK),
-                raw[:].rearrange("p i (m t) -> p m i t", t=PACK),
-            )
+            for pair in halves(PACK):
+                nc.vector.tensor_copy(
+                    rounded[:].rearrange("p (t m i) -> p m t i", t=PACK, i=PACK)[:, :, pair, :],
+                    raw[:].rearrange("p i (m t) -> p m t i", t=PACK)[:, :, pair, :],
+                )
             codes = held([P, GROUP], U32, "w1_codes%d%d" % (g, a))
             plane = held([P, GROUP], U8, "w1_plane%d%d" % (g, a))
-            nc.vector.quantize_mx(out=codes[:].bitcast(FP8X4), scales=plane[:], in_=rounded[:])
+            for words, values in zip(halves(GROUP), halves(PACK * GROUP)):
+                nc.vector.quantize_mx(out=codes[:, words].bitcast(FP8X4), scales=plane[:, words], in_=rounded[:, values])
             w1_codes[g, a], w1_planes[g, a] = codes, plane
 
-        def log_energy(dst, stationary, col0, width, slices, step, on_vector=()):
+        def log_energy(dst, stationary, col0, width, slices, step):
             u, start = divmod(col0, BANK)
             per_bank = BANK // width
+            banks = []
             for first in range(0, len(slices), per_bank):
-                part = slices[first : first + per_bank]
                 bank = psum.tile([P, BANK], F32, name="response", tag="response")
-                for place, t in enumerate(part):
+                for place, t in enumerate(slices[first : first + per_bank]):
                     for sub in range(0, width, step):
                         for a in range(PASSES):
                             codes, plane = stationary(a, t)
@@ -149,44 +150,37 @@ def tile_list_radar_log_contrast_kernel(
                                 lhsT=codes,
                                 lhsT_scale=plane,
                                 rhs=v_codes[a, u][:, start + sub : start + sub + step].bitcast(FP8X4),
-                                rhs_scale=v_scales[:, a * S + col0 + sub : a * S + col0 + sub + step],
+                                rhs_scale=v_plane[:, a * S + col0 + sub : a * S + col0 + sub + step],
                                 start=(a == 0),
                                 stop=(a == PASSES - 1),
                             )
-                squares = dst[:, part[0] * width : (part[-1] + 1) * width]
-                if part[0] in on_vector:
-                    nc.vector.tensor_copy(squares, bank[:])
-                    nc.vector.tensor_tensor(squares, bank[:], squares, ALU.mult)
-                else:
-                    nc.scalar.activation(squares, bank[:], ACT.Square)
+                banks.append(bank)
             run = dst[:, slices[0] * width : (slices[-1] + 1) * width]
-            nc.scalar.activation(run, run, ACT.Ln, bias=1.0)
+            for part in halves(len(slices) * width):
+                source = banks[part.start // BANK][:, part.start % BANK : part.start % BANK + part.stop - part.start]
+                nc.scalar.activation(run[:, part], source, ACT.Square)
+            for part in halves(len(slices) * width):
+                nc.scalar.activation(run[:, part], run[:, part], ACT.Ln, bias=1.0)
 
-        clutter = {}
+        clutter, contrast = {}, {}
 
-        def clutter_part(g, col0, width, slices, on_vector=()):
+        def clutter_part(g, col0, width, slices):
             if slices[0] == 0:
                 clutter[g, col0] = ring.tile([P, PACK * width], F32, name="clutter", bufs=3)
 
             def stationary(a, t):
                 return (
                     w2_codes[g][:, a, 2 * P * t : 2 * P * (t + 1)].bitcast(FP4X4),
-                    w2_planes[g][:, a, P * t : P * (t + 1)],
+                    w2_plane[:, a * H + g * GROUP + P * t : a * H + g * GROUP + P * (t + 1)],
                 )
 
-            log_energy(clutter[g, col0], stationary, col0, width, slices, BANK if width == BANK else P, on_vector)
-            for t in slices:
-                run = clutter[g, col0][:, t * width : (t + 1) * width]
-                nc.vector.tensor_scalar_mul(run, run, gains[:, g, t : t + 1])
-
-        h_codes = [held([P, S], U32, "h_codes%d" % g) for g in range(GROUPS)]
-        h_planes = [held([P, S], U8, "h_plane%d" % g) for g in range(GROUPS)]
-        contrast = {}
+            log_energy(clutter[g, col0], stationary, col0, width, slices, BANK if width == BANK else P)
 
         def target_part(g, col0, width, slices):
             if slices[0] == 0:
                 contrast[g, col0] = ring.tile([P, PACK * width], F32, name="contrast", bufs=3)
-            h = contrast[g, col0]
+            h = contrast[g, col0][:].rearrange("p (t j) -> p t j", t=PACK)
+            other = clutter[g, col0][:].rearrange("p (t j) -> p t j", t=PACK)
 
             def stationary(a, t):
                 return (
@@ -194,30 +188,47 @@ def tile_list_radar_log_contrast_kernel(
                     w1_planes[g, a][:, P * t : P * (t + 1)],
                 )
 
-            log_energy(h, stationary, col0, width, slices, width)
-            for t in slices:
-                run = slice(t * width, (t + 1) * width)
-                nc.vector.scalar_tensor_tensor(
-                    h[:, run], h[:, run], gains[:, g, t : t + 1], clutter[g, col0][:, run], ALU.mult, ALU.subtract
-                )
+            runs = [(t, cols) for t in slices for cols in (halves(width) if t == PACK - 1 else [slice(0, width)])]
+            if width == BANK:
+                log_energy(contrast[g, col0], stationary, col0, width, slices, width)
+                for t in slices:
+                    nc.vector.tensor_tensor(h[:, t, :], h[:, t, :], other[:, t, :], ALU.subtract)
+                for t, cols in runs:
+                    nc.vector.tensor_scalar_mul(h[:, t, cols], h[:, t, cols], gains[:, g, t : t + 1])
+            else:
+                for t in slices:
+                    nc.vector.tensor_scalar_mul(other[:, t, :], other[:, t, :], gains[:, g, t : t + 1])
+                log_energy(contrast[g, col0], stationary, col0, width, slices, width)
+                for t, cols in runs:
+                    nc.vector.scalar_tensor_tensor(
+                        h[:, t, cols], h[:, t, cols], gains[:, g, t : t + 1], other[:, t, cols], ALU.mult, ALU.subtract
+                    )
+
+        h_codes = [held([P, S], U32, "h_codes%d" % g) for g in range(GROUPS)]
+        h_planes = [held([P, S], U8, "h_plane%d" % g) for g in range(GROUPS)]
 
         def finish_contrast(g, col0, width):
-            h = contrast[g, col0]
-            cols = slice(col0, col0 + width)
-            rounded = ring.tile([P, PACK * width], BF16, name="h_rounded", align_bytes=64)
-            nc.vector.tensor_copy(
-                rounded[:].rearrange("p (c i t) -> p c t i", i=4, t=PACK),
-                h[:].rearrange("p (t c i) -> p c t i", i=4, t=PACK),
-            )
-            nc.sync.dma_start(
-                out_1[g * GROUP : (g + 1) * GROUP, cols].rearrange("(p t) j -> p t j", t=PACK),
-                h[:].rearrange("p (t j) -> p t j", t=PACK),
-            )
-            nc.vector.quantize_mx(out=h_codes[g][:, cols].bitcast(FP8X4), scales=h_planes[g][:, cols], in_=rounded[:])
+            h = contrast[g, col0][:].rearrange("p (t j) -> p t j", t=PACK)
+            rounded = ring.tile([P, width, PACK], BF16, name="h_rounded", align_bytes=64)
+            for cols in halves(width):
+                nc.vector.tensor_copy(
+                    rounded[:, cols, :].rearrange("p (c i) t -> p c t i", i=2),
+                    h[:, :, cols].rearrange("p t (c i) -> p c t i", i=2),
+                )
+            rows = out_1[g * GROUP : (g + 1) * GROUP, col0 : col0 + width]
+            nc.sync.dma_start(rows.rearrange("(p t) j -> p t j", t=PACK), h)
+            for cols in halves(width):
+                words = slice(col0 + cols.start, col0 + cols.stop)
+                nc.vector.quantize_mx(
+                    out=h_codes[g][:, words].bitcast(FP8X4),
+                    scales=h_planes[g][:, words],
+                    in_=rounded[:, cols, :].rearrange("p j t -> p (j t)"),
+                )
 
-        def store_planes(g, cols):
+        def store_codes(g, col0, col1):
             nc.sync.dma_start(
-                out_2[g, :, cols, :].rearrange("p j t -> p (j t)").bitcast(I32), h_codes[g][:, cols].bitcast(I32)
+                out_2[g, :, col0:col1, :].rearrange("p j t -> p (j t)").bitcast(I32),
+                h_codes[g][:, col0:col1].bitcast(I32),
             )
 
         def store_scales(g):
@@ -227,44 +238,61 @@ def tile_list_radar_log_contrast_kernel(
                     h_planes[g][32 * quad : 32 * quad + 4, :].bitcast(I32),
                 )
 
-        def layers(col0, width):
+        layer_banks = {}
+
+        def layer_passes(g, col0, width):
             cols = slice(col0, col0 + width)
             per_bank = BANK // width
             for first in range(0, LAYER_TILES, per_bank):
-                bank = psum.tile([P, per_bank, width], F32, name="layer_sums", tag="layer_sums")
+                if g == 0:
+                    layer_banks[col0, first] = psum.tile([P, per_bank, width], F32, name="layer_sums", tag="layer_sums")
                 for place in range(per_bank):
                     c = first + place
-                    for g in range(GROUPS):
-                        nc.tensor.matmul_mx(
-                            out=bank[:, place, :],
-                            lhsT=w3_codes[:, g, P * c : P * (c + 1)].bitcast(FP8X4),
-                            lhsT_scale=w3_plane[4 * g : P, P * c : P * (c + 1)],
-                            rhs=h_codes[g][:, cols].bitcast(FP8X4),
-                            rhs_scale=h_planes[g][:, cols],
-                            start=(g == 0),
-                            stop=(g == GROUPS - 1),
-                        )
-                y = ring.tile([P, per_bank, width], F32, name="y", bufs=4)
-                nc.vector.tensor_tensor(y[:], bank[:], depths[:, first : first + per_bank, cols], ALU.mult)
-                nc.sync.dma_start(
-                    out_0.rearrange("(c p) j -> p c j", p=P)[:, first : first + per_bank, cols], y[:]
-                )
+                    nc.tensor.matmul_mx(
+                        out=layer_banks[col0, first][:, place, :],
+                        lhsT=w3_codes[:, g, P * c : P * (c + 1)].bitcast(FP8X4),
+                        lhsT_scale=w3_plane[4 * g : P, P * c : P * (c + 1)],
+                        rhs=h_codes[g][:, cols].bitcast(FP8X4),
+                        rhs_scale=h_planes[g][:, cols],
+                        start=(g == 0 and place == 0),
+                        stop=(g == GROUPS - 1 and place == per_bank - 1),
+                    )
 
-        first, second, every = [0, 1], [2, 3], [0, 1, 2, 3]
-        clutter_part(0, 0, BANK, first)
-        clutter_part(0, 0, BANK, second)
+        def finish_layers(col0, width):
+            cols = slice(col0, col0 + width)
+            per_bank = BANK // width
+            for first in range(0, LAYER_TILES, per_bank):
+                tiles = slice(first, first + per_bank)
+                y = ring.tile([P, per_bank, width], F32, name="y", bufs=4)
+                nc.vector.tensor_tensor(y[:], layer_banks[col0, first][:], depths[:, tiles, cols], ALU.mult)
+                nc.sync.dma_start(out_0.rearrange("(c p) j -> p c j", p=P)[:, tiles, cols], y[:])
+
+        def contrast_piece(g, col0, width):
+            last = g == GROUPS - 1
+            clutter_part(g, col0, width, every_slice)
+            if last:
+                layer_passes(0, col0, width)
+            target_part(g, col0, width, every_slice)
+            finish_contrast(g, col0, width)
+            if last:
+                layer_passes(g, col0, width)
+                finish_layers(col0, width)
+
+        low_slices, high_slices, every_slice = [0, 1], [2, 3], [0, 1, 2, 3]
+        clutter_part(0, 0, BANK, low_slices)
+        clutter_part(0, 0, BANK, high_slices)
         quantize_w1(0, 0)
         quantize_w1(0, 1)
-        clutter_part(1, 0, BANK, first)
+        clutter_part(1, 0, BANK, low_slices)
         quantize_w1(1, 0)
         quantize_w1(1, 1)
-        target_part(0, 0, BANK, first)
+        target_part(0, 0, BANK, low_slices)
 
-        depths = held([P, LAYER_TILES, S], F32, "depths", "slot_b")
+        depths = held([P, LAYER_TILES, S], F32, "depths", "slot_w2")
         nc.sync.dma_start(depths[:], depth.rearrange("(c p) j -> p c j", p=P))
-        w3_codes = held([P, GROUPS, N], I32, "w3_codes", "slot_c")
+        w3_codes = held([P, GROUPS, N], I32, "w3_codes", "slot_table0")
         nc.sync.dma_start(w3_codes[:], w3_words.rearrange("g p c i -> p g (c i)").bitcast(I32))
-        w3_plane = held([P, N], U8, "w3_plane", "slot_a")
+        w3_plane = held([P, N], U8, "w3_plane", "slot_table1")
         nc.vector.memset(w3_plane[:].bitcast(I32), 0)
         for quad in range(QUADS):
             nc.sync.dma_start(
@@ -272,26 +300,26 @@ def tile_list_radar_log_contrast_kernel(
                 w3_scales[:, 4 * quad : 4 * quad + 4, :].bitcast(I32),
             )
 
-        target_part(0, 0, BANK, second)
+        target_part(0, 0, BANK, high_slices)
         finish_contrast(0, 0, BANK)
-        store_planes(0, slice(0, BANK))
-        target_part(1, 0, BANK, first)
-        clutter_part(1, 0, BANK, second)
-        target_part(1, 0, BANK, second)
+        store_codes(0, 0, BANK)
+        clutter_part(1, 0, BANK, high_slices)
+        target_part(1, 0, BANK, low_slices)
+        target_part(1, 0, BANK, high_slices)
         finish_contrast(1, 0, BANK)
-        store_planes(1, slice(0, BANK))
-        clutter_part(0, BANK, BANK, first)
-        layers(0, BANK)
-        target_part(0, BANK, BANK, first)
-        clutter_part(0, BANK, BANK, second)
-        target_part(0, BANK, BANK, second)
-        finish_contrast(0, BANK, BANK)
-        store_planes(0, slice(BANK, S))
+        store_codes(1, 0, BANK)
+        layer_passes(0, 0, BANK)
+        layer_passes(1, 0, BANK)
+        finish_layers(0, BANK)
+
+        quarter, eighth = S // 4, S // 8
+        contrast_piece(0, 2 * quarter, quarter)
+        contrast_piece(1, 2 * quarter, quarter)
+        store_codes(1, 2 * quarter, 3 * quarter)
+        contrast_piece(0, 3 * quarter, quarter)
+        store_codes(0, 2 * quarter, S)
         store_scales(0)
-        for col0, width in ((512, 256), (768, 128), (896, 128)):
-            clutter_part(1, col0, width, every)
-            target_part(1, col0, width, every)
-            finish_contrast(1, col0, width)
-            layers(col0, width)
-        store_planes(1, slice(BANK, S))
+        contrast_piece(1, 6 * eighth, eighth)
+        contrast_piece(1, 7 * eighth, eighth)
+        store_codes(1, 3 * quarter, S)
         store_scales(1)

@@ -26,6 +26,7 @@ PASSES = K // GROUP
 GROUPS = H // GROUP
 LAYER_TILES = N // P
 ROWS_AT = 96
+KB = 1024
 
 
 def halves(width):
@@ -39,68 +40,78 @@ def tile_list_radar_log_contrast_kernel(
     nc = tc.nc
     with ExitStack() as ctx:
         keep = ctx.enter_context(tc.tile_pool(name="keep", bufs=1))
+        stage = ctx.enter_context(tc.tile_pool(name="stage", bufs=1))
         ring = ctx.enter_context(tc.tile_pool(name="ring", bufs=2))
         psum = ctx.enter_context(tc.psum_pool(name="psum", bufs=4))
 
-        def held(shape, dtype, name, tag=None):
-            return keep.tile(shape, dtype, name=name, tag=tag or name, align_bytes=64)
+        def held(shape, dtype, name):
+            return keep.tile(shape, dtype, name=name, align_bytes=64)
+
+        def staged(shape, dtype, name, offset):
+            return stage.tile(shape, dtype, name=name, align_bytes=64, offset=offset)
 
         offsets = keep.tile([P, S // PER_COLUMN], U16, name="offsets")
         nc.sync.dma_start(offsets[:], offs)
 
-        def load_scale_rows(name, scales, width, tag):
-            rows = held([P, width], U8, name, tag)
+        def load_scale_rows(name, scales, width):
+            rows = held([P, width], U8, name)
             nc.vector.memset(rows[0:ROWS_AT, :].bitcast(I32), 0)
             nc.sync.dma_start(rows[ROWS_AT:P, :].bitcast(I32), scales.rearrange("a q c -> q a c").bitcast(I32))
             return rows
 
-        def place_scale_rows(plane, rows):
-            for quad in range(QUADS):
-                nc.sync.dma_start(
-                    plane[32 * quad : 32 * quad + 4, :].bitcast(I32),
-                    rows[ROWS_AT + 8 * quad : ROWS_AT + 8 * quad + 8, :].bitcast(I32),
-                )
-
-        def load_table(a):
-            window = held([P, T], I32, "table%d" % a, "slot_table%d" % a)
+        def load_table(a, offset):
+            window = staged([P, T], I32, "table%d" % a, offset)
             nc.sync.dma_start(window[:], tab_words[a].rearrange("p t i -> p (t i)").bitcast(I32))
             return window
 
-        w2_rows = load_scale_rows("w2_rows", w2_scales, H, "slot_table1")
-        scale_window = load_scale_rows("scale_window", tab_scales, T, "slot_window")
-        w2_raw = held([P, PASSES, 2 * H], U8, "w2_raw", "slot_w2")
-        nc.sync.dma_start(w2_raw[:].bitcast(I32), w2_words.rearrange("a p c -> p a c").bitcast(I32))
-        tables = [load_table(0)]
+        w2_codes = {}
+
+        def load_w2(g, raw):
+            columns = w2_words[:, :, 2 * GROUP * g : 2 * GROUP * (g + 1)]
+            nc.sync.dma_start(raw[:].bitcast(I32), columns.rearrange("a p c -> p a c").bitcast(I32))
+
+        def deal_w2(g, raw):
+            dealt = held([P, PASSES, 2 * GROUP], U8, "w2_codes%d" % g)
+            nc.vector.tensor_copy(
+                dealt[:].bitcast(U16).rearrange("p a (t m) -> p a t m", t=PACK),
+                raw[:].bitcast(U16).rearrange("p a (m t) -> p a t m", t=PACK),
+            )
+            w2_codes[g] = dealt
+
+        scale_window = load_scale_rows("scale_window", tab_scales, T)
+        w2_rows = load_scale_rows("w2_rows", w2_scales, H)
+        w2_raw0 = held([P, PASSES, 2 * GROUP], U8, "w2_raw0")
+        load_w2(0, w2_raw0)
+        tables = [load_table(0, 0)]
 
         warm = held([P, 2], F32, "warm")
         nc.vector.memset(warm[:, 0:1], 1.0)
         nc.scalar.activation(warm[:, 1:2], warm[:, 0:1], ACT.Ln)
 
-        w2_plane = held([P, PASSES * H], U8, "w2_plane")
-        nc.vector.memset(w2_plane[:].bitcast(I32), 0)
-        v_plane = held([P, PASSES * S], U8, "v_plane")
-        nc.vector.memset(v_plane[:].bitcast(I32), 0)
+        planes = [held([P, PASSES * 2 * BANK], U8, "planes%d" % n) for n in range(2)]
+        for plane in planes:
+            nc.vector.memset(plane[:].bitcast(I32), 0)
 
-        w2_rows_dealt = held([P, H], U8, "w2_rows_dealt", "slot_gains")
-        nc.vector.tensor_copy(
-            w2_rows_dealt[:].rearrange("p (g t m) -> p g t m", g=GROUPS, t=PACK),
-            w2_rows[:].rearrange("p (g m t) -> p g t m", g=GROUPS, t=PACK),
-        )
-        place_scale_rows(w2_plane, w2_rows_dealt)
-        tables.append(load_table(1))
-
-        picked_rows = held([P, S], U8, "picked_rows")
-        nc.vector.tensor_copy(picked_rows[:], scale_window[:].indirect(offsets[:]))
-        place_scale_rows(v_plane, picked_rows)
-
-        w2_codes = []
-        for g in range(GROUPS):
-            dealt = held([P, PASSES, 2 * GROUP], U8, "w2_codes%d" % g)
+        def place_scale_rows(n, picked_at, staging_at):
+            staging = staged([P, 2 * BANK], U8, "staging%d" % n, staging_at)
             nc.vector.tensor_copy(
-                dealt[:].rearrange("p a (t m b) -> p a t m b", t=PACK, b=2),
-                w2_raw[:, :, 2 * GROUP * g : 2 * GROUP * (g + 1)].rearrange("p a (m t b) -> p a t m b", t=PACK, b=2),
+                staging[:, BANK:].rearrange("p (t m) -> p t m", t=PACK),
+                w2_rows[:, n * GROUP : (n + 1) * GROUP].rearrange("p (m t) -> p t m", t=PACK),
             )
-            w2_codes.append(dealt)
+            picked = staged([P, BANK], U8, "picked_rows%d" % n, picked_at)
+            entries = offsets[:, n * BANK // PER_COLUMN : (n + 1) * BANK // PER_COLUMN]
+            nc.vector.tensor_copy(picked[:], scale_window[:].indirect(entries))
+            nc.vector.tensor_copy(staging[ROWS_AT:P, 0:BANK].bitcast(I32), picked[ROWS_AT:P, :].bitcast(I32))
+            for quad in range(QUADS):
+                nc.sync.dma_start(
+                    planes[n][32 * quad : 32 * quad + 4, :].bitcast(I32),
+                    staging[ROWS_AT + 8 * quad : ROWS_AT + 8 * quad + 8, :].bitcast(I32),
+                )
+
+        place_scale_rows(0, 17 * KB - 256, 41 * KB)
+        tables.append(load_table(1, 17 * KB))
+        place_scale_rows(1, 17 * KB - 512, 51 * KB)
+        deal_w2(0, w2_raw0)
 
         v_codes = {}
 
@@ -112,28 +123,39 @@ def tile_list_radar_log_contrast_kernel(
                 v_codes[a, u] = picked
 
         gather_words(0)
-        gains = held([P, GROUPS, PACK], F32, "gains", "slot_gains")
-        nc.sync.dma_start(gains[:], gain.rearrange("(g p t) -> p g t", g=GROUPS, t=PACK))
-        gather_words(1)
+        w2_raw1 = staged([P, PASSES, 2 * GROUP], U8, "w2_raw1", 39 * KB + 512)
+        load_w2(1, w2_raw1)
 
-        w1_codes, w1_planes = {}, {}
-        w1_slot = {(0, 0): "slot_window", (0, 1): "slot_w2", (1, 0): "slot_table0", (1, 1): "slot_table1"}
+        w1_raw, w1_codes, w1_planes = {}, {}, {}
+        w1_at = {(0, 0): 41 * KB + 512, (0, 1): 0, (1, 0): 24 * KB, (1, 1): 41 * KB + 512}
 
-        def quantize_w1(g, a):
-            raw = held([P, PACK, GROUP], F32, "w1_raw%d%d" % (g, a), w1_slot[g, a])
+        def load_w1(g, a):
+            raw = staged([P, PACK, GROUP], F32, "w1_raw%d%d" % (g, a), w1_at[g, a])
             rows = w1[a * GROUP : (a + 1) * GROUP, g * GROUP : (g + 1) * GROUP]
             nc.sync.dma_start(raw[:], rows.rearrange("(p i) c -> p i c", i=PACK))
+            w1_raw[g, a] = raw
+
+        def quantize_w1(g, a):
+            raw = w1_raw[g, a]
             rounded = ring.tile([P, PACK * GROUP], BF16, name="w1_rounded", align_bytes=64)
             for pair in halves(PACK):
                 nc.vector.tensor_copy(
-                    rounded[:].rearrange("p (t m i) -> p m t i", t=PACK, i=PACK)[:, :, pair, :],
-                    raw[:].rearrange("p i (m t) -> p m t i", t=PACK)[:, :, pair, :],
+                    rounded[:].rearrange("p (t m i) -> p m i t", t=PACK, i=PACK)[:, :, :, pair],
+                    raw[:].rearrange("p i (m t) -> p m i t", t=PACK)[:, :, :, pair],
                 )
             codes = held([P, GROUP], U32, "w1_codes%d%d" % (g, a))
             plane = held([P, GROUP], U8, "w1_plane%d%d" % (g, a))
             for words, values in zip(halves(GROUP), halves(PACK * GROUP)):
                 nc.vector.quantize_mx(out=codes[:, words].bitcast(FP8X4), scales=plane[:, words], in_=rounded[:, values])
             w1_codes[g, a], w1_planes[g, a] = codes, plane
+
+        load_w1(0, 0)
+        load_w1(0, 1)
+        gains = staged([P, GROUPS, PACK], F32, "gains", 14 * KB)
+        nc.sync.dma_start(gains[:], gain.rearrange("(g p t) -> p g t", g=GROUPS, t=PACK))
+        gather_words(1)
+        deal_w2(1, w2_raw1)
+        load_w1(1, 0)
 
         def log_energy(dst, stationary, col0, width, slices, step):
             u, start = divmod(col0, BANK)
@@ -145,12 +167,13 @@ def tile_list_radar_log_contrast_kernel(
                     for sub in range(0, width, step):
                         for a in range(PASSES):
                             codes, plane = stationary(a, t)
+                            at = a * 2 * BANK + start + sub
                             nc.tensor.matmul_mx(
                                 out=bank[:, place * width + sub : place * width + sub + step],
                                 lhsT=codes,
                                 lhsT_scale=plane,
                                 rhs=v_codes[a, u][:, start + sub : start + sub + step].bitcast(FP8X4),
-                                rhs_scale=v_plane[:, a * S + col0 + sub : a * S + col0 + sub + step],
+                                rhs_scale=planes[u][:, at : at + step],
                                 start=(a == 0),
                                 stop=(a == PASSES - 1),
                             )
@@ -162,25 +185,29 @@ def tile_list_radar_log_contrast_kernel(
             for part in halves(len(slices) * width):
                 nc.scalar.activation(run[:, part], run[:, part], ACT.Ln, bias=1.0)
 
-        clutter, contrast = {}, {}
+        clutter, scaled, contrast = {}, {}, {}
 
         def clutter_part(g, col0, width, slices):
             if slices[0] == 0:
                 clutter[g, col0] = ring.tile([P, PACK * width], F32, name="clutter", bufs=3)
 
             def stationary(a, t):
-                return (
-                    w2_codes[g][:, a, 2 * P * t : 2 * P * (t + 1)].bitcast(FP4X4),
-                    w2_plane[:, a * H + g * GROUP + P * t : a * H + g * GROUP + P * (t + 1)],
-                )
+                at = a * 2 * BANK + BANK + P * t
+                return w2_codes[g][:, a, 2 * P * t : 2 * P * (t + 1)].bitcast(FP4X4), planes[g][:, at : at + P]
 
             log_energy(clutter[g, col0], stationary, col0, width, slices, BANK if width == BANK else P)
+
+        def scale_clutter(g, col0, width, slices):
+            src = clutter[g, col0][:].rearrange("p (t j) -> p t j", t=PACK)
+            dst = scaled.get((g, col0), clutter[g, col0])[:].rearrange("p (t j) -> p t j", t=PACK)
+            for t in slices:
+                nc.vector.tensor_scalar_mul(dst[:, t, :], src[:, t, :], gains[:, g, t : t + 1])
 
         def target_part(g, col0, width, slices):
             if slices[0] == 0:
                 contrast[g, col0] = ring.tile([P, PACK * width], F32, name="contrast", bufs=3)
             h = contrast[g, col0][:].rearrange("p (t j) -> p t j", t=PACK)
-            other = clutter[g, col0][:].rearrange("p (t j) -> p t j", t=PACK)
+            other = scaled.get((g, col0), clutter[g, col0])[:].rearrange("p (t j) -> p t j", t=PACK)
 
             def stationary(a, t):
                 return (
@@ -189,27 +216,21 @@ def tile_list_radar_log_contrast_kernel(
                 )
 
             runs = [(t, cols) for t in slices for cols in (halves(width) if t == PACK - 1 else [slice(0, width)])]
-            if width == BANK:
-                log_energy(contrast[g, col0], stationary, col0, width, slices, width)
-                for t in slices:
-                    nc.vector.tensor_tensor(h[:, t, :], h[:, t, :], other[:, t, :], ALU.subtract)
-                for t, cols in runs:
-                    nc.vector.tensor_scalar_mul(h[:, t, cols], h[:, t, cols], gains[:, g, t : t + 1])
-            else:
-                for t in slices:
-                    nc.vector.tensor_scalar_mul(other[:, t, :], other[:, t, :], gains[:, g, t : t + 1])
-                log_energy(contrast[g, col0], stationary, col0, width, slices, width)
-                for t, cols in runs:
-                    nc.vector.scalar_tensor_tensor(
-                        h[:, t, cols], h[:, t, cols], gains[:, g, t : t + 1], other[:, t, cols], ALU.mult, ALU.subtract
-                    )
+            log_energy(contrast[g, col0], stationary, col0, width, slices, width)
+            for t, cols in runs:
+                nc.vector.scalar_tensor_tensor(
+                    h[:, t, cols], h[:, t, cols], gains[:, g, t : t + 1], other[:, t, cols], ALU.mult, ALU.subtract
+                )
 
         h_codes = [held([P, S], U32, "h_codes%d" % g) for g in range(GROUPS)]
         h_planes = [held([P, S], U8, "h_plane%d" % g) for g in range(GROUPS)]
 
         def finish_contrast(g, col0, width):
             h = contrast[g, col0][:].rearrange("p (t j) -> p t j", t=PACK)
-            rounded = ring.tile([P, width, PACK], BF16, name="h_rounded", align_bytes=64)
+            if (g, col0) == (1, 896):
+                rounded = staged([P, width, PACK], BF16, "h_rounded_last", 52 * KB)
+            else:
+                rounded = ring.tile([P, width, PACK], BF16, name="h_rounded", align_bytes=64)
             for cols in halves(width):
                 nc.vector.tensor_copy(
                     rounded[:, cols, :].rearrange("p (c i) t -> p c t i", i=2),
@@ -261,38 +282,27 @@ def tile_list_radar_log_contrast_kernel(
         def finish_layers(col0, width):
             cols = slice(col0, col0 + width)
             per_bank = BANK // width
+            if col0 == 768:
+                y = staged([P, LAYER_TILES, width], F32, "y_late", 52 * KB)
+            else:
+                y = ring.tile([P, LAYER_TILES, width], F32, name="y", bufs=3)
             for first in range(0, LAYER_TILES, per_bank):
                 tiles = slice(first, first + per_bank)
-                y = ring.tile([P, per_bank, width], F32, name="y", bufs=4)
-                nc.vector.tensor_tensor(y[:], layer_banks[col0, first][:], depths[:, tiles, cols], ALU.mult)
-                nc.sync.dma_start(out_0.rearrange("(c p) j -> p c j", p=P)[:, tiles, cols], y[:])
-
-        def contrast_piece(g, col0, width):
-            last = g == GROUPS - 1
-            clutter_part(g, col0, width, every_slice)
-            if last:
-                layer_passes(0, col0, width)
-            target_part(g, col0, width, every_slice)
-            finish_contrast(g, col0, width)
-            if last:
-                layer_passes(g, col0, width)
-                finish_layers(col0, width)
+                nc.vector.tensor_tensor(y[:, tiles, :], layer_banks[col0, first][:], depths[:, tiles, cols], ALU.mult)
+            nc.sync.dma_start(out_0.rearrange("(c p) j -> p c j", p=P)[:, :, cols], y[:])
 
         low_slices, high_slices, every_slice = [0, 1], [2, 3], [0, 1, 2, 3]
         clutter_part(0, 0, BANK, low_slices)
         clutter_part(0, 0, BANK, high_slices)
         quantize_w1(0, 0)
+        load_w1(1, 1)
         quantize_w1(0, 1)
-        clutter_part(1, 0, BANK, low_slices)
-        quantize_w1(1, 0)
-        quantize_w1(1, 1)
-        target_part(0, 0, BANK, low_slices)
+        scaled[0, 0] = staged([P, PACK * BANK], F32, "scaled", 6 * KB)
+        scale_clutter(0, 0, BANK, every_slice)
 
-        depths = held([P, LAYER_TILES, S], F32, "depths", "slot_w2")
-        nc.sync.dma_start(depths[:], depth.rearrange("(c p) j -> p c j", p=P))
-        w3_codes = held([P, GROUPS, N], I32, "w3_codes", "slot_table0")
+        w3_codes = staged([P, GROUPS, N], I32, "w3_codes", 0)
         nc.sync.dma_start(w3_codes[:], w3_words.rearrange("g p c i -> p g (c i)").bitcast(I32))
-        w3_plane = held([P, N], U8, "w3_plane", "slot_table1")
+        w3_plane = staged([P, N], U8, "w3_plane", 4 * KB)
         nc.vector.memset(w3_plane[:].bitcast(I32), 0)
         for quad in range(QUADS):
             nc.sync.dma_start(
@@ -300,26 +310,36 @@ def tile_list_radar_log_contrast_kernel(
                 w3_scales[:, 4 * quad : 4 * quad + 4, :].bitcast(I32),
             )
 
+        clutter_part(0, BANK, BANK, low_slices)
+        quantize_w1(1, 0)
+        depths = staged([P, LAYER_TILES, S], F32, "depths", 23 * KB)
+        nc.sync.dma_start(depths[:], depth.rearrange("(c p) j -> p c j", p=P))
+        scale_clutter(0, BANK, BANK, low_slices)
+        quantize_w1(1, 1)
+        target_part(0, 0, BANK, low_slices)
         target_part(0, 0, BANK, high_slices)
         finish_contrast(0, 0, BANK)
-        store_codes(0, 0, BANK)
-        clutter_part(1, 0, BANK, high_slices)
-        target_part(1, 0, BANK, low_slices)
-        target_part(1, 0, BANK, high_slices)
-        finish_contrast(1, 0, BANK)
-        store_codes(1, 0, BANK)
-        layer_passes(0, 0, BANK)
-        layer_passes(1, 0, BANK)
-        finish_layers(0, BANK)
-
-        quarter, eighth = S // 4, S // 8
-        contrast_piece(0, 2 * quarter, quarter)
-        contrast_piece(1, 2 * quarter, quarter)
-        store_codes(1, 2 * quarter, 3 * quarter)
-        contrast_piece(0, 3 * quarter, quarter)
-        store_codes(0, 2 * quarter, S)
+        clutter_part(0, BANK, BANK, high_slices)
+        scale_clutter(0, BANK, BANK, high_slices)
+        target_part(0, BANK, BANK, low_slices)
+        target_part(0, BANK, BANK, high_slices)
+        finish_contrast(0, BANK, BANK)
+        store_codes(0, 0, S)
         store_scales(0)
-        contrast_piece(1, 6 * eighth, eighth)
-        contrast_piece(1, 7 * eighth, eighth)
-        store_codes(1, 3 * quarter, S)
+
+        pieces = [(0, 256), (256, 256), (512, 256), (768, 128), (896, 128)]
+        for col0, width in pieces:
+            clutter_part(1, col0, width, every_slice)
+            scale_clutter(1, col0, width, every_slice)
+            layer_passes(0, col0, width)
+            target_part(1, col0, width, every_slice)
+            finish_contrast(1, col0, width)
+            if col0 == 896:
+                finish_layers(768, 128)
+            layer_passes(1, col0, width)
+            if col0 != 768:
+                finish_layers(col0, width)
+            if col0 == 512:
+                store_codes(1, 0, 768)
+        store_codes(1, 768, S)
         store_scales(1)

@@ -215,7 +215,7 @@ def tile_list_radar_log_contrast_kernel(
                     w1_planes[g, a][:, P * t : P * (t + 1)],
                 )
 
-            runs = [(t, cols) for t in slices for cols in (halves(width) if t == PACK - 1 else [slice(0, width)])]
+            runs = [(t, cols) for t in slices for cols in (halves(width) if t == PACK - 1 and col0 == 896 else [slice(0, width)])]
             log_energy(contrast[g, col0], stationary, col0, width, slices, width)
             for t, cols in runs:
                 nc.vector.scalar_tensor_tensor(
@@ -231,14 +231,15 @@ def tile_list_radar_log_contrast_kernel(
                 rounded = staged([P, width, PACK], BF16, "h_rounded_last", 52 * KB)
             else:
                 rounded = ring.tile([P, width, PACK], BF16, name="h_rounded", align_bytes=64)
-            for cols in halves(width):
+            parts = halves(width) if col0 == 896 else [slice(0, width)]
+            for cols in parts:
                 nc.vector.tensor_copy(
                     rounded[:, cols, :].rearrange("p (c i) t -> p c t i", i=2),
                     h[:, :, cols].rearrange("p t (c i) -> p c t i", i=2),
                 )
             rows = out_1[g * GROUP : (g + 1) * GROUP, col0 : col0 + width]
             nc.sync.dma_start(rows.rearrange("(p t) j -> p t j", t=PACK), h)
-            for cols in halves(width):
+            for cols in parts:
                 words = slice(col0 + cols.start, col0 + cols.stop)
                 nc.vector.quantize_mx(
                     out=h_codes[g][:, words].bitcast(FP8X4),
@@ -263,7 +264,7 @@ def tile_list_radar_log_contrast_kernel(
 
         def layer_passes(g, col0, width):
             cols = slice(col0, col0 + width)
-            per_bank = BANK // width
+            per_bank = 2 if col0 == 896 else BANK // width
             for first in range(0, LAYER_TILES, per_bank):
                 if g == 0:
                     layer_banks[col0, first] = psum.tile([P, per_bank, width], F32, name="layer_sums", tag="layer_sums")
@@ -281,7 +282,7 @@ def tile_list_radar_log_contrast_kernel(
 
         def finish_layers(col0, width):
             cols = slice(col0, col0 + width)
-            per_bank = BANK // width
+            per_bank = 2 if col0 == 896 else BANK // width
             if col0 == 768:
                 y = staged([P, LAYER_TILES, width], F32, "y_late", 52 * KB)
             else:
@@ -289,7 +290,11 @@ def tile_list_radar_log_contrast_kernel(
             for first in range(0, LAYER_TILES, per_bank):
                 tiles = slice(first, first + per_bank)
                 nc.vector.tensor_tensor(y[:, tiles, :], layer_banks[col0, first][:], depths[:, tiles, cols], ALU.mult)
-            nc.sync.dma_start(out_0.rearrange("(c p) j -> p c j", p=P)[:, :, cols], y[:])
+                if (width == BANK and first % 2 == 1) or col0 == 896:
+                    pair = slice(first - 1, first + 1) if width == BANK else tiles
+                    nc.sync.dma_start(out_0.rearrange("(c p) j -> p c j", p=P)[:, pair, cols], y[:, pair, :])
+            if width < BANK and col0 != 896:
+                nc.sync.dma_start(out_0.rearrange("(c p) j -> p c j", p=P)[:, :, cols], y[:])
 
         low_slices, high_slices, every_slice = [0, 1], [2, 3], [0, 1, 2, 3]
         clutter_part(0, 0, BANK, low_slices)
@@ -310,36 +315,44 @@ def tile_list_radar_log_contrast_kernel(
                 w3_scales[:, 4 * quad : 4 * quad + 4, :].bitcast(I32),
             )
 
-        clutter_part(0, BANK, BANK, low_slices)
+        clutter_part(1, 0, BANK, low_slices)
         quantize_w1(1, 0)
         depths = staged([P, LAYER_TILES, S], F32, "depths", 23 * KB)
         nc.sync.dma_start(depths[:], depth.rearrange("(c p) j -> p c j", p=P))
-        scale_clutter(0, BANK, BANK, low_slices)
+        scale_clutter(1, 0, BANK, low_slices)
         quantize_w1(1, 1)
         target_part(0, 0, BANK, low_slices)
         target_part(0, 0, BANK, high_slices)
         finish_contrast(0, 0, BANK)
-        clutter_part(0, BANK, BANK, high_slices)
-        scale_clutter(0, BANK, BANK, high_slices)
-        target_part(0, BANK, BANK, low_slices)
-        target_part(0, BANK, BANK, high_slices)
-        finish_contrast(0, BANK, BANK)
-        store_codes(0, 0, S)
-        store_scales(0)
+        clutter_part(1, 0, BANK, high_slices)
+        scale_clutter(1, 0, BANK, high_slices)
+        target_part(1, 0, BANK, low_slices)
+        layer_passes(0, 0, BANK)
+        target_part(1, 0, BANK, high_slices)
+        finish_contrast(1, 0, BANK)
+        layer_passes(1, 0, BANK)
 
-        pieces = [(0, 256), (256, 256), (512, 256), (768, 128), (896, 128)]
-        for col0, width in pieces:
-            clutter_part(1, col0, width, every_slice)
-            scale_clutter(1, col0, width, every_slice)
-            layer_passes(0, col0, width)
-            target_part(1, col0, width, every_slice)
-            finish_contrast(1, col0, width)
-            if col0 == 896:
-                finish_layers(768, 128)
-            layer_passes(1, col0, width)
-            if col0 != 768:
-                finish_layers(col0, width)
-            if col0 == 512:
-                store_codes(1, 0, 768)
+        def piece(g, col0, width, behind):
+            clutter_part(g, col0, width, every_slice)
+            scale_clutter(g, col0, width, every_slice)
+            if g == 1:
+                layer_passes(0, col0, width)
+            target_part(g, col0, width, every_slice)
+            finish_contrast(g, col0, width)
+            if behind:
+                finish_layers(*behind)
+            if g == 1:
+                layer_passes(1, col0, width)
+
+        store_codes(0, 0, BANK)
+        piece(0, 512, 256, (0, BANK))
+        piece(1, 512, 256, None)
+        store_codes(1, 0, 768)
+        piece(0, 768, 256, (512, 256))
+        store_codes(0, BANK, S)
+        store_scales(0)
+        piece(1, 768, 128, None)
+        piece(1, 896, 128, (768, 128))
+        finish_layers(896, 128)
         store_codes(1, 768, S)
         store_scales(1)

@@ -215,7 +215,9 @@ def tile_list_radar_log_contrast_kernel(
                     w1_planes[g, a][:, P * t : P * (t + 1)],
                 )
 
-            runs = [(t, cols) for t in slices for cols in (halves(width) if t == PACK - 1 and col0 == 896 else [slice(0, width)])]
+            cut = {BANK: [3], 256: [2, 3], P: [3] if col0 == 896 else []}[width]
+            runs = [(t, slice(0, width)) for t in slices if t not in cut]
+            runs = runs + [(t, cols) for cols in halves(width) for t in slices if t in cut]
             log_energy(contrast[g, col0], stationary, col0, width, slices, width)
             for t, cols in runs:
                 nc.vector.scalar_tensor_tensor(
@@ -231,7 +233,7 @@ def tile_list_radar_log_contrast_kernel(
                 rounded = staged([P, width, PACK], BF16, "h_rounded_last", 52 * KB)
             else:
                 rounded = ring.tile([P, width, PACK], BF16, name="h_rounded", align_bytes=64)
-            parts = halves(width) if col0 == 896 else [slice(0, width)]
+            parts = [slice(0, width)] if (g, col0) == (1, 768) else halves(width)
             for cols in parts:
                 nc.vector.tensor_copy(
                     rounded[:, cols, :].rearrange("p (c i) t -> p c t i", i=2),

@@ -42,7 +42,7 @@ def tile_list_radar_log_contrast_kernel(
         keep = ctx.enter_context(tc.tile_pool(name="keep", bufs=1))
         stage = ctx.enter_context(tc.tile_pool(name="stage", bufs=1))
         ring = ctx.enter_context(tc.tile_pool(name="ring", bufs=2))
-        psum = ctx.enter_context(tc.psum_pool(name="psum", bufs=4))
+        psum = ctx.enter_context(tc.psum_pool(name="psum", bufs=2))
 
         def held(shape, dtype, name):
             return keep.tile(shape, dtype, name=name, align_bytes=64)
@@ -88,29 +88,41 @@ def tile_list_radar_log_contrast_kernel(
         nc.vector.memset(warm[:, 0:1], 1.0)
         nc.scalar.activation(warm[:, 1:2], warm[:, 0:1], ACT.Ln)
 
-        planes = [held([P, PASSES * 2 * BANK], U8, "planes%d" % n) for n in range(2)]
-        for plane in planes:
-            nc.vector.memset(plane[:].bitcast(I32), 0)
-
-        def place_scale_rows(n, picked_at, staging_at):
-            staging = staged([P, 2 * BANK], U8, "staging%d" % n, staging_at)
-            nc.vector.tensor_copy(
-                staging[:, BANK:].rearrange("p (t m) -> p t m", t=PACK),
-                w2_rows[:, n * GROUP : (n + 1) * GROUP].rearrange("p (m t) -> p t m", t=PACK),
-            )
-            picked = staged([P, BANK], U8, "picked_rows%d" % n, picked_at)
-            entries = offsets[:, n * BANK // PER_COLUMN : (n + 1) * BANK // PER_COLUMN]
-            nc.vector.tensor_copy(picked[:], scale_window[:].indirect(entries))
-            nc.vector.tensor_copy(staging[ROWS_AT:P, 0:BANK].bitcast(I32), picked[ROWS_AT:P, :].bitcast(I32))
+        def move_rows(plane, rows):
             for quad in range(QUADS):
                 nc.sync.dma_start(
-                    planes[n][32 * quad : 32 * quad + 4, :].bitcast(I32),
-                    staging[ROWS_AT + 8 * quad : ROWS_AT + 8 * quad + 8, :].bitcast(I32),
+                    plane[32 * quad : 32 * quad + 4, :].bitcast(I32),
+                    rows[ROWS_AT + 8 * quad : ROWS_AT + 8 * quad + 8, :].bitcast(I32),
                 )
 
-        place_scale_rows(0, 17 * KB - 256, 41 * KB)
+        def deal_w2_rows(dst, g):
+            nc.vector.tensor_copy(
+                dst.rearrange("p (t m) -> p t m", t=PACK),
+                w2_rows[:, g * GROUP : (g + 1) * GROUP].rearrange("p (m t) -> p t m", t=PACK),
+            )
+
+        def pick_rows(u, offset):
+            picked = staged([P, BANK], U8, "picked_rows%d" % u, offset)
+            entries = offsets[:, u * BANK // PER_COLUMN : (u + 1) * BANK // PER_COLUMN]
+            nc.vector.tensor_copy(picked[:], scale_window[:].indirect(entries))
+            return picked
+
+        first_plane = held([P, PASSES, 2 * BANK], U8, "first_plane")
+        second_plane = held([P, PASSES, BANK], U8, "second_plane")
+        for plane in (first_plane, second_plane):
+            nc.vector.memset(plane[:].bitcast(I32), 0)
+
+        first_rows = staged([P, 2 * BANK], U8, "first_rows", 41 * KB)
+        deal_w2_rows(first_rows[:, BANK:], 0)
+        picked = pick_rows(0, 17 * KB - 256)
+        nc.vector.tensor_copy(first_rows[ROWS_AT:P, 0:BANK].bitcast(I32), picked[ROWS_AT:P, :].bitcast(I32))
+        move_rows(first_plane[:].rearrange("p a c -> p (a c)"), first_rows)
         tables.append(load_table(1, 17 * KB))
-        place_scale_rows(1, 17 * KB - 512, 51 * KB)
+        second_rows = staged([P, BANK], U8, "second_rows", 16 * KB + 384)
+        deal_w2_rows(second_rows[:], 1)
+        move_rows(second_plane[:].rearrange("p a c -> p (a c)"), second_rows)
+        v_planes = {0: first_plane[:, :, 0:BANK]}
+        w2_planes = {0: first_plane[:, :, BANK:], 1: second_plane[:]}
         deal_w2(0, w2_raw0)
 
         v_codes = {}
@@ -123,11 +135,10 @@ def tile_list_radar_log_contrast_kernel(
                 v_codes[a, u] = picked
 
         gather_words(0)
-        w2_raw1 = staged([P, PASSES, 2 * GROUP], U8, "w2_raw1", 39 * KB + 512)
-        load_w2(1, w2_raw1)
+        late_rows = pick_rows(1, 15 * KB + 512)
 
         w1_raw, w1_codes, w1_planes = {}, {}, {}
-        w1_at = {(0, 0): 41 * KB + 512, (0, 1): 0, (1, 0): 24 * KB, (1, 1): 41 * KB + 512}
+        w1_at = {(0, 0): 41 * KB + 512, (0, 1): 0, (1, 0): 26 * KB, (1, 1): 45 * KB + 512}
 
         def load_w1(g, a):
             raw = staged([P, PACK, GROUP], F32, "w1_raw%d%d" % (g, a), w1_at[g, a])
@@ -150,6 +161,8 @@ def tile_list_radar_log_contrast_kernel(
             w1_codes[g, a], w1_planes[g, a] = codes, plane
 
         load_w1(0, 0)
+        w2_raw1 = staged([P, PASSES, 2 * GROUP], U8, "w2_raw1", 39 * KB + 512)
+        load_w2(1, w2_raw1)
         load_w1(0, 1)
         gains = staged([P, GROUPS, PACK], F32, "gains", 14 * KB)
         nc.sync.dma_start(gains[:], gain.rearrange("(g p t) -> p g t", g=GROUPS, t=PACK))
@@ -157,57 +170,48 @@ def tile_list_radar_log_contrast_kernel(
         deal_w2(1, w2_raw1)
         load_w1(1, 0)
 
-        def log_energy(dst, stationary, col0, width, slices, step):
+        response_banks = [psum.tile([P, BANK], F32, name="response%d" % n, bufs=1) for n in range(6)]
+
+        turns = [0, 1, 2, 3, 4, 5, 0, 1, 2, 3, 0, 1, 4, 5, 0, 1] + [4, 5, 0, 1, 2, 3] * 3
+
+        def responses(stationary, col0, width, slices, step):
             u, start = divmod(col0, BANK)
-            per_bank = BANK // width
-            banks = []
-            for first in range(0, len(slices), per_bank):
-                bank = psum.tile([P, BANK], F32, name="response", tag="response")
-                for place, t in enumerate(slices[first : first + per_bank]):
-                    for sub in range(0, width, step):
-                        for a in range(PASSES):
-                            codes, plane = stationary(a, t)
-                            at = a * 2 * BANK + start + sub
-                            nc.tensor.matmul_mx(
-                                out=bank[:, place * width + sub : place * width + sub + step],
-                                lhsT=codes,
-                                lhsT_scale=plane,
-                                rhs=v_codes[a, u][:, start + sub : start + sub + step].bitcast(FP8X4),
-                                rhs_scale=planes[u][:, at : at + step],
-                                start=(a == 0),
-                                stop=(a == PASSES - 1),
-                            )
-                banks.append(bank)
-            run = dst[:, slices[0] * width : (slices[-1] + 1) * width]
-            for part in halves(len(slices) * width):
-                source = banks[part.start // BANK][:, part.start % BANK : part.start % BANK + part.stop - part.start]
-                nc.scalar.activation(run[:, part], source, ACT.Square)
-            for part in halves(len(slices) * width):
-                nc.scalar.activation(run[:, part], run[:, part], ACT.Ln, bias=1.0)
+            bank = response_banks[turns.pop(0)]
+            for place, t in enumerate(slices):
+                for sub in range(0, width, step):
+                    for a in range(PASSES):
+                        codes, plane = stationary(a, t)
+                        nc.tensor.matmul_mx(
+                            out=bank[:, place * width + sub : place * width + sub + step],
+                            lhsT=codes,
+                            lhsT_scale=plane,
+                            rhs=v_codes[a, u][:, start + sub : start + sub + step].bitcast(FP8X4),
+                            rhs_scale=v_planes[u][:, a, start + sub : start + sub + step],
+                            start=(a == 0),
+                            stop=(a == PASSES - 1),
+                        )
+            return bank
 
-        clutter, scaled, contrast = {}, {}, {}
+        clutter, contrast = {}, {}
 
-        def clutter_part(g, col0, width, slices):
+        def square_clutter(g, col0, width, slices):
             if slices[0] == 0:
-                clutter[g, col0] = ring.tile([P, PACK * width], F32, name="clutter", bufs=3)
+                clutter[g, col0] = held([P, PACK * width], F32, "clutter%d_%d" % (g, col0))
 
             def stationary(a, t):
-                at = a * 2 * BANK + BANK + P * t
-                return w2_codes[g][:, a, 2 * P * t : 2 * P * (t + 1)].bitcast(FP4X4), planes[g][:, at : at + P]
+                return (
+                    w2_codes[g][:, a, 2 * P * t : 2 * P * (t + 1)].bitcast(FP4X4),
+                    w2_planes[g][:, a, P * t : P * (t + 1)],
+                )
 
-            log_energy(clutter[g, col0], stationary, col0, width, slices, BANK if width == BANK else P)
+            bank = responses(stationary, col0, width, slices, BANK if width == BANK else P)
+            run = clutter[g, col0][:, slices[0] * width : (slices[-1] + 1) * width]
+            nc.scalar.activation(run, bank[:], ACT.Square)
+            return run
 
-        def scale_clutter(g, col0, width, slices):
-            src = clutter[g, col0][:].rearrange("p (t j) -> p t j", t=PACK)
-            dst = scaled.get((g, col0), clutter[g, col0])[:].rearrange("p (t j) -> p t j", t=PACK)
-            for t in slices:
-                nc.vector.tensor_scalar_mul(dst[:, t, :], src[:, t, :], gains[:, g, t : t + 1])
-
-        def target_part(g, col0, width, slices):
+        def square_target(g, col0, width, slices):
             if slices[0] == 0:
-                contrast[g, col0] = ring.tile([P, PACK * width], F32, name="contrast", bufs=3)
-            h = contrast[g, col0][:].rearrange("p (t j) -> p t j", t=PACK)
-            other = scaled.get((g, col0), clutter[g, col0])[:].rearrange("p (t j) -> p t j", t=PACK)
+                contrast[g, col0] = held([P, PACK * width], F32, "contrast%d_%d" % (g, col0))
 
             def stationary(a, t):
                 return (
@@ -215,25 +219,61 @@ def tile_list_radar_log_contrast_kernel(
                     w1_planes[g, a][:, P * t : P * (t + 1)],
                 )
 
-            cut = {BANK: [3], 256: [2, 3], P: [3] if col0 == 896 else []}[width]
-            runs = [(t, slice(0, width)) for t in slices if t not in cut]
-            runs = runs + [(t, cols) for cols in halves(width) for t in slices if t in cut]
-            log_energy(contrast[g, col0], stationary, col0, width, slices, width)
+            bank = responses(stationary, col0, width, slices, width)
+            run = contrast[g, col0][:, slices[0] * width : (slices[-1] + 1) * width]
+            nc.scalar.activation(run, bank[:], ACT.Square)
+            return run
+
+        def log1p(run):
+            nc.scalar.activation(run, run, ACT.Ln, bias=1.0)
+
+        def two_banks(square, g, col0, width, first, second):
+            runs = [square(g, col0, width, first), square(g, col0, width, second)]
+            for run in runs:
+                log1p(run)
+
+        scaled = {}
+
+        def scale_clutter(g, col0, slices, result):
+            energy = clutter[g, col0][:].rearrange("p (t j) -> p t j", t=PACK)
+            for place, t in enumerate(slices):
+                nc.vector.tensor_scalar_mul(result[:, place, :], energy[:, t, :], gains[:, g, t : t + 1])
+                scaled[g, col0, t] = result[:, place, :]
+
+        def scale_in_place(g, col0):
+            scale_clutter(g, col0, range(PACK), clutter[g, col0][:].rearrange("p (t j) -> p t j", t=PACK))
+
+        def difference(g, col0, width, clutter0, runs, result):
+            energy = contrast[g, col0][:].rearrange("p (t j) -> p t j", t=PACK)
+            h = result[:].rearrange("p (t j) -> p t j", t=PACK)
+            contrast[g, col0] = result
+            shift = col0 - clutter0
             for t, cols in runs:
                 nc.vector.scalar_tensor_tensor(
-                    h[:, t, cols], h[:, t, cols], gains[:, g, t : t + 1], other[:, t, cols], ALU.mult, ALU.subtract
+                    h[:, t, cols],
+                    energy[:, t, cols],
+                    gains[:, g, t : t + 1],
+                    scaled[g, clutter0, t][:, shift + cols.start : shift + cols.stop],
+                    ALU.mult,
+                    ALU.subtract,
                 )
 
+        SCALE_RANGES = [(0, 768), (768, 1024)]
         h_codes = [held([P, S], U32, "h_codes%d" % g) for g in range(GROUPS)]
-        h_planes = [held([P, S], U8, "h_plane%d" % g) for g in range(GROUPS)]
+        h_planes = {r: held([P, GROUPS, r[1] - r[0]], U8, "h_planes%d" % r[0]) for r in SCALE_RANGES}
 
-        def finish_contrast(g, col0, width):
+        def h_scales(g, col0, col1):
+            first, last = [r for r in SCALE_RANGES if r[0] <= col0 < r[1]][0]
+            return h_planes[first, last][:, g, col0 - first : col1 - first]
+
+        rounded_h = {}
+
+        def round_h(g, col0, width, parts):
             h = contrast[g, col0][:].rearrange("p (t j) -> p t j", t=PACK)
             if (g, col0) == (1, 896):
-                rounded = staged([P, width, PACK], BF16, "h_rounded_last", 52 * KB)
+                rounded = held([P, width, PACK], BF16, "last_rounded")
             else:
-                rounded = ring.tile([P, width, PACK], BF16, name="h_rounded", align_bytes=64)
-            parts = [slice(0, width)] if (g, col0) == (1, 768) else halves(width)
+                rounded = ring.tile([P, width, PACK], BF16, name="h_rounded", align_bytes=64, bufs=3)
             for cols in parts:
                 nc.vector.tensor_copy(
                     rounded[:, cols, :].rearrange("p (c i) t -> p c t i", i=2),
@@ -241,11 +281,14 @@ def tile_list_radar_log_contrast_kernel(
                 )
             rows = out_1[g * GROUP : (g + 1) * GROUP, col0 : col0 + width]
             nc.sync.dma_start(rows.rearrange("(p t) j -> p t j", t=PACK), h)
+            rounded_h[g, col0] = rounded
+
+        def quantize_h(g, col0, parts):
+            rounded = rounded_h[g, col0]
             for cols in parts:
-                words = slice(col0 + cols.start, col0 + cols.stop)
                 nc.vector.quantize_mx(
-                    out=h_codes[g][:, words].bitcast(FP8X4),
-                    scales=h_planes[g][:, words],
+                    out=h_codes[g][:, col0 + cols.start : col0 + cols.stop].bitcast(FP8X4),
+                    scales=h_scales(g, col0 + cols.start, col0 + cols.stop),
                     in_=rounded[:, cols, :].rearrange("p j t -> p (j t)"),
                 )
 
@@ -255,57 +298,60 @@ def tile_list_radar_log_contrast_kernel(
                 h_codes[g][:, col0:col1].bitcast(I32),
             )
 
-        def store_scales(g):
+        def store_scales(queue, col0, col1):
             for quad in range(QUADS):
-                nc.sync.dma_start(
-                    out_3[g, 4 * quad : 4 * quad + 4, :].bitcast(I32),
-                    h_planes[g][32 * quad : 32 * quad + 4, :].bitcast(I32),
+                queue.dma_start(
+                    out_3[:, 4 * quad : 4 * quad + 4, col0:col1].rearrange("g r j -> r g j").bitcast(I32),
+                    h_planes[col0, col1][32 * quad : 32 * quad + 4, :, :].bitcast(I32),
                 )
 
-        layer_banks = {}
+        layer_banks, layer_rows = {}, {}
 
-        def layer_passes(g, col0, width):
+        def layer_passes(col0, width, per_bank):
             cols = slice(col0, col0 + width)
-            per_bank = 2 if col0 == 896 else BANK // width
             for first in range(0, LAYER_TILES, per_bank):
-                if g == 0:
-                    layer_banks[col0, first] = psum.tile([P, per_bank, width], F32, name="layer_sums", tag="layer_sums")
-                for place in range(per_bank):
-                    c = first + place
-                    nc.tensor.matmul_mx(
-                        out=layer_banks[col0, first][:, place, :],
-                        lhsT=w3_codes[:, g, P * c : P * (c + 1)].bitcast(FP8X4),
-                        lhsT_scale=w3_plane[4 * g : P, P * c : P * (c + 1)],
-                        rhs=h_codes[g][:, cols].bitcast(FP8X4),
-                        rhs_scale=h_planes[g][:, cols],
-                        start=(g == 0 and place == 0),
-                        stop=(g == GROUPS - 1 and place == per_bank - 1),
-                    )
+                if col0 in (0, 896):
+                    bank = response_banks[2 + first // per_bank][:, 0 : per_bank * width]
+                    bank = bank.rearrange("p (c j) -> p c j", c=per_bank)
+                else:
+                    bank = psum.tile([P, per_bank, width], F32, name="layer_sums", tag="layer_sums")[:]
+                for g in range(GROUPS):
+                    for place in range(per_bank):
+                        c = first + place
+                        nc.tensor.matmul_mx(
+                            out=bank[:, place, :],
+                            lhsT=w3_codes[:, g, P * c : P * (c + 1)].bitcast(FP8X4),
+                            lhsT_scale=w3_plane[4 * g : P, P * c : P * (c + 1)],
+                            rhs=h_codes[g][:, cols].bitcast(FP8X4),
+                            rhs_scale=h_scales(g, col0, col0 + width),
+                            start=(g == 0 and place == 0),
+                            stop=(g == GROUPS - 1 and place == per_bank - 1),
+                        )
+                layer_banks[col0, first] = bank
 
-        def finish_layers(col0, width):
-            cols = slice(col0, col0 + width)
-            per_bank = 2 if col0 == 896 else BANK // width
-            if col0 == 768:
-                y = staged([P, LAYER_TILES, width], F32, "y_late", 52 * KB)
-            else:
-                y = ring.tile([P, LAYER_TILES, width], F32, name="y", bufs=3)
-            for first in range(0, LAYER_TILES, per_bank):
-                tiles = slice(first, first + per_bank)
-                nc.vector.tensor_tensor(y[:, tiles, :], layer_banks[col0, first][:], depths[:, tiles, cols], ALU.mult)
-                if (width == BANK and first % 2 == 1) or col0 == 896:
-                    pair = slice(first - 1, first + 1) if width == BANK else tiles
-                    nc.sync.dma_start(out_0.rearrange("(c p) j -> p c j", p=P)[:, pair, cols], y[:, pair, :])
-            if width < BANK and col0 != 896:
-                nc.sync.dma_start(out_0.rearrange("(c p) j -> p c j", p=P)[:, :, cols], y[:])
+        def scale_layers(col0, width, tiles):
+            bank = layer_banks[col0, tiles.start]
+            y = layer_rows[col0][:, tiles, :]
+            nc.vector.tensor_tensor(y, bank, depths[:, tiles, col0 : col0 + width], ALU.mult)
 
-        low_slices, high_slices, every_slice = [0, 1], [2, 3], [0, 1, 2, 3]
-        clutter_part(0, 0, BANK, low_slices)
-        clutter_part(0, 0, BANK, high_slices)
+        def store_layers(queue, col0, width, tiles):
+            stored = out_0.rearrange("(c p) j -> p c j", p=P)
+            queue.dma_start(stored[:, tiles, col0 : col0 + width], layer_rows[col0][:, tiles, :])
+
+        def whole(width):
+            return [(t, slice(0, width)) for t in range(PACK)]
+
+        two_banks(square_clutter, 0, 0, BANK, [0], [1])
+        two_banks(square_clutter, 0, 0, BANK, [2], [3])
+        two_banks(square_clutter, 1, 0, BANK, [0], [1])
         quantize_w1(0, 0)
         load_w1(1, 1)
+        scale_clutter(0, 0, [0, 1], staged([P, 2, BANK], F32, "scaled0_low", 41 * KB + 512))
         quantize_w1(0, 1)
-        scaled[0, 0] = staged([P, PACK * BANK], F32, "scaled", 6 * KB)
-        scale_clutter(0, 0, BANK, every_slice)
+        late_plane = staged([P, PASSES, BANK], U8, "late_plane", 4 * KB + 512)
+        nc.vector.memset(late_plane[:].bitcast(I32), 0)
+        move_rows(late_plane[:].rearrange("p a c -> p (a c)"), late_rows)
+        v_planes[1] = late_plane[:]
 
         w3_codes = staged([P, GROUPS, N], I32, "w3_codes", 0)
         nc.sync.dma_start(w3_codes[:], w3_words.rearrange("g p c i -> p g (c i)").bitcast(I32))
@@ -317,44 +363,79 @@ def tile_list_radar_log_contrast_kernel(
                 w3_scales[:, 4 * quad : 4 * quad + 4, :].bitcast(I32),
             )
 
-        clutter_part(1, 0, BANK, low_slices)
+        scale_clutter(0, 0, [2, 3], staged([P, 2, BANK], F32, "scaled0_high", 6 * KB))
         quantize_w1(1, 0)
-        depths = staged([P, LAYER_TILES, S], F32, "depths", 23 * KB)
+        depths = staged([P, LAYER_TILES, S], F32, "depths", 17 * KB)
         nc.sync.dma_start(depths[:], depth.rearrange("(c p) j -> p c j", p=P))
-        scale_clutter(1, 0, BANK, low_slices)
+        scale_clutter(1, 0, [0, 1], staged([P, 2, BANK], F32, "scaled1_low", 33 * KB + 512))
         quantize_w1(1, 1)
-        target_part(0, 0, BANK, low_slices)
-        target_part(0, 0, BANK, high_slices)
-        finish_contrast(0, 0, BANK)
-        clutter_part(1, 0, BANK, high_slices)
-        scale_clutter(1, 0, BANK, high_slices)
-        target_part(1, 0, BANK, low_slices)
-        layer_passes(0, 0, BANK)
-        target_part(1, 0, BANK, high_slices)
-        finish_contrast(1, 0, BANK)
-        layer_passes(1, 0, BANK)
 
-        def piece(g, col0, width, behind):
-            clutter_part(g, col0, width, every_slice)
-            scale_clutter(g, col0, width, every_slice)
-            if g == 1:
-                layer_passes(0, col0, width)
-            target_part(g, col0, width, every_slice)
-            finish_contrast(g, col0, width)
-            if behind:
-                finish_layers(*behind)
-            if g == 1:
-                layer_passes(1, col0, width)
+        def cut(width, slices):
+            runs = [(t, slice(0, width)) for t in range(PACK) if t not in slices]
+            return runs + [(t, cols) for cols in halves(width) for t in slices]
 
+        low, high, every = slice(0, 2), slice(2, 4), slice(0, 4)
+
+        def finish(g, col0, width, clutter0, result):
+            difference(g, col0, width, clutter0, cut(width, [2, 3]), result)
+            round_h(g, col0, width, halves(width))
+            quantize_h(g, col0, halves(width))
+
+        def quarter_energies(g, col0):
+            two_banks(square_clutter, g, col0, 256, [0, 1], [2, 3])
+            scale_in_place(g, col0)
+            two_banks(square_target, g, col0, 256, [0, 1], [2, 3])
+
+        def eighth_energies(g, col0, parts):
+            clutter_run = square_clutter(g, col0, P, [0, 1, 2, 3])
+            target_run = square_target(g, col0, P, [0, 1, 2, 3])
+            log1p(clutter_run)
+            scale_in_place(g, col0)
+            for part in parts:
+                log1p(target_run[:, part])
+
+        def layers(col0, width, per_bank, rows):
+            layer_passes(col0, width, per_bank)
+            layer_rows[col0] = rows
+            for first in range(0, LAYER_TILES, per_bank):
+                scale_layers(col0, width, slice(first, first + per_bank))
+            store_layers(nc.sync, col0, width, every)
+
+        two_banks(square_target, 0, 0, BANK, [0], [1])
+        two_banks(square_target, 0, 0, BANK, [2], [3])
+        two_banks(square_clutter, 1, 0, BANK, [2], [3])
+        difference(0, 0, BANK, 0, cut(BANK, [3]), staged([P, PACK * BANK], F32, "first_h", 45 * KB + 512))
+        round_h(0, 0, BANK, halves(BANK))
+        quantize_h(0, 0, halves(BANK))
         store_codes(0, 0, BANK)
-        piece(0, 512, 256, (0, BANK))
-        piece(1, 512, 256, None)
-        store_codes(1, 0, 768)
-        piece(0, 768, 256, (512, 256))
-        store_codes(0, BANK, S)
-        store_scales(0)
-        piece(1, 768, 128, None)
-        piece(1, 896, 128, (768, 128))
-        finish_layers(896, 128)
+        scale_clutter(1, 0, [2, 3], staged([P, 2, BANK], F32, "scaled1_high", 41 * KB + 512))
+        for col0 in (0, 256):
+            two_banks(square_target, 1, col0, 256, [0, 1], [2, 3])
+            finish(1, col0, 256, 0, contrast[1, col0])
+            layers(col0, 256, 2, held([P, LAYER_TILES, 256], F32, "y%d" % col0))
+        store_codes(1, 0, BANK)
+
+        for g in range(GROUPS):
+            quarter_energies(g, 512)
+            finish(g, 512, 256, 512, contrast[g, 512])
+            store_codes(g, 512, 768)
+        layers(512, 256, 2, held([P, LAYER_TILES, 256], F32, "y512"))
+        store_scales(nc.sync, 0, 768)
+
+        quarter_energies(0, 768)
+        finish(0, 768, 256, 768, contrast[0, 768])
+        store_codes(0, 768, S)
+        eighth_energies(1, 768, [slice(0, BANK)])
+        difference(1, 768, P, 768, whole(P), contrast[1, 768])
+        round_h(1, 768, P, [slice(0, P)])
+        quantize_h(1, 768, [slice(0, P)])
+        eighth_energies(1, 896, halves(BANK))
+        finish(1, 896, P, 896, contrast[1, 896])
         store_codes(1, 768, S)
-        store_scales(1)
+        layers(768, P, 4, held([P, LAYER_TILES, P], F32, "last_rounded"))
+        layer_passes(896, P, 2)
+        layer_rows[896] = held([P, LAYER_TILES, P], F32, "last_y")
+        for tiles in (low, high):
+            scale_layers(896, P, tiles)
+            store_layers(nc.sync, 896, P, tiles)
+        store_scales(nc.sync, 768, 1024)

@@ -135,10 +135,10 @@ def tile_list_radar_log_contrast_kernel(
                 v_codes[a, u] = picked
 
         gather_words(0)
-        late_rows = pick_rows(1, 15 * KB + 512)
+        late_rows = pick_rows(1, 512)
 
         w1_raw, w1_codes, w1_planes = {}, {}, {}
-        w1_at = {(0, 0): 41 * KB + 512, (0, 1): 0, (1, 0): 26 * KB, (1, 1): 45 * KB + 512}
+        w1_at = {(0, 0): 41 * KB + 512, (0, 1): 8 * KB, (1, 0): 26 * KB, (1, 1): 45 * KB + 512}
 
         def load_w1(g, a):
             raw = staged([P, PACK, GROUP], F32, "w1_raw%d%d" % (g, a), w1_at[g, a])
@@ -164,7 +164,7 @@ def tile_list_radar_log_contrast_kernel(
         w2_raw1 = staged([P, PASSES, 2 * GROUP], U8, "w2_raw1", 39 * KB + 512)
         load_w2(1, w2_raw1)
         load_w1(0, 1)
-        gains = staged([P, GROUPS, PACK], F32, "gains", 14 * KB)
+        gains = staged([P, GROUPS, PACK], F32, "gains", 0)
         nc.sync.dma_start(gains[:], gain.rearrange("(g p t) -> p g t", g=GROUPS, t=PACK))
         gather_words(1)
         deal_w2(1, w2_raw1)
@@ -270,10 +270,7 @@ def tile_list_radar_log_contrast_kernel(
 
         def round_h(g, col0, width, parts):
             h = contrast[g, col0][:].rearrange("p (t j) -> p t j", t=PACK)
-            if (g, col0) == (1, 896):
-                rounded = held([P, width, PACK], BF16, "last_rounded")
-            else:
-                rounded = ring.tile([P, width, PACK], BF16, name="h_rounded", align_bytes=64, bufs=3)
+            rounded = ring.tile([P, width, PACK], BF16, name="h_rounded", align_bytes=64, bufs=3)
             for cols in parts:
                 nc.vector.tensor_copy(
                     rounded[:, cols, :].rearrange("p (c i) t -> p c t i", i=2),
@@ -332,7 +329,7 @@ def tile_list_radar_log_contrast_kernel(
         def scale_layers(col0, width, tiles):
             bank = layer_banks[col0, tiles.start]
             y = layer_rows[col0][:, tiles, :]
-            nc.vector.tensor_tensor(y, bank, depths[:, tiles, col0 : col0 + width], ALU.mult)
+            nc.vector.tensor_tensor(y, bank, depths[col0 // BANK][:, tiles, col0 % BANK : col0 % BANK + width], ALU.mult)
 
         def store_layers(queue, col0, width, tiles):
             stored = out_0.rearrange("(c p) j -> p c j", p=P)
@@ -348,14 +345,14 @@ def tile_list_radar_log_contrast_kernel(
         load_w1(1, 1)
         scale_clutter(0, 0, [0, 1], staged([P, 2, BANK], F32, "scaled0_low", 41 * KB + 512))
         quantize_w1(0, 1)
-        late_plane = staged([P, PASSES, BANK], U8, "late_plane", 4 * KB + 512)
+        late_plane = staged([P, PASSES, BANK], U8, "late_plane", 13 * KB + 512)
         nc.vector.memset(late_plane[:].bitcast(I32), 0)
         move_rows(late_plane[:].rearrange("p a c -> p (a c)"), late_rows)
         v_planes[1] = late_plane[:]
 
-        w3_codes = staged([P, GROUPS, N], I32, "w3_codes", 0)
+        w3_codes = staged([P, GROUPS, N], I32, "w3_codes", 9 * KB)
         nc.sync.dma_start(w3_codes[:], w3_words.rearrange("g p c i -> p g (c i)").bitcast(I32))
-        w3_plane = staged([P, N], U8, "w3_plane", 4 * KB)
+        w3_plane = staged([P, N], U8, "w3_plane", 13 * KB)
         nc.vector.memset(w3_plane[:].bitcast(I32), 0)
         for quad in range(QUADS):
             nc.sync.dma_start(
@@ -363,10 +360,16 @@ def tile_list_radar_log_contrast_kernel(
                 w3_scales[:, 4 * quad : 4 * quad + 4, :].bitcast(I32),
             )
 
-        scale_clutter(0, 0, [2, 3], staged([P, 2, BANK], F32, "scaled0_high", 6 * KB))
+        depths = {}
+
+        def load_depth(u, offset):
+            depths[u] = staged([P, LAYER_TILES, BANK], F32, "depths%d" % u, offset)
+            nc.sync.dma_start(depths[u][:], depth.rearrange("(c p) j -> p c j", p=P)[:, :, u * BANK : (u + 1) * BANK])
+
+        load_depth(0, KB)
+        scale_clutter(0, 0, [2, 3], staged([P, 2, BANK], F32, "scaled0_high", 14 * KB + 512))
         quantize_w1(1, 0)
-        depths = staged([P, LAYER_TILES, S], F32, "depths", 17 * KB)
-        nc.sync.dma_start(depths[:], depth.rearrange("(c p) j -> p c j", p=P))
+        load_depth(1, 18 * KB + 512)
         scale_clutter(1, 0, [0, 1], staged([P, 2, BANK], F32, "scaled1_low", 33 * KB + 512))
         quantize_w1(1, 1)
 
@@ -422,17 +425,19 @@ def tile_list_radar_log_contrast_kernel(
         layers(512, 256, 2, held([P, LAYER_TILES, 256], F32, "y512"))
         store_scales(nc.sync, 0, 768)
 
-        quarter_energies(0, 768)
-        finish(0, 768, 256, 768, contrast[0, 768])
-        store_codes(0, 768, S)
-        eighth_energies(1, 768, [slice(0, BANK)])
-        difference(1, 768, P, 768, whole(P), contrast[1, 768])
-        round_h(1, 768, P, [slice(0, P)])
-        quantize_h(1, 768, [slice(0, P)])
-        eighth_energies(1, 896, halves(BANK))
-        finish(1, 896, P, 896, contrast[1, 896])
-        store_codes(1, 768, S)
-        layers(768, P, 4, held([P, LAYER_TILES, P], F32, "last_rounded"))
+        for col0 in (768, 896):
+            for g in range(GROUPS):
+                if (g, col0) == (1, 896):
+                    eighth_energies(g, col0, halves(BANK))
+                    finish(g, col0, P, col0, contrast[g, col0])
+                else:
+                    eighth_energies(g, col0, [slice(0, BANK)])
+                    difference(g, col0, P, col0, whole(P), contrast[g, col0])
+                    round_h(g, col0, P, [slice(0, P)])
+                    quantize_h(g, col0, [slice(0, P)])
+                store_codes(g, col0, col0 + P)
+            if col0 == 768:
+                layers(768, P, 4, held([P, LAYER_TILES, P], F32, "y768"))
         layer_passes(896, P, 2)
         layer_rows[896] = held([P, LAYER_TILES, P], F32, "last_y")
         for tiles in (low, high):

@@ -160,23 +160,22 @@ def tile_list_radar_log_contrast_kernel(
                 nc.vector.quantize_mx(out=codes[:, words].bitcast(FP8X4), scales=plane[:, words], in_=rounded[:, values])
             w1_codes[g, a], w1_planes[g, a] = codes, plane
 
-        load_w1(0, 0)
         w2_raw1 = staged([P, PASSES, 2 * GROUP], U8, "w2_raw1", 39 * KB + 512)
         load_w2(1, w2_raw1)
-        load_w1(0, 1)
+        load_w1(0, 0)
         gains = staged([P, GROUPS, PACK], F32, "gains", 0)
         nc.sync.dma_start(gains[:], gain.rearrange("(g p t) -> p g t", g=GROUPS, t=PACK))
+        load_w1(0, 1)
         gather_words(1)
         deal_w2(1, w2_raw1)
         load_w1(1, 0)
 
         response_banks = [psum.tile([P, BANK], F32, name="response%d" % n, bufs=1) for n in range(6)]
 
-        turns = [0, 1, 2, 3, 4, 5, 0, 1, 2, 3, 0, 1, 4, 5, 0, 1] + [4, 5, 0, 1, 2, 3] * 3
+        turns = [0, 1, 2, 3, 4, 5, 0, 1, 2, 3, 4, 5, 4, 5, 0, 1] + [4, 5, 0, 1, 2, 3] * 3
 
-        def responses(stationary, col0, width, slices, step):
+        def responses(stationary, col0, width, slices, step, bank):
             u, start = divmod(col0, BANK)
-            bank = response_banks[turns.pop(0)]
             for place, t in enumerate(slices):
                 for sub in range(0, width, step):
                     for a in range(PASSES):
@@ -190,7 +189,6 @@ def tile_list_radar_log_contrast_kernel(
                             start=(a == 0),
                             stop=(a == PASSES - 1),
                         )
-            return bank
 
         clutter, contrast = {}, {}
 
@@ -204,8 +202,15 @@ def tile_list_radar_log_contrast_kernel(
                     w2_planes[g][:, a, P * t : P * (t + 1)],
                 )
 
-            bank = responses(stationary, col0, width, slices, BANK if width == BANK else P)
             run = clutter[g, col0][:, slices[0] * width : (slices[-1] + 1) * width]
+            if (g, col0, slices[0]) == (0, 512, 0):
+                bank = psum.tile([P, BANK], F32, name="layer_sums", tag="layer_sums")
+                responses(stationary, col0, width, slices, P, bank)
+                copied = held([P, BANK], F32, "contrast0_0")
+                nc.vector.tensor_copy(copied[:], bank[:])
+                return lambda: nc.vector.tensor_tensor(run, bank[:], copied[:], ALU.mult)
+            bank = response_banks[turns.pop(0)]
+            responses(stationary, col0, width, slices, BANK if width == BANK else P, bank)
             nc.scalar.activation(run, bank[:], ACT.Square)
             return run
 
@@ -219,7 +224,8 @@ def tile_list_radar_log_contrast_kernel(
                     w1_planes[g, a][:, P * t : P * (t + 1)],
                 )
 
-            bank = responses(stationary, col0, width, slices, width)
+            bank = response_banks[turns.pop(0)]
+            responses(stationary, col0, width, slices, width, bank)
             run = contrast[g, col0][:, slices[0] * width : (slices[-1] + 1) * width]
             nc.scalar.activation(run, bank[:], ACT.Square)
             return run
@@ -227,10 +233,12 @@ def tile_list_radar_log_contrast_kernel(
         def log1p(run):
             nc.scalar.activation(run, run, ACT.Ln, bias=1.0)
 
-        def two_banks(square, g, col0, width, first, second):
-            runs = [square(g, col0, width, first), square(g, col0, width, second)]
+        def logs(*runs):
             for run in runs:
                 log1p(run)
+
+        def two_banks(square, g, col0, width, first, second):
+            logs(square(g, col0, width, first), square(g, col0, width, second))
 
         scaled = {}
 
@@ -273,8 +281,8 @@ def tile_list_radar_log_contrast_kernel(
             rounded = ring.tile([P, width, PACK], BF16, name="h_rounded", align_bytes=64, bufs=3)
             for cols in parts:
                 nc.vector.tensor_copy(
-                    rounded[:, cols, :].rearrange("p (c i) t -> p c t i", i=2),
-                    h[:, :, cols].rearrange("p t (c i) -> p c t i", i=2),
+                    rounded[:, cols, :].rearrange("p (c i) t -> p c t i", i=4),
+                    h[:, :, cols].rearrange("p t (c i) -> p c t i", i=4),
                 )
             rows = out_1[g * GROUP : (g + 1) * GROUP, col0 : col0 + width]
             nc.sync.dma_start(rows.rearrange("(p t) j -> p t j", t=PACK), h)
@@ -298,8 +306,8 @@ def tile_list_radar_log_contrast_kernel(
         def store_scales(queue, col0, col1):
             for quad in range(QUADS):
                 queue.dma_start(
-                    out_3[:, 4 * quad : 4 * quad + 4, col0:col1].rearrange("g r j -> r g j").bitcast(I32),
-                    h_planes[col0, col1][32 * quad : 32 * quad + 4, :, :].bitcast(I32),
+                    out_3[:, quad : 16 : 4, col0:col1].rearrange("g q j -> q g j").bitcast(I32),
+                    h_planes[col0, col1][quad : P : 32, :, :].bitcast(I32),
                 )
 
         layer_banks, layer_rows = {}, {}
@@ -308,7 +316,7 @@ def tile_list_radar_log_contrast_kernel(
             cols = slice(col0, col0 + width)
             for first in range(0, LAYER_TILES, per_bank):
                 if col0 in (0, 896):
-                    bank = response_banks[2 + first // per_bank][:, 0 : per_bank * width]
+                    bank = response_banks[(2 if col0 == 0 else 1) + first // per_bank][:, 0 : per_bank * width]
                     bank = bank.rearrange("p (c j) -> p c j", c=per_bank)
                 else:
                     bank = psum.tile([P, per_bank, width], F32, name="layer_sums", tag="layer_sums")[:]
@@ -340,7 +348,7 @@ def tile_list_radar_log_contrast_kernel(
 
         two_banks(square_clutter, 0, 0, BANK, [0], [1])
         two_banks(square_clutter, 0, 0, BANK, [2], [3])
-        two_banks(square_clutter, 1, 0, BANK, [0], [1])
+        two_banks(square_clutter, 1, 0, 256, [0, 1], [2, 3])
         quantize_w1(0, 0)
         load_w1(1, 1)
         scale_clutter(0, 0, [0, 1], staged([P, 2, BANK], F32, "scaled0_low", 41 * KB + 512))
@@ -370,7 +378,7 @@ def tile_list_radar_log_contrast_kernel(
         scale_clutter(0, 0, [2, 3], staged([P, 2, BANK], F32, "scaled0_high", 14 * KB + 512))
         quantize_w1(1, 0)
         load_depth(1, 18 * KB + 512)
-        scale_clutter(1, 0, [0, 1], staged([P, 2, BANK], F32, "scaled1_low", 33 * KB + 512))
+        scale_clutter(1, 0, range(PACK), staged([P, PACK, 256], F32, "scaled1_low", 33 * KB + 512))
         quantize_w1(1, 1)
 
         def cut(width, slices):
@@ -393,51 +401,80 @@ def tile_list_radar_log_contrast_kernel(
             clutter_run = square_clutter(g, col0, P, [0, 1, 2, 3])
             target_run = square_target(g, col0, P, [0, 1, 2, 3])
             log1p(clutter_run)
-            scale_in_place(g, col0)
             for part in parts:
                 log1p(target_run[:, part])
 
-        def layers(col0, width, per_bank, rows):
-            layer_passes(col0, width, per_bank)
-            layer_rows[col0] = rows
-            for first in range(0, LAYER_TILES, per_bank):
-                scale_layers(col0, width, slice(first, first + per_bank))
-            store_layers(nc.sync, col0, width, every)
-
         two_banks(square_target, 0, 0, BANK, [0], [1])
         two_banks(square_target, 0, 0, BANK, [2], [3])
-        two_banks(square_clutter, 1, 0, BANK, [2], [3])
-        difference(0, 0, BANK, 0, cut(BANK, [3]), staged([P, PACK * BANK], F32, "first_h", 45 * KB + 512))
-        round_h(0, 0, BANK, halves(BANK))
-        quantize_h(0, 0, halves(BANK))
+        difference(0, 0, BANK, 0, whole(BANK), staged([P, PACK * BANK], F32, "first_h", 45 * KB + 512))
+        multiply = square_clutter(0, 512, 256, [0, 1])
+        round_h(0, 0, BANK, [slice(0, BANK)])
+        multiply()
+        quantize_h(0, 0, [slice(0, BANK)])
         store_codes(0, 0, BANK)
-        scale_clutter(1, 0, [2, 3], staged([P, 2, BANK], F32, "scaled1_high", 41 * KB + 512))
-        for col0 in (0, 256):
-            two_banks(square_target, 1, col0, 256, [0, 1], [2, 3])
-            finish(1, col0, 256, 0, contrast[1, col0])
-            layers(col0, 256, 2, held([P, LAYER_TILES, 256], F32, "y%d" % col0))
+        def finish_between(g, col0, width, clutter0, first_filler, second_filler):
+            difference(g, col0, width, clutter0, whole(width), contrast[g, col0])
+            first_filler()
+            round_h(g, col0, width, [slice(0, width)])
+            second_filler()
+            quantize_h(g, col0, [slice(0, width)])
+
+        def finish_with_layers(g, col0, width, clutter0, before, before_width, rows):
+            layer_rows[before] = rows
+            finish_between(
+                g,
+                col0,
+                width,
+                clutter0,
+                lambda: scale_layers(before, before_width, low),
+                lambda: scale_layers(before, before_width, high),
+            )
+            store_layers(nc.sync, before, before_width, every)
+
+        def scale_pair(g, col0, pair):
+            energy = clutter[g, col0][:].rearrange("p (t j) -> p t j", t=PACK)
+            scale_clutter(g, col0, range(PACK)[pair], energy[:, pair, :])
+
+        two_banks(square_target, 1, 0, 256, [0, 1], [2, 3])
+        two_banks(square_clutter, 1, 256, 256, [0, 1], [2, 3])
+        finish_between(1, 0, 256, 0, lambda: scale_pair(1, 256, low), lambda: scale_pair(1, 256, high))
+        layer_passes(0, 256, 2)
+        two_banks(square_target, 1, 256, 256, [0, 1], [2, 3])
+        finish_with_layers(1, 256, 256, 256, 0, 256, held([P, LAYER_TILES, 256], F32, "clutter1_256"))
         store_codes(1, 0, BANK)
+        layer_passes(256, 256, 2)
+        logs(clutter[0, 512][:, 0:BANK], square_clutter(0, 512, 256, [2, 3]))
+        scale_in_place(0, 512)
+        two_banks(square_target, 0, 512, 256, [0, 1], [2, 3])
+        finish_with_layers(0, 512, 256, 512, 256, 256, held([P, LAYER_TILES, 256], F32, "clutter0_512"))
+        store_codes(0, 512, 768)
+        def eighth(g, col0, before):
+            eighth_energies(g, col0, halves(BANK) if (g, col0) == (1, 896) else [slice(0, BANK)])
+            scale_in_place(g, col0)
+            if before is None:
+                finish(g, col0, P, col0, contrast[g, col0])
+            else:
+                rows = held([P, LAYER_TILES, col0 - before], F32, "clutter%d_%d" % (g, col0))
+                finish_with_layers(g, col0, P, col0, before, col0 - before, rows)
+            if g == 1 and col0 < 896:
+                layer_passes(col0, P, 4)
 
-        for g in range(GROUPS):
-            quarter_energies(g, 512)
-            finish(g, 512, 256, 512, contrast[g, 512])
-            store_codes(g, 512, 768)
-        layers(512, 256, 2, held([P, LAYER_TILES, 256], F32, "y512"))
+        quarter_energies(1, 512)
+        finish(1, 512, 256, 512, contrast[1, 512])
+        layer_passes(512, 256, 2)
+        store_codes(1, 512, 768)
         store_scales(nc.sync, 0, 768)
-
-        for col0 in (768, 896):
-            for g in range(GROUPS):
-                if (g, col0) == (1, 896):
-                    eighth_energies(g, col0, halves(BANK))
-                    finish(g, col0, P, col0, contrast[g, col0])
-                else:
-                    eighth_energies(g, col0, [slice(0, BANK)])
-                    difference(g, col0, P, col0, whole(P), contrast[g, col0])
-                    round_h(g, col0, P, [slice(0, P)])
-                    quantize_h(g, col0, [slice(0, P)])
-                store_codes(g, col0, col0 + P)
-            if col0 == 768:
-                layers(768, P, 4, held([P, LAYER_TILES, P], F32, "y768"))
+        eighth(0, 768, 512)
+        store_codes(0, 768, 896)
+        eighth(1, 768, None)
+        store_codes(1, 768, 896)
+        layer_rows[768] = held([P, LAYER_TILES, P], F32, "y768")
+        scale_layers(768, P, every)
+        store_layers(nc.sync, 768, P, every)
+        eighth(0, 896, None)
+        store_codes(0, 896, S)
+        eighth(1, 896, None)
+        store_codes(1, 896, S)
         layer_passes(896, P, 2)
         layer_rows[896] = held([P, LAYER_TILES, P], F32, "last_y")
         for tiles in (low, high):

@@ -27,6 +27,8 @@ GROUPS = H // GROUP
 LAYER_TILES = N // P
 ROWS_AT = 96
 KB = 1024
+QUARTER = 256
+PIECES = [(1, 0), (1, 256), (0, 512), (1, 512), (0, 768), (1, 768), (0, 896), (1, 896)]
 
 
 def halves(width):
@@ -50,9 +52,6 @@ def tile_list_radar_log_contrast_kernel(
         def staged(shape, dtype, name, offset):
             return stage.tile(shape, dtype, name=name, align_bytes=64, offset=offset)
 
-        offsets = keep.tile([P, S // PER_COLUMN], U16, name="offsets")
-        nc.sync.dma_start(offsets[:], offs)
-
         def load_scale_rows(name, scales, width):
             rows = held([P, width], U8, name)
             nc.vector.memset(rows[0:ROWS_AT, :].bitcast(I32), 0)
@@ -70,8 +69,7 @@ def tile_list_radar_log_contrast_kernel(
             columns = w2_words[:, :, 2 * GROUP * g : 2 * GROUP * (g + 1)]
             nc.sync.dma_start(raw[:].bitcast(I32), columns.rearrange("a p c -> p a c").bitcast(I32))
 
-        def deal_w2(g, raw):
-            dealt = held([P, PASSES, 2 * GROUP], U8, "w2_codes%d" % g)
+        def deal_w2(g, raw, dealt):
             nc.vector.tensor_copy(
                 dealt[:].bitcast(U16).rearrange("p a (t m) -> p a t m", t=PACK),
                 raw[:].bitcast(U16).rearrange("p a (m t) -> p a t m", t=PACK),
@@ -79,66 +77,62 @@ def tile_list_radar_log_contrast_kernel(
             w2_codes[g] = dealt
 
         scale_window = load_scale_rows("scale_window", tab_scales, T)
+        offsets = keep.tile([P, S // PER_COLUMN], U16, name="offsets")
+        nc.sync.dma_start(offsets[:], offs)
         w2_rows = load_scale_rows("w2_rows", w2_scales, H)
         w2_raw0 = held([P, PASSES, 2 * GROUP], U8, "w2_raw0")
         load_w2(0, w2_raw0)
-        tables = [load_table(0, 0)]
+        tables = [load_table(0, 38 * KB)]
 
         warm = held([P, 2], F32, "warm")
         nc.vector.memset(warm[:, 0:1], 1.0)
         nc.scalar.activation(warm[:, 1:2], warm[:, 0:1], ACT.Ln)
 
-        def move_rows(plane, rows):
-            for quad in range(QUADS):
-                nc.sync.dma_start(
-                    plane[32 * quad : 32 * quad + 4, :].bitcast(I32),
-                    rows[ROWS_AT + 8 * quad : ROWS_AT + 8 * quad + 8, :].bitcast(I32),
-                )
+        def entries(col0, width):
+            return offsets[:, col0 // PER_COLUMN : (col0 + width) // PER_COLUMN]
 
-        def deal_w2_rows(dst, g):
-            nc.vector.tensor_copy(
-                dst.rearrange("p (t m) -> p t m", t=PACK),
-                w2_rows[:, g * GROUP : (g + 1) * GROUP].rearrange("p (m t) -> p t m", t=PACK),
-            )
-
-        def pick_rows(u, offset):
-            picked = staged([P, BANK], U8, "picked_rows%d" % u, offset)
-            entries = offsets[:, u * BANK // PER_COLUMN : (u + 1) * BANK // PER_COLUMN]
-            nc.vector.tensor_copy(picked[:], scale_window[:].indirect(entries))
-            return picked
-
-        first_plane = held([P, PASSES, 2 * BANK], U8, "first_plane")
-        second_plane = held([P, PASSES, BANK], U8, "second_plane")
-        for plane in (first_plane, second_plane):
+        planes = [held([P, PASSES, 2 * BANK], U8, "planes%d" % u) for u in range(2)]
+        for plane in planes:
             nc.vector.memset(plane[:].bitcast(I32), 0)
 
-        first_rows = staged([P, 2 * BANK], U8, "first_rows", 41 * KB)
-        deal_w2_rows(first_rows[:, BANK:], 0)
-        picked = pick_rows(0, 17 * KB - 256)
-        nc.vector.tensor_copy(first_rows[ROWS_AT:P, 0:BANK].bitcast(I32), picked[ROWS_AT:P, :].bitcast(I32))
-        move_rows(first_plane[:].rearrange("p a c -> p (a c)"), first_rows)
-        tables.append(load_table(1, 17 * KB))
-        second_rows = staged([P, BANK], U8, "second_rows", 16 * KB + 384)
-        deal_w2_rows(second_rows[:], 1)
-        move_rows(second_plane[:].rearrange("p a c -> p (a c)"), second_rows)
-        v_planes = {0: first_plane[:, :, 0:BANK]}
-        w2_planes = {0: first_plane[:, :, BANK:], 1: second_plane[:]}
-        deal_w2(0, w2_raw0)
+        def join_and_move(u, picked, joined):
+            nc.vector.tensor_copy(picked[:], scale_window[:].indirect(entries(u * BANK, BANK)))
+            nc.vector.tensor_copy(
+                joined[:, BANK:].rearrange("p (t m) -> p t m", t=PACK),
+                w2_rows[:, u * GROUP : (u + 1) * GROUP].rearrange("p (m t) -> p t m", t=PACK),
+            )
+            nc.vector.tensor_copy(joined[ROWS_AT:P, 0:BANK].bitcast(I32), picked[ROWS_AT:P, :].bitcast(I32))
+            for quad in range(QUADS):
+                nc.sync.dma_start(
+                    planes[u][32 * quad : 32 * quad + 4].rearrange("p a c -> p (a c)").bitcast(I32),
+                    joined[ROWS_AT + 8 * quad : ROWS_AT + 8 * quad + 8, :].bitcast(I32),
+                )
+
+        join_and_move(
+            0, staged([P, BANK], U8, "picked0", 3 * KB + 768), staged([P, 2 * BANK], U8, "joined0", 57 * KB + 512)
+        )
+        tables.append(load_table(1, 4 * KB))
+        join_and_move(1, staged([P, BANK], U8, "picked1", 3 * KB + 512), held([P, 2 * BANK], U8, "joined1"))
+        deal_w2(0, w2_raw0, staged([P, PASSES, 2 * GROUP], U8, "w2_codes0", KB + 768))
 
         v_codes = {}
 
-        def gather_words(a):
-            for u in range(S // BANK):
-                picked = held([P, BANK], U32, "v_codes%d%d" % (a, u))
-                entries = offsets[:, u * BANK // PER_COLUMN : (u + 1) * BANK // PER_COLUMN]
-                nc.vector.tensor_copy(picked[:], tables[a][:].bitcast(U32).indirect(entries))
-                v_codes[a, u] = picked
+        def gather_words(a, col0, width):
+            u, place = divmod(col0, BANK)
+            if place == 0:
+                v_codes[a, u] = held([P, BANK], U32, "v_codes%d_%d" % (a, u))
+            picked = v_codes[a, u][:, place : place + width]
+            nc.vector.tensor_copy(picked, tables[a][:].bitcast(U32).indirect(entries(col0, width)))
 
-        gather_words(0)
-        late_rows = pick_rows(1, 512)
+        def v_operand(a, col0, width):
+            u, place = divmod(col0, BANK)
+            return v_codes[a, u][:, place : place + width].bitcast(FP8X4), planes[u][:, a, place : place + width]
+
+        gather_words(0, BANK, BANK)
+        gather_words(0, 0, BANK)
 
         w1_raw, w1_codes, w1_planes = {}, {}, {}
-        w1_at = {(0, 0): 41 * KB + 512, (0, 1): 8 * KB, (1, 0): 26 * KB, (1, 1): 45 * KB + 512}
+        w1_at = {(0, 0): 58 * KB, (0, 1): 30 * KB + 256, (1, 0): 38 * KB + 256, (1, 1): 46 * KB + 512}
 
         def load_w1(g, a):
             raw = staged([P, PACK, GROUP], F32, "w1_raw%d%d" % (g, a), w1_at[g, a])
@@ -146,9 +140,8 @@ def tile_list_radar_log_contrast_kernel(
             nc.sync.dma_start(raw[:], rows.rearrange("(p i) c -> p i c", i=PACK))
             w1_raw[g, a] = raw
 
-        def quantize_w1(g, a):
+        def quantize_w1(g, a, rounded):
             raw = w1_raw[g, a]
-            rounded = ring.tile([P, PACK * GROUP], BF16, name="w1_rounded", align_bytes=64)
             for pair in halves(PACK):
                 nc.vector.tensor_copy(
                     rounded[:].rearrange("p (t m i) -> p m i t", t=PACK, i=PACK)[:, :, :, pair],
@@ -160,110 +153,168 @@ def tile_list_radar_log_contrast_kernel(
                 nc.vector.quantize_mx(out=codes[:, words].bitcast(FP8X4), scales=plane[:, words], in_=rounded[:, values])
             w1_codes[g, a], w1_planes[g, a] = codes, plane
 
-        w2_raw1 = staged([P, PASSES, 2 * GROUP], U8, "w2_raw1", 39 * KB + 512)
+        w2_raw1 = staged([P, PASSES, 2 * GROUP], U8, "w2_raw1", 56 * KB)
         load_w2(1, w2_raw1)
         load_w1(0, 0)
-        gains = staged([P, GROUPS, PACK], F32, "gains", 0)
+        gains = staged([P, GROUPS, PACK], F32, "gains", 46 * KB + 256)
         nc.sync.dma_start(gains[:], gain.rearrange("(g p t) -> p g t", g=GROUPS, t=PACK))
         load_w1(0, 1)
-        gather_words(1)
-        deal_w2(1, w2_raw1)
         load_w1(1, 0)
+        load_w1(1, 1)
+        gather_words(1, 0, QUARTER)
+        gather_words(1, QUARTER, QUARTER)
+        gather_words(1, BANK, BANK)
+        deal_w2(1, w2_raw1, staged([P, PASSES, 2 * GROUP], U8, "w2_codes1", 4 * KB + 256))
+
+        depths = {}
+
+        def load_depth(u, offset):
+            depths[u] = staged([P, LAYER_TILES, BANK], F32, "depths%d" % u, offset)
+            nc.sync.dma_start(depths[u][:], depth.rearrange("(c p) j -> p c j", p=P)[:, :, u * BANK : (u + 1) * BANK])
+
+        w3_codes = staged([P, GROUPS, N], I32, "w3_codes", 10 * KB + 768)
+        nc.sync.dma_start(w3_codes[:], w3_words.rearrange("g p c i -> p g (c i)").bitcast(I32))
+        load_depth(0, 65 * KB + 768)
+        w3_plane = staged([P, N], U8, "w3_plane", 10 * KB + 256)
+        nc.vector.memset(w3_plane[:].bitcast(I32), 0)
+        for quad in range(QUADS):
+            nc.sync.dma_start(
+                w3_plane[32 * quad : 32 * quad + 8, :].bitcast(I32),
+                w3_scales[:, 4 * quad : 4 * quad + 4, :].bitcast(I32),
+            )
+        load_depth(1, 22 * KB + 512)
 
         response_banks = [psum.tile([P, BANK], F32, name="response%d" % n, bufs=1) for n in range(6)]
+        turns = [0, 1, 2, 3, 4, 5] * 2 + [4, 5, 0, 1, 2, 3] * 4
 
-        turns = [0, 1, 2, 3, 4, 5, 0, 1, 2, 3, 4, 5, 4, 5, 0, 1] + [4, 5, 0, 1, 2, 3] * 3
+        def next_bank():
+            return response_banks[turns.pop(0)]
 
-        def responses(stationary, col0, width, slices, step, bank):
-            u, start = divmod(col0, BANK)
-            for place, t in enumerate(slices):
-                for sub in range(0, width, step):
-                    for a in range(PASSES):
-                        codes, plane = stationary(a, t)
-                        nc.tensor.matmul_mx(
-                            out=bank[:, place * width + sub : place * width + sub + step],
-                            lhsT=codes,
-                            lhsT_scale=plane,
-                            rhs=v_codes[a, u][:, start + sub : start + sub + step].bitcast(FP8X4),
-                            rhs_scale=v_planes[u][:, a, start + sub : start + sub + step],
-                            start=(a == 0),
-                            stop=(a == PASSES - 1),
-                        )
+        def clutter_filters(g, a, t):
+            return (
+                w2_codes[g][:, a, 2 * P * t : 2 * P * (t + 1)].bitcast(FP4X4),
+                planes[g][:, a, BANK + P * t : BANK + P * (t + 1)],
+            )
+
+        def target_filters(g, a, t):
+            return w1_codes[g, a][:, P * t : P * (t + 1)].bitcast(FP8X4), w1_planes[g, a][:, P * t : P * (t + 1)]
+
+        def responses(filters, g, col0, width, slices, bank):
+            for a in range(PASSES):
+                moving, moving_scales = v_operand(a, col0, width)
+                for place, t in enumerate(slices):
+                    codes, plane = filters(g, a, t)
+                    nc.tensor.matmul_mx(
+                        out=bank[:, place * width : (place + 1) * width],
+                        lhsT=codes,
+                        lhsT_scale=plane,
+                        rhs=moving,
+                        rhs_scale=moving_scales,
+                        start=(a == 0 and place == 0),
+                        stop=(a == PASSES - 1 and place == len(slices) - 1),
+                    )
 
         clutter, contrast = {}, {}
+        low, high, every = slice(0, 2), slice(2, 4), slice(0, 4)
 
-        def square_clutter(g, col0, width, slices):
-            if slices[0] == 0:
-                clutter[g, col0] = held([P, PACK * width], F32, "clutter%d_%d" % (g, col0))
+        def by_slice(tile):
+            return tile[:].rearrange("p (t j) -> p t j", t=PACK)
 
-            def stationary(a, t):
-                return (
-                    w2_codes[g][:, a, 2 * P * t : 2 * P * (t + 1)].bitcast(FP4X4),
-                    w2_planes[g][:, a, P * t : P * (t + 1)],
-                )
-
-            run = clutter[g, col0][:, slices[0] * width : (slices[-1] + 1) * width]
-            if (g, col0, slices[0]) == (0, 512, 0):
-                bank = psum.tile([P, BANK], F32, name="layer_sums", tag="layer_sums")
-                responses(stationary, col0, width, slices, P, bank)
-                copied = held([P, BANK], F32, "contrast0_0")
-                nc.vector.tensor_copy(copied[:], bank[:])
-                return lambda: nc.vector.tensor_tensor(run, bank[:], copied[:], ALU.mult)
-            bank = response_banks[turns.pop(0)]
-            responses(stationary, col0, width, slices, BANK if width == BANK else P, bank)
-            nc.scalar.activation(run, bank[:], ACT.Square)
-            return run
-
-        def square_target(g, col0, width, slices):
-            if slices[0] == 0:
-                contrast[g, col0] = held([P, PACK * width], F32, "contrast%d_%d" % (g, col0))
-
-            def stationary(a, t):
-                return (
-                    w1_codes[g, a][:, P * t : P * (t + 1)].bitcast(FP8X4),
-                    w1_planes[g, a][:, P * t : P * (t + 1)],
-                )
-
-            bank = response_banks[turns.pop(0)]
-            responses(stationary, col0, width, slices, width, bank)
-            run = contrast[g, col0][:, slices[0] * width : (slices[-1] + 1) * width]
+        def square(filters, energy, g, col0, width, slices):
+            bank = next_bank()
+            responses(filters, g, col0, width, slices, bank)
+            run = energy[:, slices[0] * width : (slices[-1] + 1) * width]
             nc.scalar.activation(run, bank[:], ACT.Square)
             return run
 
         def log1p(run):
             nc.scalar.activation(run, run, ACT.Ln, bias=1.0)
 
-        def logs(*runs):
+        def quarter_side(filters, energy, g, col0):
+            runs = [square(filters, energy, g, col0, QUARTER, pair) for pair in ([0, 1], [2, 3])]
             for run in runs:
                 log1p(run)
 
-        def two_banks(square, g, col0, width, first, second):
-            logs(square(g, col0, width, first), square(g, col0, width, second))
+        def clutter_quarter(g, col0, energy=None):
+            if (g, col0) in clutter:
+                energy = clutter[g, col0]
+                run = square(clutter_filters, energy, g, col0, QUARTER, [0, 1])
+                log1p(energy[:, BANK:])
+                log1p(run)
+                return
+            clutter[g, col0] = energy or held([P, PACK * QUARTER], F32, "clutter%d_%d" % (g, col0))
+            quarter_side(clutter_filters, clutter[g, col0], g, col0)
+
+        def slot(g, col0):
+            return 83 * KB + 6 * KB * PIECES.index((g, col0))
+
+        def target_quarter(g, col0):
+            contrast[g, col0] = staged([P, PACK * QUARTER], F32, "contrast%d_%d" % (g, col0), slot(g, col0))
+            quarter_side(target_filters, contrast[g, col0], g, col0)
+
+        def clutter_half(g):
+            energy = held([P, PACK * BANK], F32, "clutter%d_0" % g)
+            clutter[g, 0] = energy
+            for col0 in (0, QUARTER):
+                runs = []
+                for pair in (low, high):
+                    bank = next_bank()
+                    responses(clutter_filters, g, col0, QUARTER, range(PACK)[pair], bank)
+                    run = by_slice(energy)[:, pair, col0 : col0 + QUARTER]
+                    nc.scalar.activation(run, bank[:].rearrange("p (t j) -> p t j", t=2), ACT.Square)
+                    runs.append(run)
+                for run in runs:
+                    log1p(run)
+
+        def target_half(g):
+            contrast[g, 0] = held([P, PACK * BANK], F32, "contrast%d_0" % g)
+            for pair in ([0, 1], [2, 3]):
+                runs = [square(target_filters, contrast[g, 0], g, 0, BANK, [t]) for t in pair]
+                for run in runs:
+                    log1p(run)
+
+        def eighth_energies(g, col0, parts):
+            contrast[g, col0] = staged([P, PACK * P], F32, "contrast%d_%d" % (g, col0), slot(g, col0))
+            clutter[g, col0] = held([P, PACK * P], F32, "clutter%d_%d" % (g, col0))
+            clutter_run = square(clutter_filters, clutter[g, col0], g, col0, P, [0, 1, 2, 3])
+            target_run = square(target_filters, contrast[g, col0], g, col0, P, [0, 1, 2, 3])
+            log1p(clutter_run)
+            for part in parts:
+                log1p(target_run[:, part])
 
         scaled = {}
 
-        def scale_clutter(g, col0, slices, result):
-            energy = clutter[g, col0][:].rearrange("p (t j) -> p t j", t=PACK)
-            for place, t in enumerate(slices):
-                nc.vector.tensor_scalar_mul(result[:, place, :], energy[:, t, :], gains[:, g, t : t + 1])
-                scaled[g, col0, t] = result[:, place, :]
+        def scale_clutter(g, col0, results):
+            energy = by_slice(clutter[g, col0])
+            for t in range(PACK):
+                nc.vector.tensor_scalar_mul(results[t], energy[:, t, :], gains[:, g, t : t + 1])
+            scaled[g, col0] = results
 
-        def scale_in_place(g, col0):
-            scale_clutter(g, col0, range(PACK), clutter[g, col0][:].rearrange("p (t j) -> p t j", t=PACK))
+        def scale_into(g, col0, result):
+            scale_clutter(g, col0, [by_slice(result)[:, t, :] for t in range(PACK)])
 
-        def difference(g, col0, width, clutter0, runs, result):
-            energy = contrast[g, col0][:].rearrange("p (t j) -> p t j", t=PACK)
-            h = result[:].rearrange("p (t j) -> p t j", t=PACK)
+        def scale_over_previous(g, col0, width):
+            at = slot(*PIECES[PIECES.index((g, col0)) - 1])
+            first = staged([P, PACK - 1, width], F32, "scaled%d_%d" % (g, col0), at)
+            last = staged([P, width], F32, "last_scaled%d_%d" % (g, col0), at + 4 * (PACK - 1) * width)
+            scale_clutter(g, col0, [first[:, t, :] for t in range(PACK - 1)] + [last[:]])
+
+        def rows_over_scaled(g, col0, width, rows_width):
+            end = slot(*PIECES[PIECES.index((g, col0)) - 1]) + 4 * (PACK - 1) * width
+            return staged([P, LAYER_TILES, rows_width], F32, "layers_at%d_%d" % (g, col0), end - 4 * LAYER_TILES * rows_width)
+
+        def w1_rounded(offset):
+            return staged([P, PACK * GROUP], BF16, "w1_rounded%d" % len(w1_codes), offset)
+
+        def half_tile(name, offset):
+            return staged([P, PACK * BANK], F32, name, offset)
+
+        def difference(g, col0, runs, result):
+            energy, h = by_slice(contrast[g, col0]), by_slice(result)
             contrast[g, col0] = result
-            shift = col0 - clutter0
             for t, cols in runs:
                 nc.vector.scalar_tensor_tensor(
-                    h[:, t, cols],
-                    energy[:, t, cols],
-                    gains[:, g, t : t + 1],
-                    scaled[g, clutter0, t][:, shift + cols.start : shift + cols.stop],
-                    ALU.mult,
-                    ALU.subtract,
+                    h[:, t, cols], energy[:, t, cols], gains[:, g, t : t + 1], scaled[g, col0][t][:, cols], ALU.mult, ALU.subtract
                 )
 
         SCALE_RANGES = [(0, 768), (768, 1024)]
@@ -277,16 +328,43 @@ def tile_list_radar_log_contrast_kernel(
         rounded_h = {}
 
         def round_h(g, col0, width, parts):
-            h = contrast[g, col0][:].rearrange("p (t j) -> p t j", t=PACK)
+            h = by_slice(contrast[g, col0])
             rounded = ring.tile([P, width, PACK], BF16, name="h_rounded", align_bytes=64, bufs=3)
             for cols in parts:
                 nc.vector.tensor_copy(
                     rounded[:, cols, :].rearrange("p (c i) t -> p c t i", i=4),
                     h[:, :, cols].rearrange("p t (c i) -> p c t i", i=4),
                 )
-            rows = out_1[g * GROUP : (g + 1) * GROUP, col0 : col0 + width]
-            nc.sync.dma_start(rows.rearrange("(p t) j -> p t j", t=PACK), h)
             rounded_h[g, col0] = rounded
+
+        def round_on_gpsimd(g, col0, width, cols):
+            h = by_slice(contrast[g, col0])
+            rounded = ring.tile([P, width, PACK], BF16, name="h_rounded", align_bytes=64, bufs=3)
+            nc.gpsimd.tensor_scalar(
+                rounded[:, cols, :], h[:, :, cols].rearrange("p t j -> p j t"), 1.0, 1.0, ALU.mult, ALU.mult
+            )
+            rounded_h[g, col0] = rounded
+
+        def round_rest(g, col0, cols):
+            nc.vector.tensor_copy(
+                rounded_h[g, col0][:, cols, :].rearrange("p (c i) t -> p c t i", i=4),
+                by_slice(contrast[g, col0])[:, :, cols].rearrange("p t (c i) -> p c t i", i=4),
+            )
+
+        def finish_shared(g, col0, width, result, bank_reads, parts):
+            difference(g, col0, whole(width), result)
+            store_h(g, col0, width)
+            round_on_gpsimd(g, col0, width, slice(0, P))
+            for read in bank_reads:
+                read()
+            if width > P:
+                round_rest(g, col0, slice(P, width))
+            quantize_h(g, col0, parts)
+            store_codes(g, col0, col0 + width)
+
+        def store_h(g, col0, width):
+            rows = out_1[g * GROUP : (g + 1) * GROUP, col0 : col0 + width]
+            nc.sync.dma_start(rows.rearrange("(p t) j -> p t j", t=PACK), by_slice(contrast[g, col0]))
 
         def quantize_h(g, col0, parts):
             rounded = rounded_h[g, col0]
@@ -303,181 +381,145 @@ def tile_list_radar_log_contrast_kernel(
                 h_codes[g][:, col0:col1].bitcast(I32),
             )
 
-        def store_scales(queue, col0, col1):
+        def store_scales(col0, col1):
             for quad in range(QUADS):
-                queue.dma_start(
+                nc.sync.dma_start(
                     out_3[:, quad : 16 : 4, col0:col1].rearrange("g q j -> q g j").bitcast(I32),
                     h_planes[col0, col1][quad : P : 32, :, :].bitcast(I32),
                 )
 
         layer_banks, layer_rows = {}, {}
+        spare_banks = [psum.tile([P, BANK], F32, name="spare%d" % n, bufs=1) for n in range(2)]
+        spare_turn = []
 
-        def layer_passes(col0, width, per_bank):
+        def next_spare():
+            spare_turn.append(None)
+            return spare_banks[(len(spare_turn) - 1) % len(spare_banks)]
+
+        def layer_passes(col0, width, tiles):
             cols = slice(col0, col0 + width)
-            for first in range(0, LAYER_TILES, per_bank):
-                if col0 in (0, 896):
-                    bank = response_banks[(2 if col0 == 0 else 1) + first // per_bank][:, 0 : per_bank * width]
-                    bank = bank.rearrange("p (c j) -> p c j", c=per_bank)
-                else:
-                    bank = psum.tile([P, per_bank, width], F32, name="layer_sums", tag="layer_sums")[:]
-                for g in range(GROUPS):
-                    for place in range(per_bank):
-                        c = first + place
-                        nc.tensor.matmul_mx(
-                            out=bank[:, place, :],
-                            lhsT=w3_codes[:, g, P * c : P * (c + 1)].bitcast(FP8X4),
-                            lhsT_scale=w3_plane[4 * g : P, P * c : P * (c + 1)],
-                            rhs=h_codes[g][:, cols].bitcast(FP8X4),
-                            rhs_scale=h_scales(g, col0, col0 + width),
-                            start=(g == 0 and place == 0),
-                            stop=(g == GROUPS - 1 and place == per_bank - 1),
-                        )
-                layer_banks[col0, first] = bank
+            per_bank = tiles.stop - tiles.start
+            bank = next_spare()[:, 0 : per_bank * width].rearrange("p (c j) -> p c j", c=per_bank)
+            for g in range(GROUPS):
+                for place in range(per_bank):
+                    c = tiles.start + place
+                    nc.tensor.matmul_mx(
+                        out=bank[:, place, :],
+                        lhsT=w3_codes[:, g, P * c : P * (c + 1)].bitcast(FP8X4),
+                        lhsT_scale=w3_plane[4 * g : P, P * c : P * (c + 1)],
+                        rhs=h_codes[g][:, cols].bitcast(FP8X4),
+                        rhs_scale=h_scales(g, col0, col0 + width),
+                        start=(g == 0 and place == 0),
+                        stop=(g == GROUPS - 1 and place == per_bank - 1),
+                    )
+            layer_banks[col0, tiles.start] = bank
 
         def scale_layers(col0, width, tiles):
             bank = layer_banks[col0, tiles.start]
             y = layer_rows[col0][:, tiles, :]
             nc.vector.tensor_tensor(y, bank, depths[col0 // BANK][:, tiles, col0 % BANK : col0 % BANK + width], ALU.mult)
 
-        def store_layers(queue, col0, width, tiles):
+        def store_layers(col0, width, tiles):
             stored = out_0.rearrange("(c p) j -> p c j", p=P)
-            queue.dma_start(stored[:, tiles, col0 : col0 + width], layer_rows[col0][:, tiles, :])
+            nc.sync.dma_start(stored[:, tiles, col0 : col0 + width], layer_rows[col0][:, tiles, :])
+
+        def square_on_vector(g, col0, width, slices, copied):
+            bank = next_spare()
+            responses(clutter_filters, g, col0, width, slices, bank)
+            clutter[g, col0] = held([P, PACK * width], F32, "clutter%d_%d" % (g, col0))
+            run = clutter[g, col0][:, slices[0] * width : (slices[-1] + 1) * width]
+
+            def reads():
+                for cols in halves(BANK):
+                    nc.vector.tensor_copy(copied[:, cols], bank[:, cols])
+                for cols in halves(BANK):
+                    nc.vector.tensor_tensor(run[:, cols], bank[:, cols], copied[:, cols], ALU.mult)
+
+            return reads
 
         def whole(width):
             return [(t, slice(0, width)) for t in range(PACK)]
-
-        two_banks(square_clutter, 0, 0, BANK, [0], [1])
-        two_banks(square_clutter, 0, 0, BANK, [2], [3])
-        two_banks(square_clutter, 1, 0, 256, [0, 1], [2, 3])
-        quantize_w1(0, 0)
-        load_w1(1, 1)
-        scale_clutter(0, 0, [0, 1], staged([P, 2, BANK], F32, "scaled0_low", 41 * KB + 512))
-        quantize_w1(0, 1)
-        late_plane = staged([P, PASSES, BANK], U8, "late_plane", 13 * KB + 512)
-        nc.vector.memset(late_plane[:].bitcast(I32), 0)
-        move_rows(late_plane[:].rearrange("p a c -> p (a c)"), late_rows)
-        v_planes[1] = late_plane[:]
-
-        w3_codes = staged([P, GROUPS, N], I32, "w3_codes", 9 * KB)
-        nc.sync.dma_start(w3_codes[:], w3_words.rearrange("g p c i -> p g (c i)").bitcast(I32))
-        w3_plane = staged([P, N], U8, "w3_plane", 13 * KB)
-        nc.vector.memset(w3_plane[:].bitcast(I32), 0)
-        for quad in range(QUADS):
-            nc.sync.dma_start(
-                w3_plane[32 * quad : 32 * quad + 8, :].bitcast(I32),
-                w3_scales[:, 4 * quad : 4 * quad + 4, :].bitcast(I32),
-            )
-
-        depths = {}
-
-        def load_depth(u, offset):
-            depths[u] = staged([P, LAYER_TILES, BANK], F32, "depths%d" % u, offset)
-            nc.sync.dma_start(depths[u][:], depth.rearrange("(c p) j -> p c j", p=P)[:, :, u * BANK : (u + 1) * BANK])
-
-        load_depth(0, KB)
-        scale_clutter(0, 0, [2, 3], staged([P, 2, BANK], F32, "scaled0_high", 14 * KB + 512))
-        quantize_w1(1, 0)
-        load_depth(1, 18 * KB + 512)
-        scale_clutter(1, 0, range(PACK), staged([P, PACK, 256], F32, "scaled1_low", 33 * KB + 512))
-        quantize_w1(1, 1)
 
         def cut(width, slices):
             runs = [(t, slice(0, width)) for t in range(PACK) if t not in slices]
             return runs + [(t, cols) for cols in halves(width) for t in slices]
 
-        low, high, every = slice(0, 2), slice(2, 4), slice(0, 4)
 
-        def finish(g, col0, width, clutter0, result):
-            difference(g, col0, width, clutter0, cut(width, [2, 3]), result)
-            round_h(g, col0, width, halves(width))
-            quantize_h(g, col0, halves(width))
+        def finish(g, col0, width, result=None):
+            difference(g, col0, whole(width), result or contrast[g, col0])
+            store_h(g, col0, width)
+            round_h(g, col0, width, [slice(0, width)])
+            quantize_h(g, col0, [slice(0, width)])
+            store_codes(g, col0, col0 + width)
 
-        def quarter_energies(g, col0):
-            two_banks(square_clutter, g, col0, 256, [0, 1], [2, 3])
-            scale_in_place(g, col0)
-            two_banks(square_target, g, col0, 256, [0, 1], [2, 3])
-
-        def eighth_energies(g, col0, parts):
-            clutter_run = square_clutter(g, col0, P, [0, 1, 2, 3])
-            target_run = square_target(g, col0, P, [0, 1, 2, 3])
-            log1p(clutter_run)
-            for part in parts:
-                log1p(target_run[:, part])
-
-        two_banks(square_target, 0, 0, BANK, [0], [1])
-        two_banks(square_target, 0, 0, BANK, [2], [3])
-        difference(0, 0, BANK, 0, whole(BANK), staged([P, PACK * BANK], F32, "first_h", 45 * KB + 512))
-        multiply = square_clutter(0, 512, 256, [0, 1])
-        round_h(0, 0, BANK, [slice(0, BANK)])
-        multiply()
-        quantize_h(0, 0, [slice(0, BANK)])
-        store_codes(0, 0, BANK)
-        def finish_between(g, col0, width, clutter0, first_filler, second_filler):
-            difference(g, col0, width, clutter0, whole(width), contrast[g, col0])
+        def finish_between(g, col0, width, first_filler, second_filler):
+            difference(g, col0, whole(width), clutter[g, col0])
+            store_h(g, col0, width)
             first_filler()
             round_h(g, col0, width, [slice(0, width)])
             second_filler()
             quantize_h(g, col0, [slice(0, width)])
+            store_codes(g, col0, col0 + width)
 
-        def finish_with_layers(g, col0, width, clutter0, before, before_width, rows):
-            layer_rows[before] = rows
-            finish_between(
-                g,
-                col0,
-                width,
-                clutter0,
-                lambda: scale_layers(before, before_width, low),
-                lambda: scale_layers(before, before_width, high),
-            )
-            store_layers(nc.sync, before, before_width, every)
+        def finish_cut(g, col0, width):
+            difference(g, col0, cut(width, [2, 3]), clutter[g, col0])
+            store_h(g, col0, width)
+            round_h(g, col0, width, halves(width))
+            quantize_h(g, col0, halves(width))
+            store_codes(g, col0, col0 + width)
 
-        def scale_pair(g, col0, pair):
-            energy = clutter[g, col0][:].rearrange("p (t j) -> p t j", t=PACK)
-            scale_clutter(g, col0, range(PACK)[pair], energy[:, pair, :])
+        def layers(col0, width, parts):
+            layer_rows[col0] = held([P, LAYER_TILES, width], F32, "layers%d" % col0)
+            for tiles in parts:
+                layer_passes(col0, width, tiles)
+                scale_layers(col0, width, tiles)
 
-        two_banks(square_target, 1, 0, 256, [0, 1], [2, 3])
-        two_banks(square_clutter, 1, 256, 256, [0, 1], [2, 3])
-        finish_between(1, 0, 256, 0, lambda: scale_pair(1, 256, low), lambda: scale_pair(1, 256, high))
-        layer_passes(0, 256, 2)
-        two_banks(square_target, 1, 256, 256, [0, 1], [2, 3])
-        finish_with_layers(1, 256, 256, 256, 0, 256, held([P, LAYER_TILES, 256], F32, "clutter1_256"))
-        store_codes(1, 0, BANK)
-        layer_passes(256, 256, 2)
-        logs(clutter[0, 512][:, 0:BANK], square_clutter(0, 512, 256, [2, 3]))
-        scale_in_place(0, 512)
-        two_banks(square_target, 0, 512, 256, [0, 1], [2, 3])
-        finish_with_layers(0, 512, 256, 512, 256, 256, held([P, LAYER_TILES, 256], F32, "clutter0_512"))
-        store_codes(0, 512, 768)
-        def eighth(g, col0, before):
-            eighth_energies(g, col0, halves(BANK) if (g, col0) == (1, 896) else [slice(0, BANK)])
-            scale_in_place(g, col0)
-            if before is None:
-                finish(g, col0, P, col0, contrast[g, col0])
+        clutter_half(0)
+        clutter_quarter(1, 0)
+        quantize_w1(0, 0, w1_rounded(6 * KB + 256))
+        quantize_w1(0, 1, w1_rounded(74 * KB))
+        target_half(0)
+        first_scaled = staged([P, PACK - 1, BANK], F32, "scaled0_0", 30 * KB + 512)
+        last_scaled = staged([P, BANK], F32, "last_scaled0_0", 36 * KB + 512)
+        scale_clutter(0, 0, [first_scaled[:, t, :] for t in range(PACK - 1)] + [last_scaled[:]])
+        quantize_w1(1, 0, w1_rounded(78 * KB))
+        quantize_w1(1, 1, w1_rounded(74 * KB))
+        scale_into(1, 0, staged([P, PACK * QUARTER], F32, "scaled1", 46 * KB + 512))
+        target_quarter(1, 0)
+        reads = square_on_vector(0, 512, QUARTER, [2, 3], staged([P, BANK], F32, "copied", 30 * KB + 512))
+        finish_shared(0, 0, BANK, half_tile("first_h", 74 * KB), [reads], [slice(0, BANK)])
+
+        def finish_with_layers(g, col0, width, before, before_width, shared):
+            for tiles in (low, high):
+                layer_passes(before, before_width, tiles)
+            layer_rows[before] = rows_over_scaled(g, col0, width, before_width)
+            reads = [lambda: scale_layers(before, before_width, low), lambda: scale_layers(before, before_width, high)]
+            if shared:
+                finish_shared(g, col0, width, clutter[g, col0], reads, [slice(0, width)])
             else:
-                rows = held([P, LAYER_TILES, col0 - before], F32, "clutter%d_%d" % (g, col0))
-                finish_with_layers(g, col0, P, col0, before, col0 - before, rows)
-            if g == 1 and col0 < 896:
-                layer_passes(col0, P, 4)
+                finish_between(g, col0, width, *reads)
+            store_layers(before, before_width, every)
 
-        quarter_energies(1, 512)
-        finish(1, 512, 256, 512, contrast[1, 512])
-        layer_passes(512, 256, 2)
-        store_codes(1, 512, 768)
-        store_scales(nc.sync, 0, 768)
-        eighth(0, 768, 512)
-        store_codes(0, 768, 896)
-        eighth(1, 768, None)
-        store_codes(1, 768, 896)
-        layer_rows[768] = held([P, LAYER_TILES, P], F32, "y768")
-        scale_layers(768, P, every)
-        store_layers(nc.sync, 768, P, every)
-        eighth(0, 896, None)
-        store_codes(0, 896, S)
-        eighth(1, 896, None)
-        store_codes(1, 896, S)
-        layer_passes(896, P, 2)
-        layer_rows[896] = held([P, LAYER_TILES, P], F32, "last_y")
+        finish_cut(1, 0, QUARTER)
+        for g, col0 in PIECES[1:4]:
+            clutter_quarter(g, col0)
+            target_quarter(g, col0)
+            scale_over_previous(g, col0, QUARTER)
+            if (g, col0) == (1, 512):
+                finish_cut(g, col0, QUARTER)
+            else:
+                finish_with_layers(g, col0, QUARTER, col0 - QUARTER, QUARTER, True)
+        store_scales(0, 768)
+        for g, col0 in PIECES[4:]:
+            eighth_energies(g, col0, halves(BANK) if (g, col0) == PIECES[-1] else [slice(0, BANK)])
+            scale_over_previous(g, col0, P)
+            if g == 1:
+                finish_cut(g, col0, P)
+            elif col0 == 768:
+                finish_with_layers(g, col0, P, 512, QUARTER, True)
+            else:
+                finish_with_layers(g, col0, P, 768, P, False)
+        layers(896, P, [low, high])
         for tiles in (low, high):
-            scale_layers(896, P, tiles)
-            store_layers(nc.sync, 896, P, tiles)
-        store_scales(nc.sync, 768, 1024)
+            store_layers(896, P, tiles)
+        store_scales(768, 1024)

@@ -484,7 +484,9 @@ def tile_list_radar_log_contrast_kernel(
         scale_clutter(0, 0, [first_scaled[:, t, :] for t in range(PACK - 1)] + [last_scaled[:]])
         quantize_w1(1, 0, w1_rounded(78 * KB))
         quantize_w1(1, 1, w1_rounded(74 * KB))
-        scale_into(1, 0, staged([P, PACK * QUARTER], F32, "scaled1", 46 * KB + 512))
+        first_scaled = staged([P, PACK - 1, QUARTER], F32, "scaled1_0", 46 * KB + 512)
+        last_scaled = staged([P, QUARTER], F32, "last_scaled1_0", 49 * KB + 512)
+        scale_clutter(1, 0, [first_scaled[:, t, :] for t in range(PACK - 1)] + [last_scaled[:]])
         target_quarter(1, 0)
         reads = square_on_vector(0, 512, QUARTER, [2, 3], staged([P, BANK], F32, "copied", 30 * KB + 512))
         finish_shared(0, 0, BANK, half_tile("first_h", 74 * KB), [reads], [slice(0, BANK)])
@@ -500,7 +502,8 @@ def tile_list_radar_log_contrast_kernel(
                 finish_between(g, col0, width, *reads)
             store_layers(before, before_width, every)
 
-        finish_cut(1, 0, QUARTER)
+        reads = square_on_vector(1, 512, QUARTER, [2, 3], staged([P, BANK], F32, "copied1", 46 * KB + 512))
+        finish_shared(1, 0, QUARTER, clutter[1, 0], [reads], [slice(0, QUARTER)])
         for g, col0 in PIECES[1:4]:
             clutter_quarter(g, col0)
             target_quarter(g, col0)

@@ -267,7 +267,7 @@ def tile_list_radar_log_contrast_kernel(
                     log1p(run)
 
         def target_half(g):
-            contrast[g, 0] = held([P, PACK * BANK], F32, "contrast%d_0" % g)
+            contrast[g, 0] = staged([P, PACK * BANK], F32, "contrast%d_0" % g, 131 * KB)
             for pair in ([0, 1], [2, 3]):
                 runs = [square(target_filters, contrast[g, 0], g, 0, BANK, [t]) for t in pair]
                 for run in runs:
@@ -284,20 +284,23 @@ def tile_list_radar_log_contrast_kernel(
 
         scaled = {}
 
-        def scale_clutter(g, col0, results):
+        def scale_clutter(g, col0, results, on_gpsimd=()):
             energy = by_slice(clutter[g, col0])
+            for t in on_gpsimd:
+                nc.gpsimd.tensor_scalar(results[t], energy[:, t, :], gains[:, g, t : t + 1], 1.0, ALU.mult, ALU.mult)
             for t in range(PACK):
-                nc.vector.tensor_scalar_mul(results[t], energy[:, t, :], gains[:, g, t : t + 1])
+                if t not in on_gpsimd:
+                    nc.vector.tensor_scalar_mul(results[t], energy[:, t, :], gains[:, g, t : t + 1])
             scaled[g, col0] = results
 
         def scale_into(g, col0, result):
             scale_clutter(g, col0, [by_slice(result)[:, t, :] for t in range(PACK)])
 
-        def scale_over_previous(g, col0, width):
+        def scale_over_previous(g, col0, width, on_gpsimd):
             at = slot(*PIECES[PIECES.index((g, col0)) - 1])
             first = staged([P, PACK - 1, width], F32, "scaled%d_%d" % (g, col0), at)
             last = staged([P, width], F32, "last_scaled%d_%d" % (g, col0), at + 4 * (PACK - 1) * width)
-            scale_clutter(g, col0, [first[:, t, :] for t in range(PACK - 1)] + [last[:]])
+            scale_clutter(g, col0, [first[:, t, :] for t in range(PACK - 1)] + [last[:]], on_gpsimd)
 
         def rows_over_scaled(g, col0, width, rows_width):
             end = slot(*PIECES[PIECES.index((g, col0)) - 1]) + 4 * (PACK - 1) * width
@@ -337,28 +340,12 @@ def tile_list_radar_log_contrast_kernel(
                 )
             rounded_h[g, col0] = rounded
 
-        def round_on_gpsimd(g, col0, width, cols):
-            h = by_slice(contrast[g, col0])
-            rounded = ring.tile([P, width, PACK], BF16, name="h_rounded", align_bytes=64, bufs=3)
-            nc.gpsimd.tensor_scalar(
-                rounded[:, cols, :], h[:, :, cols].rearrange("p t j -> p j t"), 1.0, 1.0, ALU.mult, ALU.mult
-            )
-            rounded_h[g, col0] = rounded
-
-        def round_rest(g, col0, cols):
-            nc.vector.tensor_copy(
-                rounded_h[g, col0][:, cols, :].rearrange("p (c i) t -> p c t i", i=4),
-                by_slice(contrast[g, col0])[:, :, cols].rearrange("p t (c i) -> p c t i", i=4),
-            )
-
         def finish_shared(g, col0, width, result, bank_reads, parts):
             difference(g, col0, whole(width), result)
             store_h(g, col0, width)
-            round_on_gpsimd(g, col0, width, slice(0, P))
             for read in bank_reads:
                 read()
-            if width > P:
-                round_rest(g, col0, slice(P, width))
+            round_h(g, col0, width, parts)
             quantize_h(g, col0, parts)
             store_codes(g, col0, col0 + width)
 
@@ -484,12 +471,13 @@ def tile_list_radar_log_contrast_kernel(
         scale_clutter(0, 0, [first_scaled[:, t, :] for t in range(PACK - 1)] + [last_scaled[:]])
         quantize_w1(1, 0, w1_rounded(78 * KB))
         quantize_w1(1, 1, w1_rounded(74 * KB))
-        first_scaled = staged([P, PACK - 1, QUARTER], F32, "scaled1_0", 46 * KB + 512)
-        last_scaled = staged([P, QUARTER], F32, "last_scaled1_0", 49 * KB + 512)
-        scale_clutter(1, 0, [first_scaled[:, t, :] for t in range(PACK - 1)] + [last_scaled[:]])
+        early = staged([P, 2, QUARTER], F32, "scaled1_0", 46 * KB + 512)
+        third = staged([P, QUARTER], F32, "third_scaled1_0", 132 * KB)
+        last_scaled = staged([P, QUARTER], F32, "last_scaled1_0", 133 * KB)
+        scale_clutter(1, 0, [early[:, 0, :], early[:, 1, :], third[:], last_scaled[:]], [2, 3])
         target_quarter(1, 0)
         reads = square_on_vector(0, 512, QUARTER, [2, 3], staged([P, BANK], F32, "copied", 30 * KB + 512))
-        finish_shared(0, 0, BANK, half_tile("first_h", 74 * KB), [reads], [slice(0, BANK)])
+        finish_shared(0, 0, BANK, half_tile("first_h", 74 * KB), [reads], halves(BANK))
 
         def finish_with_layers(g, col0, width, before, before_width, shared):
             for tiles in (low, high):
@@ -502,12 +490,12 @@ def tile_list_radar_log_contrast_kernel(
                 finish_between(g, col0, width, *reads)
             store_layers(before, before_width, every)
 
-        reads = square_on_vector(1, 512, QUARTER, [2, 3], staged([P, BANK], F32, "copied1", 46 * KB + 512))
+        reads = square_on_vector(1, 512, QUARTER, [2, 3], staged([P, BANK], F32, "copied1", 131 * KB))
         finish_shared(1, 0, QUARTER, clutter[1, 0], [reads], [slice(0, QUARTER)])
         for g, col0 in PIECES[1:4]:
             clutter_quarter(g, col0)
             target_quarter(g, col0)
-            scale_over_previous(g, col0, QUARTER)
+            scale_over_previous(g, col0, QUARTER, [0, 1] if col0 == 256 else [2, 3])
             if (g, col0) == (1, 512):
                 finish_cut(g, col0, QUARTER)
             else:
@@ -515,7 +503,7 @@ def tile_list_radar_log_contrast_kernel(
         store_scales(0, 768)
         for g, col0 in PIECES[4:]:
             eighth_energies(g, col0, halves(BANK) if (g, col0) == PIECES[-1] else [slice(0, BANK)])
-            scale_over_previous(g, col0, P)
+            scale_over_previous(g, col0, P, [0, 1, 2] if (g, col0) == (1, 768) else [])
             if g == 1:
                 finish_cut(g, col0, P)
             elif col0 == 768:

@@ -490,12 +490,11 @@ def tile_list_radar_log_contrast_kernel(
                 finish_between(g, col0, width, *reads)
             store_layers(before, before_width, every)
 
-        reads = square_on_vector(1, 512, QUARTER, [2, 3], staged([P, BANK], F32, "copied1", 131 * KB))
-        finish_shared(1, 0, QUARTER, clutter[1, 0], [reads], [slice(0, QUARTER)])
+        finish_cut(1, 0, QUARTER)
         for g, col0 in PIECES[1:4]:
             clutter_quarter(g, col0)
             target_quarter(g, col0)
-            scale_over_previous(g, col0, QUARTER, [0, 1] if col0 == 256 else [2, 3])
+            scale_over_previous(g, col0, QUARTER, {(1, 256): [], (0, 512): [2, 3], (1, 512): [0, 1]}[g, col0])
             if (g, col0) == (1, 512):
                 finish_cut(g, col0, QUARTER)
             else:

@@ -466,17 +466,16 @@ def tile_list_radar_log_contrast_kernel(
         quantize_w1(0, 0, w1_rounded(6 * KB + 256))
         quantize_w1(0, 1, w1_rounded(74 * KB))
         target_half(0)
-        first_scaled = staged([P, PACK - 1, BANK], F32, "scaled0_0", 30 * KB + 512)
-        last_scaled = staged([P, BANK], F32, "last_scaled0_0", 36 * KB + 512)
-        scale_clutter(0, 0, [first_scaled[:, t, :] for t in range(PACK - 1)] + [last_scaled[:]])
         quantize_w1(1, 0, w1_rounded(78 * KB))
         quantize_w1(1, 1, w1_rounded(74 * KB))
-        early = staged([P, 2, QUARTER], F32, "scaled1_0", 46 * KB + 512)
+        places = (w1_at[0, 1] + 256, w1_at[1, 0], w1_at[1, 1], w1_at[1, 1] + 2 * KB)
+        scale_clutter(0, 0, [staged([P, BANK], F32, "scaled0_%d" % t, at)[:] for t, at in enumerate(places)])
+        early = staged([P, 2, QUARTER], F32, "scaled1_0", w1_at[1, 1] + 4 * KB)
         third = staged([P, QUARTER], F32, "third_scaled1_0", 132 * KB)
         last_scaled = staged([P, QUARTER], F32, "last_scaled1_0", 133 * KB)
         scale_clutter(1, 0, [early[:, 0, :], early[:, 1, :], third[:], last_scaled[:]], [2, 3])
         target_quarter(1, 0)
-        reads = square_on_vector(0, 512, QUARTER, [2, 3], staged([P, BANK], F32, "copied", 30 * KB + 512))
+        reads = square_on_vector(0, 512, QUARTER, [2, 3], staged([P, BANK], F32, "copied", w1_at[1, 1]))
         finish_shared(0, 0, BANK, half_tile("first_h", 74 * KB), [reads], halves(BANK))
 
         def finish_with_layers(g, col0, width, before, before_width, shared):

@@ -28,6 +28,7 @@ LAYER_TILES = N // P
 ROWS_AT = 96
 KB = 1024
 QUARTER = 256
+LAST_AT = 140 * KB
 PIECES = [(1, 0), (1, 256), (0, 512), (1, 512), (0, 768), (1, 768), (0, 896), (1, 896)]
 
 
@@ -259,9 +260,14 @@ def tile_list_radar_log_contrast_kernel(
                 runs = []
                 for pair in (low, high):
                     bank = next_bank()
-                    responses(clutter_filters, g, col0, QUARTER, range(PACK)[pair], bank)
                     run = by_slice(energy)[:, pair, col0 : col0 + QUARTER]
-                    nc.scalar.activation(run, bank[:].rearrange("p (t j) -> p t j", t=2), ACT.Square)
+                    if col0 == 0 and pair == low:
+                        for t, alone in ((0, spare_banks[1]), (1, bank)):
+                            responses(clutter_filters, g, col0, QUARTER, [t], alone)
+                            nc.scalar.activation(run[:, t, :], alone[:, 0:QUARTER], ACT.Square)
+                    else:
+                        responses(clutter_filters, g, col0, QUARTER, range(PACK)[pair], bank)
+                        nc.scalar.activation(run, bank[:].rearrange("p (t j) -> p t j", t=2), ACT.Square)
                     runs.append(run)
                 for run in runs:
                     log1p(run)
@@ -281,6 +287,20 @@ def tile_list_radar_log_contrast_kernel(
             log1p(clutter_run)
             for part in parts:
                 log1p(target_run[:, part])
+
+        last_banks = []
+
+        def last_energies(g, col0):
+            contrast[g, col0] = staged([P, PACK * P], F32, "contrast%d_%d" % (g, col0), slot(g, col0))
+            clutter[g, col0] = held([P, PACK * P], F32, "clutter%d_%d" % (g, col0))
+            for filters, energy in ((clutter_filters, clutter[g, col0]), (target_filters, contrast[g, col0])):
+                bank = next_bank()
+                last_banks.append(bank)
+                responses(filters, g, col0, P, range(PACK), bank)
+                for part in halves(BANK):
+                    nc.scalar.activation(energy[:, part], bank[:, part], ACT.Square)
+                for part in halves(BANK):
+                    log1p(energy[:, part])
 
         scaled = {}
 
@@ -332,7 +352,10 @@ def tile_list_radar_log_contrast_kernel(
 
         def round_h(g, col0, width, parts):
             h = by_slice(contrast[g, col0])
-            rounded = ring.tile([P, width, PACK], BF16, name="h_rounded", align_bytes=64, bufs=3)
+            if (g, col0) == PIECES[-1]:
+                rounded = staged([P, width, PACK], BF16, "last_rounded", LAST_AT)
+            else:
+                rounded = ring.tile([P, width, PACK], BF16, name="h_rounded", align_bytes=64, bufs=3)
             for cols in parts:
                 nc.vector.tensor_copy(
                     rounded[:, cols, :].rearrange("p (c i) t -> p c t i", i=4),
@@ -383,10 +406,10 @@ def tile_list_radar_log_contrast_kernel(
             spare_turn.append(None)
             return spare_banks[(len(spare_turn) - 1) % len(spare_banks)]
 
-        def layer_passes(col0, width, tiles):
+        def layer_passes(col0, width, tiles, bank=None):
             cols = slice(col0, col0 + width)
             per_bank = tiles.stop - tiles.start
-            bank = next_spare()[:, 0 : per_bank * width].rearrange("p (c j) -> p c j", c=per_bank)
+            bank = (bank or next_spare())[:, 0 : per_bank * width].rearrange("p (c j) -> p c j", c=per_bank)
             for g in range(GROUPS):
                 for place in range(per_bank):
                     c = tiles.start + place
@@ -500,15 +523,32 @@ def tile_list_radar_log_contrast_kernel(
                 finish_with_layers(g, col0, QUARTER, col0 - QUARTER, QUARTER, True)
         store_scales(0, 768)
         for g, col0 in PIECES[4:]:
-            eighth_energies(g, col0, halves(BANK) if (g, col0) == PIECES[-1] else [slice(0, BANK)])
-            scale_over_previous(g, col0, P, [0, 1, 2] if (g, col0) == (1, 768) else [])
             if g == 1:
-                finish_cut(g, col0, P)
-            elif col0 == 768:
-                finish_with_layers(g, col0, P, 512, QUARTER, True)
+                last_energies(g, col0)
             else:
-                finish_with_layers(g, col0, P, 768, P, False)
-        layers(896, P, [low, high])
-        for tiles in (low, high):
+                eighth_energies(g, col0, [slice(0, BANK)])
+            scale_over_previous(g, col0, P, [0, 1, 2] if (g, col0) == (1, 768) else [])
+            if (g, col0) == (0, 768):
+                finish_with_layers(g, col0, P, 512, QUARTER, True)
+            elif (g, col0) == (0, 896):
+                layer_passes(768, P, low)
+                layer_rows[768] = rows_over_scaled(g, col0, P, P // 2)[:].rearrange("p (c e) j -> p c (e j)", e=2)
+                difference(g, col0, whole(P), clutter[g, col0])
+                store_h(g, col0, P)
+                scale_layers(768, P, low)
+                store_layers(768, P, low)
+                round_h(g, col0, P, halves(P))
+                quantize_h(g, col0, halves(P))
+                store_codes(g, col0, col0 + P)
+            else:
+                finish_cut(g, col0, P)
+        layer_passes(768, P, high, last_banks[-1])
+        late_rows = staged([P, 2, P], F32, "layers768", LAST_AT)
+        nc.vector.tensor_tensor(late_rows[:], layer_banks[768, 2], depths[1][:, high, 256:384], ALU.mult)
+        nc.sync.dma_start(out_0.rearrange("(c p) j -> p c j", p=P)[:, high, 768:896], late_rows[:])
+        layer_rows[896] = held([P, LAYER_TILES, P], F32, "layers896")
+        for tiles, bank in ((low, next_spare()), (high, next_spare())):
+            layer_passes(896, P, tiles, bank)
+            scale_layers(896, P, tiles)
             store_layers(896, P, tiles)
         store_scales(768, 1024)

@@ -66,23 +66,25 @@ def tile_list_radar_log_contrast_kernel(
 
         w2_codes = {}
 
-        def load_w2(g, raw):
-            columns = w2_words[:, :, 2 * GROUP * g : 2 * GROUP * (g + 1)]
+        def load_w2(g, passes, raw):
+            columns = w2_words[passes, :, 2 * GROUP * g : 2 * GROUP * (g + 1)]
             nc.sync.dma_start(raw[:].bitcast(I32), columns.rearrange("a p c -> p a c").bitcast(I32))
 
-        def deal_w2(g, raw, dealt):
-            nc.vector.tensor_copy(
-                dealt[:].bitcast(U16).rearrange("p a (t m) -> p a t m", t=PACK),
-                raw[:].bitcast(U16).rearrange("p a (m t) -> p a t m", t=PACK),
-            )
-            w2_codes[g] = dealt
+        def deal_w2(g, passes, raw, dealt, parts):
+            for part in parts:
+                nc.vector.tensor_copy(
+                    dealt[:].bitcast(U16).rearrange("p a (t m) -> p a t m", t=PACK)[:, :, part, :],
+                    raw[:].bitcast(U16).rearrange("p a (m t) -> p a t m", t=PACK)[:, :, part, :],
+                )
+            for place, a in enumerate(range(PASSES)[passes]):
+                w2_codes[g, a] = dealt[:, place, :]
 
         scale_window = load_scale_rows("scale_window", tab_scales, T)
         offsets = keep.tile([P, S // PER_COLUMN], U16, name="offsets")
         nc.sync.dma_start(offsets[:], offs)
         w2_rows = load_scale_rows("w2_rows", w2_scales, H)
-        w2_raw0 = held([P, PASSES, 2 * GROUP], U8, "w2_raw0")
-        load_w2(0, w2_raw0)
+        w2_raw0 = staged([P, 1, 2 * GROUP], U8, "w2_raw0", 55 * KB)
+        load_w2(0, slice(0, 1), w2_raw0)
         tables = [load_table(0, 38 * KB)]
 
         warm = held([P, 2], F32, "warm")
@@ -110,30 +112,31 @@ def tile_list_radar_log_contrast_kernel(
                 )
 
         join_and_move(
-            0, staged([P, BANK], U8, "picked0", 3 * KB + 768), staged([P, 2 * BANK], U8, "joined0", 57 * KB + 512)
+            0, staged([P, BANK], U8, "picked0", 3 * KB + 768), staged([P, 2 * BANK], U8, "joined0", 59 * KB)
         )
         tables.append(load_table(1, 4 * KB))
         join_and_move(1, staged([P, BANK], U8, "picked1", 3 * KB + 512), held([P, 2 * BANK], U8, "joined1"))
-        deal_w2(0, w2_raw0, staged([P, PASSES, 2 * GROUP], U8, "w2_codes0", KB + 768))
+        deal_w2(0, slice(0, 1), w2_raw0, staged([P, 1, 2 * GROUP], U8, "w2_codes0", 2 * KB + 768), [slice(0, 4)])
+        w2_late = staged([P, 1, 2 * GROUP], U8, "w2_late", 55 * KB)
+        load_w2(0, slice(1, 2), w2_late)
 
         v_codes = {}
 
-        def gather_words(a, col0, width):
-            u, place = divmod(col0, BANK)
-            if place == 0:
-                v_codes[a, u] = held([P, BANK], U32, "v_codes%d_%d" % (a, u))
-            picked = v_codes[a, u][:, place : place + width]
-            nc.vector.tensor_copy(picked, tables[a][:].bitcast(U32).indirect(entries(col0, width)))
+        def gather_words(a, col0, width, picked=None):
+            picked = picked or held([P, width], U32, "v_codes%d_%d" % (a, col0))
+            nc.vector.tensor_copy(picked[:], tables[a][:].bitcast(U32).indirect(entries(col0, width)))
+            v_codes[a, col0, col0 + width] = picked
 
         def v_operand(a, col0, width):
             u, place = divmod(col0, BANK)
-            return v_codes[a, u][:, place : place + width].bitcast(FP8X4), planes[u][:, a, place : place + width]
+            first, picked = [(c0, t) for (b, c0, c1), t in v_codes.items() if b == a and c0 <= col0 < c1][0]
+            return picked[:, col0 - first : col0 - first + width].bitcast(FP8X4), planes[u][:, a, place : place + width]
 
         gather_words(0, BANK, BANK)
         gather_words(0, 0, BANK)
 
         w1_raw, w1_codes, w1_planes = {}, {}, {}
-        w1_at = {(0, 0): 58 * KB, (0, 1): 30 * KB + 256, (1, 0): 38 * KB + 256, (1, 1): 46 * KB + 512}
+        w1_at = {(0, 0): 59 * KB + 512, (0, 1): 30 * KB + 256, (1, 0): 38 * KB + 256, (1, 1): 46 * KB + 512}
 
         def load_w1(g, a):
             raw = staged([P, PACK, GROUP], F32, "w1_raw%d%d" % (g, a), w1_at[g, a])
@@ -154,8 +157,8 @@ def tile_list_radar_log_contrast_kernel(
                 nc.vector.quantize_mx(out=codes[:, words].bitcast(FP8X4), scales=plane[:, words], in_=rounded[:, values])
             w1_codes[g, a], w1_planes[g, a] = codes, plane
 
-        w2_raw1 = staged([P, PASSES, 2 * GROUP], U8, "w2_raw1", 56 * KB)
-        load_w2(1, w2_raw1)
+        w2_raw1 = staged([P, PASSES, 2 * GROUP], U8, "w2_raw1", 57 * KB + 512)
+        load_w2(1, slice(0, 2), w2_raw1)
         load_w1(0, 0)
         gains = staged([P, GROUPS, PACK], F32, "gains", 46 * KB + 256)
         nc.sync.dma_start(gains[:], gain.rearrange("(g p t) -> p g t", g=GROUPS, t=PACK))
@@ -163,9 +166,10 @@ def tile_list_radar_log_contrast_kernel(
         load_w1(1, 0)
         load_w1(1, 1)
         gather_words(1, 0, QUARTER)
-        gather_words(1, QUARTER, QUARTER)
-        gather_words(1, BANK, BANK)
-        deal_w2(1, w2_raw1, staged([P, PASSES, 2 * GROUP], U8, "w2_codes1", 4 * KB + 256))
+        deal_w2(0, slice(1, 2), w2_late, held([P, 1, 2 * GROUP], U8, "w2_codes_late"), halves(PACK))
+        gather_words(1, QUARTER, QUARTER, staged([P, QUARTER], U32, "v_codes_second", 54 * KB + 512))
+        gather_words(1, BANK, BANK, staged([P, BANK], U32, "v_codes_third", 55 * KB + 512))
+        deal_w2(1, slice(0, 2), w2_raw1, staged([P, PASSES, 2 * GROUP], U8, "w2_codes1", 4 * KB + 256), [slice(0, 4)])
 
         depths = {}
 
@@ -175,7 +179,7 @@ def tile_list_radar_log_contrast_kernel(
 
         w3_codes = staged([P, GROUPS, N], I32, "w3_codes", 10 * KB + 768)
         nc.sync.dma_start(w3_codes[:], w3_words.rearrange("g p c i -> p g (c i)").bitcast(I32))
-        load_depth(0, 65 * KB + 768)
+        load_depth(0, 67 * KB + 256)
         w3_plane = staged([P, N], U8, "w3_plane", 10 * KB + 256)
         nc.vector.memset(w3_plane[:].bitcast(I32), 0)
         for quad in range(QUADS):
@@ -193,7 +197,7 @@ def tile_list_radar_log_contrast_kernel(
 
         def clutter_filters(g, a, t):
             return (
-                w2_codes[g][:, a, 2 * P * t : 2 * P * (t + 1)].bitcast(FP4X4),
+                w2_codes[g, a][:, 2 * P * t : 2 * P * (t + 1)].bitcast(FP4X4),
                 planes[g][:, a, BANK + P * t : BANK + P * (t + 1)],
             )
 
@@ -201,19 +205,23 @@ def tile_list_radar_log_contrast_kernel(
             return w1_codes[g, a][:, P * t : P * (t + 1)].bitcast(FP8X4), w1_planes[g, a][:, P * t : P * (t + 1)]
 
         def responses(filters, g, col0, width, slices, bank):
+            steps = []
             for a in range(PASSES):
-                moving, moving_scales = v_operand(a, col0, width)
                 for place, t in enumerate(slices):
-                    codes, plane = filters(g, a, t)
-                    nc.tensor.matmul_mx(
-                        out=bank[:, place * width : (place + 1) * width],
-                        lhsT=codes,
-                        lhsT_scale=plane,
-                        rhs=moving,
-                        rhs_scale=moving_scales,
-                        start=(a == 0 and place == 0),
-                        stop=(a == PASSES - 1 and place == len(slices) - 1),
-                    )
+                    for cols in halves(width) if a == 1 and width == BANK else [slice(0, width)]:
+                        steps.append((a, place * width, t, cols))
+            for n, (a, at, t, cols) in enumerate(steps):
+                moving, moving_scales = v_operand(a, col0 + cols.start, cols.stop - cols.start)
+                codes, plane = filters(g, a, t)
+                nc.tensor.matmul_mx(
+                    out=bank[:, at + cols.start : at + cols.stop],
+                    lhsT=codes,
+                    lhsT_scale=plane,
+                    rhs=moving,
+                    rhs_scale=moving_scales,
+                    start=(n == 0),
+                    stop=(n == len(steps) - 1),
+                )
 
         clutter, contrast = {}, {}
         low, high, every = slice(0, 2), slice(2, 4), slice(0, 4)
@@ -247,7 +255,7 @@ def tile_list_radar_log_contrast_kernel(
             quarter_side(clutter_filters, clutter[g, col0], g, col0)
 
         def slot(g, col0):
-            return 83 * KB + 6 * KB * PIECES.index((g, col0))
+            return 83 * KB + 512 + 6 * KB * PIECES.index((g, col0))
 
         def target_quarter(g, col0):
             contrast[g, col0] = staged([P, PACK * QUARTER], F32, "contrast%d_%d" % (g, col0), slot(g, col0))
@@ -374,7 +382,8 @@ def tile_list_radar_log_contrast_kernel(
 
         def store_h(g, col0, width):
             rows = out_1[g * GROUP : (g + 1) * GROUP, col0 : col0 + width]
-            nc.sync.dma_start(rows.rearrange("(p t) j -> p t j", t=PACK), by_slice(contrast[g, col0]))
+            for part in halves(PACK) if (g, col0) == PIECES[-1] else [every]:
+                nc.sync.dma_start(rows.rearrange("(p t) j -> p t j", t=PACK)[:, part, :], by_slice(contrast[g, col0])[:, part, :])
 
         def quantize_h(g, col0, parts):
             rounded = rounded_h[g, col0]
@@ -487,10 +496,10 @@ def tile_list_radar_log_contrast_kernel(
         clutter_half(0)
         clutter_quarter(1, 0)
         quantize_w1(0, 0, w1_rounded(6 * KB + 256))
-        quantize_w1(0, 1, w1_rounded(74 * KB))
+        quantize_w1(0, 1, w1_rounded(75 * KB + 512))
         target_half(0)
-        quantize_w1(1, 0, w1_rounded(78 * KB))
-        quantize_w1(1, 1, w1_rounded(74 * KB))
+        quantize_w1(1, 0, w1_rounded(79 * KB + 512))
+        quantize_w1(1, 1, w1_rounded(75 * KB + 512))
         places = (w1_at[0, 1] + 256, w1_at[1, 0], w1_at[1, 1], w1_at[1, 1] + 2 * KB)
         scale_clutter(0, 0, [staged([P, BANK], F32, "scaled0_%d" % t, at)[:] for t, at in enumerate(places)])
         early = staged([P, 2, QUARTER], F32, "scaled1_0", w1_at[1, 1] + 4 * KB)
@@ -499,7 +508,7 @@ def tile_list_radar_log_contrast_kernel(
         scale_clutter(1, 0, [early[:, 0, :], early[:, 1, :], third[:], last_scaled[:]], [2, 3])
         target_quarter(1, 0)
         reads = square_on_vector(0, 512, QUARTER, [2, 3], staged([P, BANK], F32, "copied", w1_at[1, 1]))
-        finish_shared(0, 0, BANK, half_tile("first_h", 74 * KB), [reads], halves(BANK))
+        finish_shared(0, 0, BANK, half_tile("first_h", 75 * KB + 512), [reads], halves(BANK))
 
         def finish_with_layers(g, col0, width, before, before_width, shared):
             for tiles in (low, high):

@@ -105,7 +105,7 @@ def tile_list_radar_log_contrast_kernel(
                 w2_rows[:, u * GROUP : (u + 1) * GROUP].rearrange("p (m t) -> p t m", t=PACK),
             )
             nc.vector.tensor_copy(joined[ROWS_AT:P, 0:BANK].bitcast(I32), picked[ROWS_AT:P, :].bitcast(I32))
-            for quad in range(QUADS):
+            for quad in (0, 2, 1, 3):
                 nc.sync.dma_start(
                     planes[u][32 * quad : 32 * quad + 4].rearrange("p a c -> p (a c)").bitcast(I32),
                     joined[ROWS_AT + 8 * quad : ROWS_AT + 8 * quad + 8, :].bitcast(I32),

@@ -83,7 +83,7 @@ def tile_list_radar_log_contrast_kernel(
         offsets = keep.tile([P, S // PER_COLUMN], U16, name="offsets")
         nc.sync.dma_start(offsets[:], offs)
         w2_rows = load_scale_rows("w2_rows", w2_scales, H)
-        w2_raw0 = staged([P, 1, 2 * GROUP], U8, "w2_raw0", 55 * KB)
+        w2_raw0 = staged([P, 1, 2 * GROUP], U8, "w2_raw0", 54 * KB + 768)
         load_w2(0, slice(0, 1), w2_raw0)
         tables = [load_table(0, 38 * KB)]
 
@@ -115,10 +115,10 @@ def tile_list_radar_log_contrast_kernel(
             0, staged([P, BANK], U8, "picked0", 3 * KB + 768), staged([P, 2 * BANK], U8, "joined0", 59 * KB)
         )
         tables.append(load_table(1, 4 * KB))
-        join_and_move(1, staged([P, BANK], U8, "picked1", 3 * KB + 512), held([P, 2 * BANK], U8, "joined1"))
-        deal_w2(0, slice(0, 1), w2_raw0, staged([P, 1, 2 * GROUP], U8, "w2_codes0", 2 * KB + 768), [slice(0, 4)])
+        deal_w2(0, slice(0, 1), w2_raw0, staged([P, 1, 2 * GROUP], U8, "w2_codes0", 3 * KB), [slice(0, 4)])
         w2_late = staged([P, 1, 2 * GROUP], U8, "w2_late", 55 * KB)
         load_w2(0, slice(1, 2), w2_late)
+        join_and_move(1, staged([P, BANK], U8, "picked1", 54 * KB + 512), held([P, 2 * BANK], U8, "joined1"))
 
         v_codes = {}
 

@@ -83,7 +83,7 @@ def tile_list_radar_log_contrast_kernel(
         offsets = keep.tile([P, S // PER_COLUMN], U16, name="offsets")
         nc.sync.dma_start(offsets[:], offs)
         w2_rows = load_scale_rows("w2_rows", w2_scales, H)
-        w2_raw0 = staged([P, 1, 2 * GROUP], U8, "w2_raw0", 54 * KB + 768)
+        w2_raw0 = staged([P, 1, 2 * GROUP], U8, "w2_raw0", 57 * KB + 512)
         load_w2(0, slice(0, 1), w2_raw0)
         tables = [load_table(0, 38 * KB)]
 
@@ -94,49 +94,61 @@ def tile_list_radar_log_contrast_kernel(
         def entries(col0, width):
             return offsets[:, col0 // PER_COLUMN : (col0 + width) // PER_COLUMN]
 
-        planes = [held([P, PASSES, 2 * BANK], U8, "planes%d" % u) for u in range(2)]
-        for plane in planes:
+        first_planes = [held([P, 2 * BANK], U8, "first_planes%d" % a) for a in range(PASSES)]
+        second_planes = held([P, PASSES, 2 * BANK], U8, "second_planes")
+        for plane in first_planes + [second_planes]:
             nc.vector.memset(plane[:].bitcast(I32), 0)
 
-        def join_and_move(u, picked, joined):
+        def plane_of(u, a):
+            return first_planes[a][:] if u == 0 else second_planes[:, a, :]
+
+        def join(u, picked, joined):
             nc.vector.tensor_copy(picked[:], scale_window[:].indirect(entries(u * BANK, BANK)))
             nc.vector.tensor_copy(
                 joined[:, BANK:].rearrange("p (t m) -> p t m", t=PACK),
                 w2_rows[:, u * GROUP : (u + 1) * GROUP].rearrange("p (m t) -> p t m", t=PACK),
             )
             nc.vector.tensor_copy(joined[ROWS_AT:P, 0:BANK].bitcast(I32), picked[ROWS_AT:P, :].bitcast(I32))
+            return joined
+
+        def move_one_pass(joined, a):
+            for quad in (0, 2, 1, 3):
+                first = ROWS_AT + 8 * quad + a
+                nc.sync.dma_start(
+                    first_planes[a][32 * quad : 32 * quad + 4, :].bitcast(I32),
+                    joined[first : first + 7 : 2, :].bitcast(I32),
+                )
+
+        def move_both_passes(joined):
             for quad in (0, 2, 1, 3):
                 nc.sync.dma_start(
-                    planes[u][32 * quad : 32 * quad + 4].rearrange("p a c -> p (a c)").bitcast(I32),
+                    second_planes[32 * quad : 32 * quad + 4].rearrange("p a c -> p (a c)").bitcast(I32),
                     joined[ROWS_AT + 8 * quad : ROWS_AT + 8 * quad + 8, :].bitcast(I32),
                 )
 
-        join_and_move(
-            0, staged([P, BANK], U8, "picked0", 3 * KB + 768), staged([P, 2 * BANK], U8, "joined0", 59 * KB)
-        )
+        joined0 = join(0, staged([P, BANK], U8, "picked0", 3 * KB + 768), held([P, 2 * BANK], U8, "joined0"))
+        move_one_pass(joined0, 0)
         tables.append(load_table(1, 4 * KB))
         deal_w2(0, slice(0, 1), w2_raw0, staged([P, 1, 2 * GROUP], U8, "w2_codes0", 3 * KB), [slice(0, 4)])
-        w2_late = staged([P, 1, 2 * GROUP], U8, "w2_late", 55 * KB)
+        w2_late = staged([P, 1, 2 * GROUP], U8, "w2_late", 56 * KB + 768)
         load_w2(0, slice(1, 2), w2_late)
-        join_and_move(1, staged([P, BANK], U8, "picked1", 54 * KB + 512), held([P, 2 * BANK], U8, "joined1"))
+        move_one_pass(joined0, 1)
 
         v_codes = {}
 
         def gather_words(a, col0, width, picked=None):
-            picked = picked or held([P, width], U32, "v_codes%d_%d" % (a, col0))
-            nc.vector.tensor_copy(picked[:], tables[a][:].bitcast(U32).indirect(entries(col0, width)))
+            if picked is None:
+                picked = held([P, width], U32, "v_codes%d_%d" % (a, col0))[:]
+            nc.vector.tensor_copy(picked, tables[a][:].bitcast(U32).indirect(entries(col0, width)))
             v_codes[a, col0, col0 + width] = picked
 
         def v_operand(a, col0, width):
             u, place = divmod(col0, BANK)
             first, picked = [(c0, t) for (b, c0, c1), t in v_codes.items() if b == a and c0 <= col0 < c1][0]
-            return picked[:, col0 - first : col0 - first + width].bitcast(FP8X4), planes[u][:, a, place : place + width]
-
-        gather_words(0, BANK, BANK)
-        gather_words(0, 0, BANK)
+            return picked[:, col0 - first : col0 - first + width].bitcast(FP8X4), plane_of(u, a)[:, place : place + width]
 
         w1_raw, w1_codes, w1_planes = {}, {}, {}
-        w1_at = {(0, 0): 59 * KB + 512, (0, 1): 30 * KB + 256, (1, 0): 38 * KB + 256, (1, 1): 46 * KB + 512}
+        w1_at = {(0, 0): 58 * KB + 256, (0, 1): 30 * KB + 256, (1, 0): 46 * KB, (1, 1): 58 * KB + 256}
 
         def load_w1(g, a):
             raw = staged([P, PACK, GROUP], F32, "w1_raw%d%d" % (g, a), w1_at[g, a])
@@ -157,19 +169,22 @@ def tile_list_radar_log_contrast_kernel(
                 nc.vector.quantize_mx(out=codes[:, words].bitcast(FP8X4), scales=plane[:, words], in_=rounded[:, values])
             w1_codes[g, a], w1_planes[g, a] = codes, plane
 
-        w2_raw1 = staged([P, PASSES, 2 * GROUP], U8, "w2_raw1", 57 * KB + 512)
-        load_w2(1, slice(0, 2), w2_raw1)
         load_w1(0, 0)
-        gains = staged([P, GROUPS, PACK], F32, "gains", 46 * KB + 256)
+        picked1 = staged([P, BANK], U8, "picked1", 57 * KB + 768)
+        move_both_passes(join(1, picked1, held([P, 2 * BANK], U8, "joined1")))
+        gather_words(0, BANK, BANK)
+        gather_words(0, 0, BANK)
+        gains = staged([P, GROUPS, PACK], F32, "gains", 45 * KB + 768)
         nc.sync.dma_start(gains[:], gain.rearrange("(g p t) -> p g t", g=GROUPS, t=PACK))
         load_w1(0, 1)
+        w2_raw1 = staged([P, PASSES, 2 * GROUP], U8, "w2_raw1", 39 * KB)
+        load_w2(1, slice(0, 2), w2_raw1)
         load_w1(1, 0)
-        load_w1(1, 1)
         gather_words(1, 0, QUARTER)
         deal_w2(0, slice(1, 2), w2_late, held([P, 1, 2 * GROUP], U8, "w2_codes_late"), halves(PACK))
-        gather_words(1, QUARTER, QUARTER, staged([P, QUARTER], U32, "v_codes_second", 54 * KB + 512))
-        gather_words(1, BANK, BANK, staged([P, BANK], U32, "v_codes_third", 55 * KB + 512))
-        deal_w2(1, slice(0, 2), w2_raw1, staged([P, PASSES, 2 * GROUP], U8, "w2_codes1", 4 * KB + 256), [slice(0, 4)])
+        later_words = staged([P, S - QUARTER], U32, "later_words", 54 * KB)
+        for col0 in range(QUARTER, S, QUARTER):
+            gather_words(1, col0, QUARTER, later_words[:, col0 - QUARTER : col0])
 
         depths = {}
 
@@ -177,20 +192,20 @@ def tile_list_radar_log_contrast_kernel(
             depths[u] = staged([P, LAYER_TILES, BANK], F32, "depths%d" % u, offset)
             nc.sync.dma_start(depths[u][:], depth.rearrange("(c p) j -> p c j", p=P)[:, :, u * BANK : (u + 1) * BANK])
 
-        w3_codes = staged([P, GROUPS, N], I32, "w3_codes", 10 * KB + 768)
-        nc.sync.dma_start(w3_codes[:], w3_words.rearrange("g p c i -> p g (c i)").bitcast(I32))
-        load_depth(0, 67 * KB + 256)
-        w3_plane = staged([P, N], U8, "w3_plane", 10 * KB + 256)
-        nc.vector.memset(w3_plane[:].bitcast(I32), 0)
-        for quad in range(QUADS):
-            nc.sync.dma_start(
-                w3_plane[32 * quad : 32 * quad + 8, :].bitcast(I32),
-                w3_scales[:, 4 * quad : 4 * quad + 4, :].bitcast(I32),
-            )
-        load_depth(1, 22 * KB + 512)
+        def load_w3():
+            codes = staged([P, GROUPS, N], I32, "w3_codes", 10 * KB)
+            nc.sync.dma_start(codes[:], w3_words.rearrange("g p c i -> p g (c i)").bitcast(I32))
+            plane = staged([P, N], U8, "w3_plane", 6 * KB)
+            nc.vector.memset(plane[:].bitcast(I32), 0)
+            for quad in range(QUADS):
+                nc.sync.dma_start(
+                    plane[32 * quad : 32 * quad + 8, :].bitcast(I32),
+                    w3_scales[:, 4 * quad : 4 * quad + 4, :].bitcast(I32),
+                )
+            return codes, plane
 
         response_banks = [psum.tile([P, BANK], F32, name="response%d" % n, bufs=1) for n in range(6)]
-        turns = [0, 1, 2, 3, 4, 5] * 2 + [4, 5, 0, 1, 2, 3] * 4
+        turns = [0, 1, 2, 3] + [4, 5] * 4 + [0, 1, 0, 1, 2, 3, 2, 3, 0, 4, 5, 1, 2, 3, 0, 4, 5, 1, 2]
 
         def next_bank():
             return response_banks[turns.pop(0)]
@@ -198,7 +213,7 @@ def tile_list_radar_log_contrast_kernel(
         def clutter_filters(g, a, t):
             return (
                 w2_codes[g, a][:, 2 * P * t : 2 * P * (t + 1)].bitcast(FP4X4),
-                planes[g][:, a, BANK + P * t : BANK + P * (t + 1)],
+                plane_of(g, a)[:, BANK + P * t : BANK + P * (t + 1)],
             )
 
         def target_filters(g, a, t):
@@ -255,7 +270,7 @@ def tile_list_radar_log_contrast_kernel(
             quarter_side(clutter_filters, clutter[g, col0], g, col0)
 
         def slot(g, col0):
-            return 83 * KB + 512 + 6 * KB * PIECES.index((g, col0))
+            return 85 * KB + 6 * KB * PIECES.index((g, col0))
 
         def target_quarter(g, col0):
             contrast[g, col0] = staged([P, PACK * QUARTER], F32, "contrast%d_%d" % (g, col0), slot(g, col0))
@@ -320,6 +335,11 @@ def tile_list_radar_log_contrast_kernel(
                 if t not in on_gpsimd:
                     nc.vector.tensor_scalar_mul(results[t], energy[:, t, :], gains[:, g, t : t + 1])
             scaled[g, col0] = results
+
+        def gain_on_gpsimd(g, col0, slices, results):
+            energy = by_slice(clutter[g, col0])
+            for t, result in zip(slices, results):
+                nc.gpsimd.tensor_scalar(result, energy[:, t, :], gains[:, g, t : t + 1], 1.0, ALU.mult, ALU.mult)
 
         def scale_into(g, col0, result):
             scale_clutter(g, col0, [by_slice(result)[:, t, :] for t in range(PACK)])
@@ -494,21 +514,32 @@ def tile_list_radar_log_contrast_kernel(
                 scale_layers(col0, width, tiles)
 
         clutter_half(0)
-        clutter_quarter(1, 0)
+        clutter_quarter(0, 512)
         quantize_w1(0, 0, w1_rounded(6 * KB + 256))
-        quantize_w1(0, 1, w1_rounded(75 * KB + 512))
+        load_w1(1, 1)
+        w3_codes, w3_plane = load_w3()
+        quantize_w1(0, 1, w1_rounded(68 * KB))
+        load_depth(0, 22 * KB + 512)
+        deal_w2(1, slice(0, 2), w2_raw1, held([P, PASSES, 2 * GROUP], U8, "w2_codes1"), [slice(0, 4)])
         target_half(0)
-        quantize_w1(1, 0, w1_rounded(79 * KB + 512))
-        quantize_w1(1, 1, w1_rounded(75 * KB + 512))
-        places = (w1_at[0, 1] + 256, w1_at[1, 0], w1_at[1, 1], w1_at[1, 1] + 2 * KB)
+        quantize_w1(1, 0, w1_rounded(72 * KB))
+        load_depth(1, 75 * KB + 768)
+        places = [w1_at[0, 1] + 256 + 2 * KB * t for t in range(PACK)]
         scale_clutter(0, 0, [staged([P, BANK], F32, "scaled0_%d" % t, at)[:] for t, at in enumerate(places)])
-        early = staged([P, 2, QUARTER], F32, "scaled1_0", w1_at[1, 1] + 4 * KB)
-        third = staged([P, QUARTER], F32, "third_scaled1_0", 132 * KB)
-        last_scaled = staged([P, QUARTER], F32, "last_scaled1_0", 133 * KB)
-        scale_clutter(1, 0, [early[:, 0, :], early[:, 1, :], third[:], last_scaled[:]], [2, 3])
+        quantize_w1(1, 1, w1_rounded(68 * KB))
+        clutter_quarter(1, 0)
         target_quarter(1, 0)
-        reads = square_on_vector(0, 512, QUARTER, [2, 3], staged([P, BANK], F32, "copied", w1_at[1, 1]))
-        finish_shared(0, 0, BANK, half_tile("first_h", 75 * KB + 512), [reads], halves(BANK))
+        reads = square_on_vector(1, 512, QUARTER, [2, 3], staged([P, BANK], F32, "copied", places[2]))
+        third_quarter = [staged([P, QUARTER], F32, "scaled0_512_%d" % t, (131 + t) * KB)[:] for t in range(2)]
+        first_h = half_tile("first_h", w1_at[1, 0])
+        difference(0, 0, whole(BANK), first_h)
+        store_h(0, 0, BANK)
+        gain_on_gpsimd(0, 512, [0, 1], third_quarter)
+        reads()
+        round_h(0, 0, BANK, halves(BANK))
+        scale_into(1, 0, staged([P, PACK * QUARTER], F32, "scaled1_0", 133 * KB))
+        quantize_h(0, 0, halves(BANK))
+        store_codes(0, 0, BANK)
 
         def finish_with_layers(g, col0, width, before, before_width, shared):
             for tiles in (low, high):
@@ -523,9 +554,16 @@ def tile_list_radar_log_contrast_kernel(
 
         finish_cut(1, 0, QUARTER)
         for g, col0 in PIECES[1:4]:
-            clutter_quarter(g, col0)
+            if g == 1:
+                clutter_quarter(g, col0)
             target_quarter(g, col0)
-            scale_over_previous(g, col0, QUARTER, {(1, 256): [], (0, 512): [2, 3], (1, 512): [0, 1]}[g, col0])
+            if g == 0:
+                for t in (2, 3):
+                    third_quarter.append(staged([P, QUARTER], F32, "scaled0_512_%d" % t, slot(1, 256) + t * KB)[:])
+                gain_on_gpsimd(0, 512, [2, 3], third_quarter[2:])
+                scaled[0, 512] = third_quarter
+            else:
+                scale_over_previous(g, col0, QUARTER, {256: [], 512: [2, 3]}[col0])
             if (g, col0) == (1, 512):
                 finish_cut(g, col0, QUARTER)
             else:

@@ -144,7 +144,7 @@ def tile_list_radar_log_contrast_kernel(
 
         def v_operand(a, col0, width):
             u, place = divmod(col0, BANK)
-            first, picked = [(c0, t) for (b, c0, c1), t in v_codes.items() if b == a and c0 <= col0 < c1][0]
+            first, picked = [(c0, t) for (b, c0, c1), t in v_codes.items() if b == a and c0 <= col0 and col0 + width <= c1][0]
             return picked[:, col0 - first : col0 - first + width].bitcast(FP8X4), plane_of(u, a)[:, place : place + width]
 
         w1_raw, w1_codes, w1_planes = {}, {}, {}
@@ -173,7 +173,10 @@ def tile_list_radar_log_contrast_kernel(
         picked1 = staged([P, BANK], U8, "picked1", 57 * KB + 768)
         move_both_passes(join(1, picked1, held([P, 2 * BANK], U8, "joined1")))
         gather_words(0, BANK, BANK)
-        gather_words(0, 0, BANK)
+        first_words = held([P, BANK], U32, "first_words")
+        for col0 in (0, QUARTER):
+            gather_words(0, col0, QUARTER, first_words[:, col0 : col0 + QUARTER])
+        v_codes[0, 0, BANK] = first_words[:]
         gains = staged([P, GROUPS, PACK], F32, "gains", 45 * KB + 768)
         nc.sync.dma_start(gains[:], gain.rearrange("(g p t) -> p g t", g=GROUPS, t=PACK))
         load_w1(0, 1)
@@ -205,7 +208,7 @@ def tile_list_radar_log_contrast_kernel(
             return codes, plane
 
         response_banks = [psum.tile([P, BANK], F32, name="response%d" % n, bufs=1) for n in range(6)]
-        turns = [0, 1, 2, 3] + [4, 5] * 4 + [0, 1, 0, 1, 2, 3, 2, 3, 0, 4, 5, 1, 2, 3, 0, 4, 5, 1, 2]
+        turns = [0, 1, 2, 3] + [4, 5] * 4 + [0, 1, 0, 1, 2, 3, 2, 3, 0, 1, 4, 5, 2, 3, 0, 1, 4, 5, 2, 3]
 
         def next_bank():
             return response_banks[turns.pop(0)]
@@ -248,7 +251,7 @@ def tile_list_radar_log_contrast_kernel(
             bank = next_bank()
             responses(filters, g, col0, width, slices, bank)
             run = energy[:, slices[0] * width : (slices[-1] + 1) * width]
-            nc.scalar.activation(run, bank[:], ACT.Square)
+            nc.scalar.activation(run, bank[:, 0 : len(slices) * width], ACT.Square)
             return run
 
         def log1p(run):
@@ -262,6 +265,7 @@ def tile_list_radar_log_contrast_kernel(
         def clutter_quarter(g, col0, energy=None):
             if (g, col0) in clutter:
                 energy = clutter[g, col0]
+                square(clutter_filters, energy, g, col0, QUARTER, [2])
                 run = square(clutter_filters, energy, g, col0, QUARTER, [0, 1])
                 log1p(energy[:, BANK:])
                 log1p(run)
@@ -288,6 +292,15 @@ def tile_list_radar_log_contrast_kernel(
                         for t, alone in ((0, spare_banks[1]), (1, bank)):
                             responses(clutter_filters, g, col0, QUARTER, [t], alone)
                             nc.scalar.activation(run[:, t, :], alone[:, 0:QUARTER], ACT.Square)
+                    elif col0 == QUARTER and pair == high:
+                        responses(clutter_filters, g, col0, QUARTER, [2], bank)
+                        nc.scalar.activation(run[:, 0, :], bank[:, 0:QUARTER], ACT.Square)
+                        responses(clutter_filters, g, col0, QUARTER, [3], spare_banks[0])
+                        copied = held([P, QUARTER], F32, "early_copied")
+                        for cols in halves(QUARTER):
+                            nc.vector.tensor_copy(copied[:, cols], spare_banks[0][:, cols])
+                        for cols in halves(QUARTER):
+                            nc.vector.tensor_tensor(run[:, 1, cols], spare_banks[0][:, cols], copied[:, cols], ALU.mult)
                     else:
                         responses(clutter_filters, g, col0, QUARTER, range(PACK)[pair], bank)
                         nc.scalar.activation(run, bank[:].rearrange("p (t j) -> p t j", t=2), ACT.Square)
@@ -469,9 +482,9 @@ def tile_list_radar_log_contrast_kernel(
             run = clutter[g, col0][:, slices[0] * width : (slices[-1] + 1) * width]
 
             def reads():
-                for cols in halves(BANK):
+                for cols in halves(QUARTER):
                     nc.vector.tensor_copy(copied[:, cols], bank[:, cols])
-                for cols in halves(BANK):
+                for cols in halves(QUARTER):
                     nc.vector.tensor_tensor(run[:, cols], bank[:, cols], copied[:, cols], ALU.mult)
 
             return reads
@@ -529,14 +542,15 @@ def tile_list_radar_log_contrast_kernel(
         quantize_w1(1, 1, w1_rounded(68 * KB))
         clutter_quarter(1, 0)
         target_quarter(1, 0)
-        reads = square_on_vector(1, 512, QUARTER, [2, 3], staged([P, BANK], F32, "copied", places[2]))
+        reads = square_on_vector(1, 512, QUARTER, [3], staged([P, QUARTER], F32, "copied", places[2]))
         third_quarter = [staged([P, QUARTER], F32, "scaled0_512_%d" % t, (131 + t) * KB)[:] for t in range(2)]
         first_h = half_tile("first_h", w1_at[1, 0])
         difference(0, 0, whole(BANK), first_h)
         store_h(0, 0, BANK)
-        gain_on_gpsimd(0, 512, [0, 1], third_quarter)
+        gain_on_gpsimd(0, 512, [0], third_quarter)
         reads()
         round_h(0, 0, BANK, halves(BANK))
+        nc.vector.tensor_scalar_mul(third_quarter[1], by_slice(clutter[0, 512])[:, 1, :], gains[:, 0, 1:2])
         scale_into(1, 0, staged([P, PACK * QUARTER], F32, "scaled1_0", 133 * KB))
         quantize_h(0, 0, halves(BANK))
         store_codes(0, 0, BANK)

@@ -208,7 +208,7 @@ def tile_list_radar_log_contrast_kernel(
             return codes, plane
 
         response_banks = [psum.tile([P, BANK], F32, name="response%d" % n, bufs=1) for n in range(6)]
-        turns = [0, 1, 2, 3] + [4, 5] * 4 + [0, 1, 0, 1, 2, 3, 2, 3, 0, 1, 4, 5, 2, 3, 0, 1, 4, 5, 2, 3]
+        turns = [0, 1, 2, 3] + [4, 5] * 4 + [0, 1, 0, 1, 2, 3, 2, 3, 0, 4, 5, 1, 2, 3, 0, 4, 5, 1, 2]
 
         def next_bank():
             return response_banks[turns.pop(0)]
@@ -265,7 +265,6 @@ def tile_list_radar_log_contrast_kernel(
         def clutter_quarter(g, col0, energy=None):
             if (g, col0) in clutter:
                 energy = clutter[g, col0]
-                square(clutter_filters, energy, g, col0, QUARTER, [2])
                 run = square(clutter_filters, energy, g, col0, QUARTER, [0, 1])
                 log1p(energy[:, BANK:])
                 log1p(run)
@@ -482,9 +481,9 @@ def tile_list_radar_log_contrast_kernel(
             run = clutter[g, col0][:, slices[0] * width : (slices[-1] + 1) * width]
 
             def reads():
-                for cols in halves(QUARTER):
+                for cols in halves(BANK):
                     nc.vector.tensor_copy(copied[:, cols], bank[:, cols])
-                for cols in halves(QUARTER):
+                for cols in halves(BANK):
                     nc.vector.tensor_tensor(run[:, cols], bank[:, cols], copied[:, cols], ALU.mult)
 
             return reads
@@ -542,15 +541,14 @@ def tile_list_radar_log_contrast_kernel(
         quantize_w1(1, 1, w1_rounded(68 * KB))
         clutter_quarter(1, 0)
         target_quarter(1, 0)
-        reads = square_on_vector(1, 512, QUARTER, [3], staged([P, QUARTER], F32, "copied", places[2]))
+        reads = square_on_vector(1, 512, QUARTER, [2, 3], staged([P, BANK], F32, "copied", places[2]))
         third_quarter = [staged([P, QUARTER], F32, "scaled0_512_%d" % t, (131 + t) * KB)[:] for t in range(2)]
         first_h = half_tile("first_h", w1_at[1, 0])
         difference(0, 0, whole(BANK), first_h)
         store_h(0, 0, BANK)
-        gain_on_gpsimd(0, 512, [0], third_quarter)
+        gain_on_gpsimd(0, 512, [0, 1], third_quarter)
         reads()
         round_h(0, 0, BANK, halves(BANK))
-        nc.vector.tensor_scalar_mul(third_quarter[1], by_slice(clutter[0, 512])[:, 1, :], gains[:, 0, 1:2])
         scale_into(1, 0, staged([P, PACK * QUARTER], F32, "scaled1_0", 133 * KB))
         quantize_h(0, 0, halves(BANK))
         store_codes(0, 0, BANK)

@@ -184,10 +184,10 @@ def tile_list_radar_log_contrast_kernel(
         load_w2(1, slice(0, 2), w2_raw1)
         load_w1(1, 0)
         gather_words(1, 0, QUARTER)
-        deal_w2(0, slice(1, 2), w2_late, held([P, 1, 2 * GROUP], U8, "w2_codes_late"), halves(PACK))
+        deal_w2(0, slice(1, 2), w2_late, held([P, 1, 2 * GROUP], U8, "w2_codes_late"), [slice(0, 1), slice(1, 2), slice(2, 4)])
         later_words = staged([P, S - QUARTER], U32, "later_words", 54 * KB)
-        for col0 in range(QUARTER, S, QUARTER):
-            gather_words(1, col0, QUARTER, later_words[:, col0 - QUARTER : col0])
+        for col0, width in ((QUARTER, QUARTER), (BANK, BANK)):
+            gather_words(1, col0, width, later_words[:, col0 - QUARTER : col0 - QUARTER + width])
 
         depths = {}
 
@@ -548,9 +548,9 @@ def tile_list_radar_log_contrast_kernel(
         store_h(0, 0, BANK)
         gain_on_gpsimd(0, 512, [0, 1], third_quarter)
         reads()
-        round_h(0, 0, BANK, halves(BANK))
+        round_h(0, 0, BANK, [slice(0, BANK)])
         scale_into(1, 0, staged([P, PACK * QUARTER], F32, "scaled1_0", 133 * KB))
-        quantize_h(0, 0, halves(BANK))
+        quantize_h(0, 0, [slice(0, BANK)])
         store_codes(0, 0, BANK)
 
         def finish_with_layers(g, col0, width, before, before_width, shared):

@@ -208,7 +208,7 @@ def tile_list_radar_log_contrast_kernel(
             return codes, plane
 
         response_banks = [psum.tile([P, BANK], F32, name="response%d" % n, bufs=1) for n in range(6)]
-        turns = [0, 1, 2, 3] + [4, 5] * 4 + [0, 1, 0, 1, 2, 3, 2, 3, 0, 4, 5, 1, 2, 3, 0, 4, 5, 1, 2]
+        turns = [0, 1] + [2, 3] * 5 + [0, 1, 0, 1, 4, 5, 4, 5, 0, 2, 3, 1, 4, 5, 0, 2, 3, 1, 4]
 
         def next_bank():
             return response_banks[turns.pop(0)]

from contextlib import ExitStack

import concourse.mybir as mybir

K, H, N, T, S = 1024, 1024, 512, 4096, 1024
FLOPS = 2 * S * (2 * K * H + H * N)

F32 = mybir.dt.float32
BF16 = mybir.dt.bfloat16
I32 = mybir.dt.int32
U32 = mybir.dt.uint32
U16 = mybir.dt.uint16
U8 = mybir.dt.uint8
FP8X4 = mybir.dt.float8_e4m3fn_x4
FP4X4 = mybir.dt.float4_e2m1fn_x4
ACT = mybir.ActivationFunctionType
ALU = mybir.AluOpType

P = 128
PACK = 4
GROUP = P * PACK
BANK = 512
QUADS = 4
PER_COLUMN = 16
PASSES = K // GROUP
GROUPS = H // GROUP
LAYER_TILES = N // P
ROWS_AT = 96
KB = 1024
QUARTER = 256
LAST_AT = 140 * KB
PIECES = [(1, 0), (1, 256), (0, 512), (1, 512), (0, 768), (1, 768), (0, 896), (1, 896)]


def halves(width):
    return slice(0, width // 2), slice(width // 2, width)


def tile_list_radar_log_contrast_kernel(
    tc, tab_words, tab_scales, offs, w1, w2_words, w2_scales, gain, w3_words, w3_scales, depth,
    out_0, out_1, out_2, out_3,
):
    nc = tc.nc
    with ExitStack() as ctx:
        keep = ctx.enter_context(tc.tile_pool(name="keep", bufs=1))
        stage = ctx.enter_context(tc.tile_pool(name="stage", bufs=1))
        ring = ctx.enter_context(tc.tile_pool(name="ring", bufs=2))
        psum = ctx.enter_context(tc.psum_pool(name="psum", bufs=2))

        def held(shape, dtype, name):
            return keep.tile(shape, dtype, name=name, align_bytes=64)

        def staged(shape, dtype, name, offset):
            return stage.tile(shape, dtype, name=name, align_bytes=64, offset=offset)

        def load_scale_rows(name, scales, width):
            rows = held([P, width], U8, name)
            nc.vector.memset(rows[0:ROWS_AT, :].bitcast(I32), 0)
            nc.sync.dma_start(rows[ROWS_AT:P, :].bitcast(I32), scales.rearrange("a q c -> q a c").bitcast(I32))
            return rows

        def load_table(a, offset):
            window = staged([P, T], I32, "table%d" % a, offset)
            nc.sync.dma_start(window[:], tab_words[a].rearrange("p t i -> p (t i)").bitcast(I32))
            return window

        w2_codes = {}

        def load_w2(g, passes, raw):
            columns = w2_words[passes, :, 2 * GROUP * g : 2 * GROUP * (g + 1)]
            nc.sync.dma_start(raw[:].bitcast(I32), columns.rearrange("a p c -> p a c").bitcast(I32))

        def deal_w2(g, passes, raw, dealt, parts):
            for part in parts:
                nc.vector.tensor_copy(
                    dealt[:].bitcast(U16).rearrange("p a (t m) -> p a t m", t=PACK)[:, :, part, :],
                    raw[:].bitcast(U16).rearrange("p a (m t) -> p a t m", t=PACK)[:, :, part, :],
                )
            for place, a in enumerate(range(PASSES)[passes]):
                w2_codes[g, a] = dealt[:, place, :]

        scale_window = load_scale_rows("scale_window", tab_scales, T)
        offsets = keep.tile([P, S // PER_COLUMN], U16, name="offsets")
        nc.sync.dma_start(offsets[:], offs)
        w2_rows = load_scale_rows("w2_rows", w2_scales, H)
        w2_raw0 = staged([P, 1, 2 * GROUP], U8, "w2_raw0", 57 * KB + 512)
        load_w2(0, slice(0, 1), w2_raw0)
        tables = [load_table(0, 38 * KB)]

        warm = held([P, 2], F32, "warm")
        nc.vector.memset(warm[:, 0:1], 1.0)
        nc.scalar.activation(warm[:, 1:2], warm[:, 0:1], ACT.Ln)

        def entries(col0, width):
            return offsets[:, col0 // PER_COLUMN : (col0 + width) // PER_COLUMN]

        first_planes = [held([P, 2 * BANK], U8, "first_planes%d" % a) for a in range(PASSES)]
        second_planes = held([P, PASSES, 2 * BANK], U8, "second_planes")
        for plane in first_planes + [second_planes]:
            nc.vector.memset(plane[:].bitcast(I32), 0)

        def plane_of(u, a):
            return first_planes[a][:] if u == 0 else second_planes[:, a, :]

        def join(u, picked, joined):
            nc.vector.tensor_copy(picked[:], scale_window[:].indirect(entries(u * BANK, BANK)))
            nc.vector.tensor_copy(
                joined[:, BANK:].rearrange("p (t m) -> p t m", t=PACK),
                w2_rows[:, u * GROUP : (u + 1) * GROUP].rearrange("p (m t) -> p t m", t=PACK),
            )
            nc.vector.tensor_copy(joined[ROWS_AT:P, 0:BANK].bitcast(I32), picked[ROWS_AT:P, :].bitcast(I32))
            return joined

        def move_one_pass(joined, a):
            for quad in (0, 2, 1, 3):
                first = ROWS_AT + 8 * quad + a
                nc.sync.dma_start(
                    first_planes[a][32 * quad : 32 * quad + 4, :].bitcast(I32),
                    joined[first : first + 7 : 2, :].bitcast(I32),
                )

        def move_both_passes(joined):
            for quad in (0, 2, 1, 3):
                nc.sync.dma_start(
                    second_planes[32 * quad : 32 * quad + 4].rearrange("p a c -> p (a c)").bitcast(I32),
                    joined[ROWS_AT + 8 * quad : ROWS_AT + 8 * quad + 8, :].bitcast(I32),
                )

        joined0 = join(0, staged([P, BANK], U8, "picked0", 3 * KB + 768), held([P, 2 * BANK], U8, "joined0"))
        move_one_pass(joined0, 0)
        tables.append(load_table(1, 4 * KB))
        deal_w2(0, slice(0, 1), w2_raw0, staged([P, 1, 2 * GROUP], U8, "w2_codes0", 3 * KB), [slice(0, 4)])
        w2_late = staged([P, 1, 2 * GROUP], U8, "w2_late", 56 * KB + 768)
        load_w2(0, slice(1, 2), w2_late)
        move_one_pass(joined0, 1)

        v_codes = {}

        def gather_words(a, col0, width, picked=None):
            if picked is None:
                picked = held([P, width], U32, "v_codes%d_%d" % (a, col0))[:]
            nc.vector.tensor_copy(picked, tables[a][:].bitcast(U32).indirect(entries(col0, width)))
            v_codes[a, col0, col0 + width] = picked

        def v_operand(a, col0, width):
            u, place = divmod(col0, BANK)
            first, picked = [(c0, t) for (b, c0, c1), t in v_codes.items() if b == a and c0 <= col0 and col0 + width <= c1][0]
            return picked[:, col0 - first : col0 - first + width].bitcast(FP8X4), plane_of(u, a)[:, place : place + width]

        w1_raw, w1_codes, w1_planes = {}, {}, {}
        w1_at = {(0, 0): 58 * KB + 256, (0, 1): 30 * KB + 256, (1, 0): 46 * KB, (1, 1): 58 * KB + 256}

        def load_w1(g, a):
            raw = staged([P, PACK, GROUP], F32, "w1_raw%d%d" % (g, a), w1_at[g, a])
            rows = w1[a * GROUP : (a + 1) * GROUP, g * GROUP : (g + 1) * GROUP]
            nc.sync.dma_start(raw[:], rows.rearrange("(p i) c -> p i c", i=PACK))
            w1_raw[g, a] = raw

        def quantize_w1(g, a, rounded):
            raw = w1_raw[g, a]
            for pair in halves(PACK):
                nc.vector.tensor_copy(
                    rounded[:].rearrange("p (t m i) -> p m i t", t=PACK, i=PACK)[:, :, :, pair],
                    raw[:].rearrange("p i (m t) -> p m i t", t=PACK)[:, :, :, pair],
                )
            codes = held([P, GROUP], U32, "w1_codes%d%d" % (g, a))
            plane = held([P, GROUP], U8, "w1_plane%d%d" % (g, a))
            for words, values in zip(halves(GROUP), halves(PACK * GROUP)):
                nc.vector.quantize_mx(out=codes[:, words].bitcast(FP8X4), scales=plane[:, words], in_=rounded[:, values])
            w1_codes[g, a], w1_planes[g, a] = codes, plane

        load_w1(0, 0)
        picked1 = staged([P, BANK], U8, "picked1", 57 * KB + 768)
        move_both_passes(join(1, picked1, held([P, 2 * BANK], U8, "joined1")))
        gather_words(0, BANK, BANK)
        first_words = held([P, BANK], U32, "first_words")
        for col0 in (0, QUARTER):
            gather_words(0, col0, QUARTER, first_words[:, col0 : col0 + QUARTER])
        v_codes[0, 0, BANK] = first_words[:]
        gains = staged([P, GROUPS, PACK], F32, "gains", 45 * KB + 768)
        nc.sync.dma_start(gains[:], gain.rearrange("(g p t) -> p g t", g=GROUPS, t=PACK))
        load_w1(0, 1)
        w2_raw1 = staged([P, PASSES, 2 * GROUP], U8, "w2_raw1", 39 * KB)
        load_w2(1, slice(0, 2), w2_raw1)
        load_w1(1, 0)
        gather_words(1, 0, QUARTER)
        deal_w2(0, slice(1, 2), w2_late, held([P, 1, 2 * GROUP], U8, "w2_codes_late"), [slice(0, 1), slice(1, 2), slice(2, 4)])
        later_words = staged([P, S - QUARTER], U32, "later_words", 54 * KB)
        for col0, width in ((QUARTER, QUARTER), (BANK, BANK)):
            gather_words(1, col0, width, later_words[:, col0 - QUARTER : col0 - QUARTER + width])

        depths = {}

        def load_depth(u, offset):
            depths[u] = staged([P, LAYER_TILES, BANK], F32, "depths%d" % u, offset)
            nc.sync.dma_start(depths[u][:], depth.rearrange("(c p) j -> p c j", p=P)[:, :, u * BANK : (u + 1) * BANK])

        def load_w3():
            codes = staged([P, GROUPS, N], I32, "w3_codes", 10 * KB)
            nc.sync.dma_start(codes[:], w3_words.rearrange("g p c i -> p g (c i)").bitcast(I32))
            plane = staged([P, N], U8, "w3_plane", 6 * KB)
            nc.vector.memset(plane[:].bitcast(I32), 0)
            for quad in range(QUADS):
                nc.sync.dma_start(
                    plane[32 * quad : 32 * quad + 8, :].bitcast(I32),
                    w3_scales[:, 4 * quad : 4 * quad + 4, :].bitcast(I32),
                )
            return codes, plane

        response_banks = [psum.tile([P, BANK], F32, name="response%d" % n, bufs=1) for n in range(6)]
        turns = [0, 1] + [2, 3] * 5 + [0, 1, 0, 1, 4, 5, 4, 5, 0, 2, 3, 1, 4, 5, 0, 2, 3, 1, 4]

        def next_bank():
            return response_banks[turns.pop(0)]

        def clutter_filters(g, a, t):
            return (
                w2_codes[g, a][:, 2 * P * t : 2 * P * (t + 1)].bitcast(FP4X4),
                plane_of(g, a)[:, BANK + P * t : BANK + P * (t + 1)],
            )

        def target_filters(g, a, t):
            return w1_codes[g, a][:, P * t : P * (t + 1)].bitcast(FP8X4), w1_planes[g, a][:, P * t : P * (t + 1)]

        def responses(filters, g, col0, width, slices, bank):
            steps = []
            for a in range(PASSES):
                for place, t in enumerate(slices):
                    for cols in halves(width) if a == 1 and width == BANK else [slice(0, width)]:
                        steps.append((a, place * width, t, cols))
            for n, (a, at, t, cols) in enumerate(steps):
                moving, moving_scales = v_operand(a, col0 + cols.start, cols.stop - cols.start)
                codes, plane = filters(g, a, t)
                nc.tensor.matmul_mx(
                    out=bank[:, at + cols.start : at + cols.stop],
                    lhsT=codes,
                    lhsT_scale=plane,
                    rhs=moving,
                    rhs_scale=moving_scales,
                    start=(n == 0),
                    stop=(n == len(steps) - 1),
                )

        clutter, contrast = {}, {}
        low, high, every = slice(0, 2), slice(2, 4), slice(0, 4)

        def by_slice(tile):
            return tile[:].rearrange("p (t j) -> p t j", t=PACK)

        def square(filters, energy, g, col0, width, slices):
            bank = next_bank()
            responses(filters, g, col0, width, slices, bank)
            run = energy[:, slices[0] * width : (slices[-1] + 1) * width]
            nc.scalar.activation(run, bank[:, 0 : len(slices) * width], ACT.Square)
            return run

        def log1p(run):
            nc.scalar.activation(run, run, ACT.Ln, bias=1.0)

        def quarter_side(filters, energy, g, col0):
            runs = [square(filters, energy, g, col0, QUARTER, pair) for pair in ([0, 1], [2, 3])]
            for run in runs:
                log1p(run)

        def clutter_quarter(g, col0, energy=None):
            if (g, col0) in clutter:
                energy = clutter[g, col0]
                run = square(clutter_filters, energy, g, col0, QUARTER, [0, 1])
                log1p(energy[:, BANK:])
                log1p(run)
                return
            clutter[g, col0] = energy or held([P, PACK * QUARTER], F32, "clutter%d_%d" % (g, col0))
            quarter_side(clutter_filters, clutter[g, col0], g, col0)

        def slot(g, col0):
            return 85 * KB + 6 * KB * PIECES.index((g, col0))

        def target_quarter(g, col0):
            contrast[g, col0] = staged([P, PACK * QUARTER], F32, "contrast%d_%d" % (g, col0), slot(g, col0))
            quarter_side(target_filters, contrast[g, col0], g, col0)

        def clutter_half(g):
            energy = held([P, PACK * BANK], F32, "clutter%d_0" % g)
            clutter[g, 0] = energy
            for col0 in (0, QUARTER):
                runs = []
                for pair in (low, high):
                    bank = next_bank()
                    run = by_slice(energy)[:, pair, col0 : col0 + QUARTER]
                    if col0 == 0 and pair == low:
                        for t, alone in ((0, spare_banks[1]), (1, bank)):
                            responses(clutter_filters, g, col0, QUARTER, [t], alone)
                            nc.scalar.activation(run[:, t, :], alone[:, 0:QUARTER], ACT.Square)
                    elif col0 == QUARTER and pair == high:
                        responses(clutter_filters, g, col0, QUARTER, [2], bank)
                        nc.scalar.activation(run[:, 0, :], bank[:, 0:QUARTER], ACT.Square)
                        responses(clutter_filters, g, col0, QUARTER, [3], spare_banks[0])
                        copied = held([P, QUARTER], F32, "early_copied")
                        for cols in halves(QUARTER):
                            nc.vector.tensor_copy(copied[:, cols], spare_banks[0][:, cols])
                        for cols in halves(QUARTER):
                            nc.vector.tensor_tensor(run[:, 1, cols], spare_banks[0][:, cols], copied[:, cols], ALU.mult)
                    else:
                        responses(clutter_filters, g, col0, QUARTER, range(PACK)[pair], bank)
                        nc.scalar.activation(run, bank[:].rearrange("p (t j) -> p t j", t=2), ACT.Square)
                    runs.append(run)
                for run in runs:
                    log1p(run)

        def target_half(g):
            contrast[g, 0] = staged([P, PACK * BANK], F32, "contrast%d_0" % g, 131 * KB)
            for pair in ([0, 1], [2, 3]):
                runs = [square(target_filters, contrast[g, 0], g, 0, BANK, [t]) for t in pair]
                for run in runs:
                    log1p(run)

        def eighth_energies(g, col0, parts):
            contrast[g, col0] = staged([P, PACK * P], F32, "contrast%d_%d" % (g, col0), slot(g, col0))
            clutter[g, col0] = held([P, PACK * P], F32, "clutter%d_%d" % (g, col0))
            clutter_run = square(clutter_filters, clutter[g, col0], g, col0, P, [0, 1, 2, 3])
            target_run = square(target_filters, contrast[g, col0], g, col0, P, [0, 1, 2, 3])
            log1p(clutter_run)
            for part in parts:
                log1p(target_run[:, part])

        last_banks = []

        def last_energies(g, col0):
            contrast[g, col0] = staged([P, PACK * P], F32, "contrast%d_%d" % (g, col0), slot(g, col0))
            clutter[g, col0] = held([P, PACK * P], F32, "clutter%d_%d" % (g, col0))
            for filters, energy in ((clutter_filters, clutter[g, col0]), (target_filters, contrast[g, col0])):
                bank = next_bank()
                last_banks.append(bank)
                responses(filters, g, col0, P, range(PACK), bank)
                for part in halves(BANK):
                    nc.scalar.activation(energy[:, part], bank[:, part], ACT.Square)
                for part in halves(BANK):
                    log1p(energy[:, part])

        scaled = {}

        def scale_clutter(g, col0, results, on_gpsimd=()):
            energy = by_slice(clutter[g, col0])
            for t in on_gpsimd:
                nc.gpsimd.tensor_scalar(results[t], energy[:, t, :], gains[:, g, t : t + 1], 1.0, ALU.mult, ALU.mult)
            for t in range(PACK):
                if t not in on_gpsimd:
                    nc.vector.tensor_scalar_mul(results[t], energy[:, t, :], gains[:, g, t : t + 1])
            scaled[g, col0] = results

        def gain_on_gpsimd(g, col0, slices, results):
            energy = by_slice(clutter[g, col0])
            for t, result in zip(slices, results):
                nc.gpsimd.tensor_scalar(result, energy[:, t, :], gains[:, g, t : t + 1], 1.0, ALU.mult, ALU.mult)

        def scale_into(g, col0, result):
            scale_clutter(g, col0, [by_slice(result)[:, t, :] for t in range(PACK)])

        def scale_over_previous(g, col0, width, on_gpsimd):
            at = slot(*PIECES[PIECES.index((g, col0)) - 1])
            first = staged([P, PACK - 1, width], F32, "scaled%d_%d" % (g, col0), at)
            last = staged([P, width], F32, "last_scaled%d_%d" % (g, col0), at + 4 * (PACK - 1) * width)
            scale_clutter(g, col0, [first[:, t, :] for t in range(PACK - 1)] + [last[:]], on_gpsimd)

        def rows_over_scaled(g, col0, width, rows_width):
            end = slot(*PIECES[PIECES.index((g, col0)) - 1]) + 4 * (PACK - 1) * width
            return staged([P, LAYER_TILES, rows_width], F32, "layers_at%d_%d" % (g, col0), end - 4 * LAYER_TILES * rows_width)

        def w1_rounded(offset):
            return staged([P, PACK * GROUP], BF16, "w1_rounded%d" % len(w1_codes), offset)

        def half_tile(name, offset):
            return staged([P, PACK * BANK], F32, name, offset)

        def difference(g, col0, runs, result):
            energy, h = by_slice(contrast[g, col0]), by_slice(result)
            contrast[g, col0] = result
            for t, cols in runs:
                nc.vector.scalar_tensor_tensor(
                    h[:, t, cols], energy[:, t, cols], gains[:, g, t : t + 1], scaled[g, col0][t][:, cols], ALU.mult, ALU.subtract
                )

        SCALE_RANGES = [(0, 768), (768, 1024)]
        h_codes = [held([P, S], U32, "h_codes%d" % g) for g in range(GROUPS)]
        h_planes = {r: held([P, GROUPS, r[1] - r[0]], U8, "h_planes%d" % r[0]) for r in SCALE_RANGES}

        def h_scales(g, col0, col1):
            first, last = [r for r in SCALE_RANGES if r[0] <= col0 < r[1]][0]
            return h_planes[first, last][:, g, col0 - first : col1 - first]

        rounded_h = {}

        def round_h(g, col0, width, parts):
            h = by_slice(contrast[g, col0])
            if (g, col0) == PIECES[-1]:
                rounded = staged([P, width, PACK], BF16, "last_rounded", LAST_AT)
            else:
                rounded = ring.tile([P, width, PACK], BF16, name="h_rounded", align_bytes=64, bufs=3)
            for cols in parts:
                nc.vector.tensor_copy(
                    rounded[:, cols, :].rearrange("p (c i) t -> p c t i", i=4),
                    h[:, :, cols].rearrange("p t (c i) -> p c t i", i=4),
                )
            rounded_h[g, col0] = rounded

        def finish_shared(g, col0, width, result, bank_reads, parts):
            difference(g, col0, whole(width), result)
            store_h(g, col0, width)
            for read in bank_reads:
                read()
            round_h(g, col0, width, parts)
            quantize_h(g, col0, parts)
            store_codes(g, col0, col0 + width)

        def store_h(g, col0, width):
            rows = out_1[g * GROUP : (g + 1) * GROUP, col0 : col0 + width]
            for part in halves(PACK) if (g, col0) == PIECES[-1] else [every]:
                nc.sync.dma_start(rows.rearrange("(p t) j -> p t j", t=PACK)[:, part, :], by_slice(contrast[g, col0])[:, part, :])

        def quantize_h(g, col0, parts):
            rounded = rounded_h[g, col0]
            for cols in parts:
                nc.vector.quantize_mx(
                    out=h_codes[g][:, col0 + cols.start : col0 + cols.stop].bitcast(FP8X4),
                    scales=h_scales(g, col0 + cols.start, col0 + cols.stop),
                    in_=rounded[:, cols, :].rearrange("p j t -> p (j t)"),
                )

        def store_codes(g, col0, col1):
            nc.sync.dma_start(
                out_2[g, :, col0:col1, :].rearrange("p j t -> p (j t)").bitcast(I32),
                h_codes[g][:, col0:col1].bitcast(I32),
            )

        def store_scales(col0, col1):
            for quad in range(QUADS):
                nc.sync.dma_start(
                    out_3[:, quad : 16 : 4, col0:col1].rearrange("g q j -> q g j").bitcast(I32),
                    h_planes[col0, col1][quad : P : 32, :, :].bitcast(I32),
                )

        layer_banks, layer_rows = {}, {}
        spare_banks = [psum.tile([P, BANK], F32, name="spare%d" % n, bufs=1) for n in range(2)]
        spare_turn = []

        def next_spare():
            spare_turn.append(None)
            return spare_banks[(len(spare_turn) - 1) % len(spare_banks)]

        def layer_passes(col0, width, tiles, bank=None):
            cols = slice(col0, col0 + width)
            per_bank = tiles.stop - tiles.start
            bank = (bank or next_spare())[:, 0 : per_bank * width].rearrange("p (c j) -> p c j", c=per_bank)
            for g in range(GROUPS):
                for place in range(per_bank):
                    c = tiles.start + place
                    nc.tensor.matmul_mx(
                        out=bank[:, place, :],
                        lhsT=w3_codes[:, g, P * c : P * (c + 1)].bitcast(FP8X4),
                        lhsT_scale=w3_plane[4 * g : P, P * c : P * (c + 1)],
                        rhs=h_codes[g][:, cols].bitcast(FP8X4),
                        rhs_scale=h_scales(g, col0, col0 + width),
                        start=(g == 0 and place == 0),
                        stop=(g == GROUPS - 1 and place == per_bank - 1),
                    )
            layer_banks[col0, tiles.start] = bank

        def scale_layers(col0, width, tiles):
            bank = layer_banks[col0, tiles.start]
            y = layer_rows[col0][:, tiles, :]
            nc.vector.tensor_tensor(y, bank, depths[col0 // BANK][:, tiles, col0 % BANK : col0 % BANK + width], ALU.mult)

        def store_layers(col0, width, tiles):
            stored = out_0.rearrange("(c p) j -> p c j", p=P)
            nc.sync.dma_start(stored[:, tiles, col0 : col0 + width], layer_rows[col0][:, tiles, :])

        def square_on_vector(g, col0, width, slices, copied):
            bank = next_spare()
            responses(clutter_filters, g, col0, width, slices, bank)
            clutter[g, col0] = held([P, PACK * width], F32, "clutter%d_%d" % (g, col0))
            run = clutter[g, col0][:, slices[0] * width : (slices[-1] + 1) * width]

            def reads():
                for cols in halves(BANK):
                    nc.vector.tensor_copy(copied[:, cols], bank[:, cols])
                for cols in halves(BANK):
                    nc.vector.tensor_tensor(run[:, cols], bank[:, cols], copied[:, cols], ALU.mult)

            return reads

        def whole(width):
            return [(t, slice(0, width)) for t in range(PACK)]

        def cut(width, slices):
            runs = [(t, slice(0, width)) for t in range(PACK) if t not in slices]
            return runs + [(t, cols) for cols in halves(width) for t in slices]


        def finish(g, col0, width, result=None):
            difference(g, col0, whole(width), result or contrast[g, col0])
            store_h(g, col0, width)
            round_h(g, col0, width, [slice(0, width)])
            quantize_h(g, col0, [slice(0, width)])
            store_codes(g, col0, col0 + width)

        def finish_between(g, col0, width, first_filler, second_filler):
            difference(g, col0, whole(width), clutter[g, col0])
            store_h(g, col0, width)
            first_filler()
            round_h(g, col0, width, [slice(0, width)])
            second_filler()
            quantize_h(g, col0, [slice(0, width)])
            store_codes(g, col0, col0 + width)

        def finish_cut(g, col0, width):
            difference(g, col0, cut(width, [2, 3]), clutter[g, col0])
            store_h(g, col0, width)
            round_h(g, col0, width, halves(width))
            quantize_h(g, col0, halves(width))
            store_codes(g, col0, col0 + width)

        def layers(col0, width, parts):
            layer_rows[col0] = held([P, LAYER_TILES, width], F32, "layers%d" % col0)
            for tiles in parts:
                layer_passes(col0, width, tiles)
                scale_layers(col0, width, tiles)

        clutter_half(0)
        clutter_quarter(0, 512)
        quantize_w1(0, 0, w1_rounded(6 * KB + 256))
        load_w1(1, 1)
        w3_codes, w3_plane = load_w3()
        quantize_w1(0, 1, w1_rounded(68 * KB))
        load_depth(0, 22 * KB + 512)
        deal_w2(1, slice(0, 2), w2_raw1, held([P, PASSES, 2 * GROUP], U8, "w2_codes1"), [slice(0, 4)])
        target_half(0)
        quantize_w1(1, 0, w1_rounded(72 * KB))
        load_depth(1, 75 * KB + 768)
        places = [w1_at[0, 1] + 256 + 2 * KB * t for t in range(PACK)]
        scale_clutter(0, 0, [staged([P, BANK], F32, "scaled0_%d" % t, at)[:] for t, at in enumerate(places)])
        quantize_w1(1, 1, w1_rounded(68 * KB))
        clutter_quarter(1, 0)
        target_quarter(1, 0)
        reads = square_on_vector(1, 512, QUARTER, [2, 3], staged([P, BANK], F32, "copied", places[2]))
        third_quarter = [staged([P, QUARTER], F32, "scaled0_512_%d" % t, (131 + t) * KB)[:] for t in range(2)]
        first_h = half_tile("first_h", w1_at[1, 0])
        difference(0, 0, whole(BANK), first_h)
        store_h(0, 0, BANK)
        gain_on_gpsimd(0, 512, [0, 1], third_quarter)
        reads()
        round_h(0, 0, BANK, [slice(0, BANK)])
        scale_into(1, 0, staged([P, PACK * QUARTER], F32, "scaled1_0", 133 * KB))
        quantize_h(0, 0, [slice(0, BANK)])
        store_codes(0, 0, BANK)

        def finish_with_layers(g, col0, width, before, before_width, shared):
            for tiles in (low, high):
                layer_passes(before, before_width, tiles)
            layer_rows[before] = rows_over_scaled(g, col0, width, before_width)
            reads = [lambda: scale_layers(before, before_width, low), lambda: scale_layers(before, before_width, high)]
            if shared:
                finish_shared(g, col0, width, clutter[g, col0], reads, [slice(0, width)])
            else:
                finish_between(g, col0, width, *reads)
            store_layers(before, before_width, every)

        finish_cut(1, 0, QUARTER)
        for g, col0 in PIECES[1:4]:
            if g == 1:
                clutter_quarter(g, col0)
            target_quarter(g, col0)
            if g == 0:
                for t in (2, 3):
                    third_quarter.append(staged([P, QUARTER], F32, "scaled0_512_%d" % t, slot(1, 256) + t * KB)[:])
                gain_on_gpsimd(0, 512, [2, 3], third_quarter[2:])
                scaled[0, 512] = third_quarter
            else:
                scale_over_previous(g, col0, QUARTER, {256: [], 512: [2, 3]}[col0])
            if (g, col0) == (1, 512):
                finish_cut(g, col0, QUARTER)
            else:
                finish_with_layers(g, col0, QUARTER, col0 - QUARTER, QUARTER, True)
        store_scales(0, 768)
        for g, col0 in PIECES[4:]:
            if g == 1:
                last_energies(g, col0)
            else:
                eighth_energies(g, col0, [slice(0, BANK)])
            scale_over_previous(g, col0, P, [0, 1, 2] if (g, col0) == (1, 768) else [])
            if (g, col0) == (0, 768):
                finish_with_layers(g, col0, P, 512, QUARTER, True)
            elif (g, col0) == (0, 896):
                layer_passes(768, P, low)
                layer_rows[768] = rows_over_scaled(g, col0, P, P // 2)[:].rearrange("p (c e) j -> p c (e j)", e=2)
                difference(g, col0, whole(P), clutter[g, col0])
                store_h(g, col0, P)
                scale_layers(768, P, low)
                store_layers(768, P, low)
                round_h(g, col0, P, halves(P))
                quantize_h(g, col0, halves(P))
                store_codes(g, col0, col0 + P)
            else:
                finish_cut(g, col0, P)
        layer_passes(768, P, high, last_banks[-1])
        late_rows = staged([P, 2, P], F32, "layers768", LAST_AT)
        nc.vector.tensor_tensor(late_rows[:], layer_banks[768, 2], depths[1][:, high, 256:384], ALU.mult)
        nc.sync.dma_start(out_0.rearrange("(c p) j -> p c j", p=P)[:, high, 768:896], late_rows[:])
        layer_rows[896] = held([P, LAYER_TILES, P], F32, "layers896")
        for tiles, bank in ((low, next_spare()), (high, next_spare())):
            layer_passes(896, P, tiles, bank)
            scale_layers(896, P, tiles)
            store_layers(896, P, tiles)
        store_scales(768, 1024)
